import numpy as np
import ml_dtypes


def mxq(x, axis, fmt="e4m3"):
    dtype, down = {"e4m3": (ml_dtypes.float8_e4m3fn, 7), "e5m2": (ml_dtypes.float8_e5m2, 14)}[fmt]
    v = np.moveaxis(np.asarray(x, np.float32).astype(ml_dtypes.bfloat16).astype(np.float64), axis, -1)
    blocks = v.reshape(v.shape[:-1] + (-1, 32))
    amax = np.abs(blocks).max(-1, keepdims=True)
    byte = np.maximum(np.where(amax > 0, np.frexp(amax)[1] - 1 + 127, 0) - down, 1)
    scale = np.exp2(byte - 127.0)
    codes = (blocks / scale).astype(np.float32).astype(dtype).astype(np.float64)
    return np.moveaxis((codes * scale).reshape(v.shape), -1, axis)


WIDE = False


def mx_kscale(k):
    if not WIDE:
        return np.ones(k)
    levels = np.array([10, -10, 5, -5, 0])
    if k % 512:
        return np.exp2(np.random.permutation(np.resize(levels, k // 32))).repeat(32)
    a = np.empty((k // 512, 16))
    for p in range(k // 512):
        a[p, :8] = np.random.permutation(np.resize(levels, 8))
        for g in range(8):
            far = levels[np.abs(levels - a[p, g]) >= 10]
            a[p, g + 8] = far[np.random.randint(len(far))]
    return np.exp2(a.ravel()).repeat(32)


def f64(x):
    return np.asarray(x).astype(np.float64)


def striped(idx):
    return np.tile(idx.reshape(-1, 16).T, (8, 1)).astype(np.uint16)


def unstriped(offs):
    return offs[:16].T.reshape(-1).astype(np.int64)


def striped8(idx):
    return np.concatenate([x.reshape(-1, 16).T for x in idx]).astype(np.uint16)


def runs(offs, k):
    lists = np.stack([offs[16 * r : 16 * r + 16].T.reshape(-1) for r in range(8)]).astype(np.int64)
    return lists[np.arange(k) % 512 // 64]


def pack_weight(w):
    k, n = w.shape
    w = f64(np.asarray(w, np.float32).astype(ml_dtypes.bfloat16)).reshape(k // 32, 32, n)
    amax = np.abs(w).max(1)
    byte = np.clip(np.where(amax > 0, np.frexp(amax)[1] - 1 + 127 - 7, 1), 1, 254)
    scaled = (w * np.exp2(127.0 - byte)[:, None, :]).reshape(k, n).astype(np.float32)
    words = np.ascontiguousarray(scaled.reshape(k // 512, 128, 4, n).transpose(0, 1, 3, 2)).astype(ml_dtypes.float8_e4m3fn).view(np.uint8)
    return words, np.ascontiguousarray(byte.astype(np.uint8).reshape(k // 512, 16, n))


def unpack_weight(words, scales):
    g, p, n, _ = words.shape
    vals = np.ascontiguousarray(words).view(ml_dtypes.float8_e4m3fn).astype(np.float64) * np.repeat(np.exp2(scales.astype(np.float64) - 127.0), 8, axis=1)[..., None]
    return vals.transpose(0, 1, 3, 2).reshape(g * 512, n)


def relu(v):
    return np.maximum(v, 0.0)


K, T, S, N, H, U = 1024, 2048, 512, 512, 512, 512


def setup_inputs():
    n = np.random.standard_normal
    s = mx_kscale(K)[:, None]
    u = mx_kscale(H)
    packed_xT = pack_weight(n((K, T)) * s)
    return {
        "x_words": packed_xT[0],
        "x_scales": packed_xT[1],
        "w1": (n((K, H)) / np.sqrt(K) / s * u).astype(np.float32),
        "emb": (0.5 * n((H, U)) * u[:, None]).astype(np.float32),
        "w2": (n((H, N)) / np.sqrt(H) / u[:, None]).astype(np.float32),
        "offs": striped(np.random.permutation(T)[:S]),
        "up1": striped8(np.random.randint(0, U, (8, S))),
        "up2": striped8(np.random.randint(0, U, (8, S))),
        "up3": striped8(np.random.randint(0, U, (8, S))),
    }


def reference(x_words, x_scales, w1, emb, w2, offs, up1, up2, up3):
    xq = unpack_weight(x_words, x_scales)[:, unstriped(offs)]
    y = mxq(f64(w1), 0, "e4m3").T @ xq
    z = relu(y + f64(emb)[np.arange(H)[:, None], runs(up1, H)] + f64(emb)[np.arange(H)[:, None], runs(up2, H)] + f64(emb)[np.arange(H)[:, None], runs(up3, H)])
    return mxq(f64(w2), 0, "e4m3").T @ mxq(z, 0, "e4m3")

@@ -1,0 +1,192 @@
+from contextlib import ExitStack
+
+import concourse.mybir as mybir
+from concourse.masks import make_identity
+
+K, T, S, H, N, U = 1024, 2048, 512, 512, 512, 512
+FLOPS = 2 * K * H * S + 2 * H * N * S
+
+F32 = mybir.dt.float32
+BF16 = mybir.dt.bfloat16
+I32 = mybir.dt.int32
+U32 = mybir.dt.uint32
+U16 = mybir.dt.uint16
+U8 = mybir.dt.uint8
+FP8X4 = mybir.dt.float8_e4m3fn_x4
+COPY = mybir.ActivationFunctionType.Copy
+RELU = mybir.ActivationFunctionType.Relu
+
+P = 128
+PACK = 4
+PASSES = K // (P * PACK)
+CHUNK = 128
+CHUNKS = S // CHUNK
+
+
+def tile_picked_anc8_relu_p_kernel(tc, x_words, x_scales, w1, emb, w2, offs, up1, up2, up3, out):
+    nc = tc.nc
+    with ExitStack() as ctx:
+        keep = ctx.enter_context(tc.tile_pool(name="keep", bufs=1))
+        psum = ctx.enter_context(tc.psum_pool(name="psum", bufs=1))
+
+        x_scale_table = keep.tile([P, T], U8, name="x_scale_table", align_bytes=64)
+        nc.gpsimd.memset(x_scale_table[:].bitcast(I32), 0)
+        ident = keep.tile([P, P], F32, name="ident")
+        make_identity(nc, ident[:])
+        for q in range(4):
+            nc.scalar.dma_start(
+                out=x_scale_table[32 * q : 32 * q + 4 * PASSES, :].bitcast(I32),
+                in_=x_scales[:, 4 * q : 4 * q + 4, :].bitcast(I32),
+            )
+
+        emb_planes = emb.rearrange("(p t) u -> p t u", t=PACK)
+        ups = [keep.tile([P, S // 16], U16, name="up_list%d" % l) for l in range(3)]
+        picks = keep.tile([P, S // 16], U16, name="picks")
+        emb_table = [keep.tile([P, U], F32, name="emb_table%d" % t) for t in range(PACK)]
+        w1_raw = [keep.tile([P, PACK, H], F32, name="w1_raw%d" % g) for g in range(PASSES)]
+        w2_raw = keep.tile([P, PACK, N], F32, name="w2_raw")
+        x_word_table = [keep.tile([P, T], I32, name="x_word_table%d" % g) for g in range(PASSES)]
+
+        def load_emb(t):
+            nc.sync.dma_start(out=emb_table[t][:], in_=emb_planes[:, t, :])
+
+        def load_w1(g):
+            nc.sync.dma_start(out=w1_raw[g][:], in_=w1[g * 512 : (g + 1) * 512, :].rearrange("(p j) c -> p j c", j=PACK))
+
+        def load_x(g):
+            nc.sync.dma_start(out=x_word_table[g][:], in_=x_words[g].rearrange("p n t -> p (n t)").bitcast(I32))
+
+        nc.sync.dma_start(ups[0][:], up1)
+        load_emb(0)
+        nc.sync.dma_start(ups[1][:], up2)
+        nc.sync.dma_start(ups[2][:], up3)
+        load_emb(1)
+        load_w1(0)
+        load_w1(1)
+        nc.sync.dma_start(picks[:], offs)
+        nc.sync.dma_start(out=w2_raw[:], in_=w2.rearrange("(p j) c -> p j c", j=PACK))
+        load_x(0)
+        load_x(1)
+        load_emb(2)
+        load_emb(3)
+
+        def gather_emb(t, l, first, count, tag):
+            g = keep.tile([P, count], F32, name="anc_%d_%d_%d" % (t, l, first), tag=tag)
+            nc.vector.tensor_copy(out=g[:], in_=emb_table[t][:].indirect(ups[l][:, first // 16 : (first + count) // 16]))
+            return g
+
+        def add_turned(dst, src, start, stop):
+            nc.tensor.matmul(dst, lhsT=src, rhs=ident[:], start=start, stop=stop, is_transpose=True)
+
+        pre0 = [psum.tile([P, 2, 2, P], F32, name="pre0_%d" % h, tag="bank%d" % h) for h in range(2)]
+        for e in range(2):
+            for l in range(3):
+                for h in range(2):
+                    g = gather_emb(e, l, h * 256, 256, "early_%d_%d_%d" % (e, l, h))
+                    for c in range(2):
+                        add_turned(pre0[h][:, c, e, :], g[:, c * P : (c + 1) * P], e == 0 and l == 0 and c == 0, False)
+
+        w1_codes = []
+        w1_scales = []
+        for g in range(PASSES):
+            grouped = keep.tile([P, PACK * H], BF16, name="w1_grouped%d" % g, align_bytes=64)
+            nc.scalar.activation(
+                out=grouped[:].rearrange("p (t m j) -> p m j t", t=PACK, j=PACK),
+                in_=w1_raw[g][:].rearrange("p j (m t) -> p m j t", t=PACK),
+                func=COPY,
+            )
+            codes = keep.tile([P, H], U32, name="w1_codes%d" % g, align_bytes=64)
+            scales = keep.tile([P, H], U8, name="w1_scales%d" % g, align_bytes=64)
+            nc.vector.quantize_mx(out=codes[:].bitcast(FP8X4), scales=scales[:], in_=grouped[:])
+            w1_codes.append(codes)
+            w1_scales.append(scales)
+        w2_grouped = keep.tile([P, PACK * N], BF16, name="w2_grouped", align_bytes=64)
+        nc.scalar.activation(
+            out=w2_grouped[:].rearrange("p (c i j) -> p c j i", i=4, j=PACK),
+            in_=w2_raw[:].rearrange("p j (c i) -> p c j i", i=4),
+            func=COPY,
+        )
+        w2_codes = keep.tile([P, N], U32, name="w2_codes", align_bytes=64)
+        w2_scales = keep.tile([P, N], U8, name="w2_scales", align_bytes=64)
+        nc.vector.quantize_mx(out=w2_codes[:].bitcast(FP8X4), scales=w2_scales[:], in_=w2_grouped[:])
+
+        x_sc = keep.tile([P, S], U8, name="x_sc", align_bytes=64)
+        nc.vector.tensor_copy(out=x_sc[:], in_=x_scale_table[:].indirect(picks[:]))
+        y_bank = [[psum.tile([P, 2, 256], F32, name="y_bank%d_%d" % (h, u), tag="bank%d" % (4 + 2 * h + u)) for u in range(2)] for h in range(2)]
+        for g in range(PASSES):
+            x_cd = keep.tile([P, S], U32, name="x_cd%d" % g, align_bytes=64)
+            if g < PASSES - 1:
+                nc.vector.tensor_copy(out=x_cd[:], in_=x_word_table[g][:].bitcast(U32).indirect(picks[:]))
+            for h in range(2):
+                half = slice(h * 256, (h + 1) * 256)
+                if g == PASSES - 1:
+                    nc.vector.tensor_copy(out=x_cd[:, half], in_=x_word_table[g][:].bitcast(U32).indirect(picks[:, h * 16 : (h + 1) * 16]))
+                for t in range(PACK):
+                    nc.tensor.matmul_mx(
+                        out=y_bank[h][t // 2][:, t % 2, :],
+                        lhsT=w1_codes[g][:, t * P : (t + 1) * P].bitcast(FP8X4),
+                        lhsT_scale=w1_scales[g][:, t * P : (t + 1) * P],
+                        rhs=x_cd[:, half].bitcast(FP8X4),
+                        rhs_scale=x_sc[4 * g : P, half],
+                        start=(g == 0 and t % 2 == 0),
+                        stop=(g == PASSES - 1 and t % 2 == 1),
+                    )
+
+        out_view = out.rearrange("(t p) s -> p t s", p=P)
+        for h in range(2):
+            y_pair = [keep.tile([P, 2, 256], F32, name="y_pair%d_%d" % (u, h)) for u in range(2)]
+            for u in range(2):
+                nc.scalar.copy(out=y_pair[u][:], in_=y_bank[h][u][:])
+            y_sb = [y_pair[t // 2][:, t % 2, :] for t in range(PACK)]
+            for e in range(2):
+                for c in range(2):
+                    add_turned(pre0[h][:, c, e, :], y_sb[e][:, c * P : (c + 1) * P], False, e == 1 and c == 1)
+            z_turned = keep.tile([P, 2, P, 2], BF16, name="z_turned0_%d" % h)
+            nc.scalar.activation(out=z_turned[:], in_=pre0[h][:].rearrange("s c e p -> s c p e"), func=RELU)
+            back = psum.tile([P, 2, 2, P], F32, name="back%d" % h, tag="bank%d" % h)
+            for c in range(2):
+                add_turned(back[:, c, 0, :], z_turned[:, c].rearrange("s p e -> s (p e)").bitcast(F32), True, True)
+
+            for c in range(2):
+                chunk = 2 * h + c
+                tok = slice(chunk * P, (chunk + 1) * P)
+                pre1 = psum.tile([P, 2, P], F32, name="pre1_%d" % chunk, tag="bank%d" % (2 + c))
+                y_first = h > 0
+                if y_first:
+                    for e in range(2):
+                        add_turned(pre1[:, e, :], y_sb[2 + e][:, c * P : (c + 1) * P], e == 0, False)
+                for e in range(2):
+                    for l in range(3):
+                        g = gather_emb(2 + e, l, chunk * P, P, "late_%d_%d" % (e, l))
+                        add_turned(pre1[:, e, :], g[:], not y_first and e == 0 and l == 0, y_first and e == 1 and l == 2)
+                if not y_first:
+                    for e in range(2):
+                        add_turned(pre1[:, e, :], y_sb[2 + e][:, c * P : (c + 1) * P], False, e == 1)
+                z_turned = keep.tile([P, P, 2], BF16, name="z_turned1_%d" % chunk)
+                nc.scalar.activation(out=z_turned[:], in_=pre1[:].rearrange("s e p -> s p e"), func=RELU)
+                add_turned(back[:, c, 1, :], z_turned[:].rearrange("s p e -> s (p e)").bitcast(F32), True, True)
+                z_grouped = keep.tile([P, PACK * P], BF16, name="z_grouped%d" % chunk, align_bytes=64)
+                nc.scalar.copy(
+                    out=z_grouped[:].bitcast(F32).rearrange("p (s u) -> p s u", u=2),
+                    in_=back[:, c].rearrange("p u s -> p s u"),
+                )
+                z_codes = keep.tile([P, P], U32, name="z_codes%d" % chunk, align_bytes=64)
+                z_scales = keep.tile([P, P], U8, name="z_scales%d" % chunk, align_bytes=64)
+                nc.vector.quantize_mx(out=z_codes[:].bitcast(FP8X4), scales=z_scales[:], in_=z_grouped[:])
+                acc = psum.tile([P, PACK, P], F32, name="acc%d" % chunk, tag="bank%d" % (4 + chunk))
+                for t in range(PACK):
+                    nc.tensor.matmul_mx(
+                        out=acc[:, t, :],
+                        lhsT=w2_codes[:, t * P : (t + 1) * P].bitcast(FP8X4),
+                        lhsT_scale=w2_scales[:, t * P : (t + 1) * P],
+                        rhs=z_codes[:].bitcast(FP8X4),
+                        rhs_scale=z_scales[:],
+                        start=True,
+                        stop=True,
+                    )
+                result = keep.tile([P, PACK, P], F32, name="result%d" % chunk)
+                if chunk == CHUNKS - 1:
+                    nc.vector.tensor_copy(out=result[:], in_=acc[:])
+                else:
+                    nc.scalar.copy(out=result[:], in_=acc[:])
+                nc.sync.dma_start(out=out_view[:, :, tok], in_=result[:])

@@ -1,7 +1,6 @@
 from contextlib import ExitStack
 
 import concourse.mybir as mybir
-from concourse.masks import make_identity
 
 K, T, S, H, N, U = 1024, 2048, 512, 512, 512, 512
 FLOPS = 2 * K * H * S + 2 * H * N * S
@@ -15,6 +14,8 @@ U8 = mybir.dt.uint8
 FP8X4 = mybir.dt.float8_e4m3fn_x4
 COPY = mybir.ActivationFunctionType.Copy
 RELU = mybir.ActivationFunctionType.Relu
+ADD = mybir.AluOpType.add
+PIECES = ((0, 256), (256, 128), (384, 128))
 
 P = 128
 PACK = 4
@@ -31,8 +32,6 @@ def tile_picked_anc8_relu_p_kernel(tc, x_words, x_scales, w1, emb, w2, offs, up1
 
         x_scale_table = keep.tile([P, T], U8, name="x_scale_table", align_bytes=64)
         nc.gpsimd.memset(x_scale_table[:].bitcast(I32), 0)
-        ident = keep.tile([P, P], F32, name="ident")
-        make_identity(nc, ident[:])
         for q in range(4):
             nc.scalar.dma_start(
                 out=x_scale_table[32 * q : 32 * q + 4 * PASSES, :].bitcast(I32),
@@ -44,8 +43,8 @@ def tile_picked_anc8_relu_p_kernel(tc, x_words, x_scales, w1, emb, w2, offs, up1
         picks = keep.tile([P, S // 16], U16, name="picks")
         emb_table = [keep.tile([P, U], F32, name="emb_table%d" % t) for t in range(PACK)]
         w1_raw = [keep.tile([P, PACK, H], F32, name="w1_raw%d" % g) for g in range(PASSES)]
-        w2_raw = keep.tile([P, PACK, N], F32, name="w2_raw")
-        x_word_table = [keep.tile([P, T], I32, name="x_word_table%d" % g) for g in range(PASSES)]
+        w2_raw = keep.tile([P, PACK, N], F32, name="w2_raw", tag="z_grouped0", align_bytes=64)
+        x_word_table = [keep.tile([P, T], I32, name="x_word_table%d" % g, tag="x_word_table%d" % g) for g in range(PASSES)]
 
         def load_emb(t):
             nc.sync.dma_start(out=emb_table[t][:], in_=emb_planes[:, t, :])
@@ -64,27 +63,33 @@ def tile_picked_anc8_relu_p_kernel(tc, x_words, x_scales, w1, emb, w2, offs, up1
         load_w1(0)
         load_w1(1)
         nc.sync.dma_start(picks[:], offs)
-        nc.sync.dma_start(out=w2_raw[:], in_=w2.rearrange("(p j) c -> p j c", j=PACK))
         load_x(0)
         load_x(1)
         load_emb(2)
         load_emb(3)
+        nc.sync.dma_start(out=w2_raw[:], in_=w2.rearrange("(p j) c -> p j c", j=PACK))
 
-        def gather_emb(t, l, first, count, tag):
-            g = keep.tile([P, count], F32, name="anc_%d_%d_%d" % (t, l, first), tag=tag)
-            nc.vector.tensor_copy(out=g[:], in_=emb_table[t][:].indirect(ups[l][:, first // 16 : (first + count) // 16]))
-            return g
+        def looked_up(t, l, first, count):
+            return emb_table[t][:].indirect(ups[l][:, first // 16 : (first + count) // 16])
 
-        def add_turned(dst, src, start, stop):
-            nc.tensor.matmul(dst, lhsT=src, rhs=ident[:], start=start, stop=stop, is_transpose=True)
-
-        pre0 = [psum.tile([P, 2, 2, P], F32, name="pre0_%d" % h, tag="bank%d" % h) for h in range(2)]
+        early = [keep.tile([P, 2, 256], F32, name="early0"), None]
+        held = []
         for e in range(2):
+            part = [None, None]
             for l in range(3):
                 for h in range(2):
-                    g = gather_emb(e, l, h * 256, 256, "early_%d_%d_%d" % (e, l, h))
-                    for c in range(2):
-                        add_turned(pre0[h][:, c, e, :], g[:, c * P : (c + 1) * P], e == 0 and l == 0 and c == 0, False)
+                    if l == 2 and h == 1:
+                        held.append(part[h])
+                        continue
+                    if l == 2:
+                        dst = early[h][:, e, :]
+                    else:
+                        dst = keep.tile([P, 256], F32, name="early_part%d_%d_%d" % (e, l, h))[:]
+                    if l == 0:
+                        nc.vector.tensor_copy(out=dst, in_=looked_up(e, l, h * 256, 256))
+                    else:
+                        nc.vector.tensor_tensor(out=dst, in0=looked_up(e, l, h * 256, 256), in1=part[h], op=ADD)
+                    part[h] = dst
 
         w1_codes = []
         w1_scales = []
@@ -112,7 +117,7 @@ def tile_picked_anc8_relu_p_kernel(tc, x_words, x_scales, w1, emb, w2, offs, up1
 
         x_sc = keep.tile([P, S], U8, name="x_sc", align_bytes=64)
         nc.vector.tensor_copy(out=x_sc[:], in_=x_scale_table[:].indirect(picks[:]))
-        y_bank = [[psum.tile([P, 2, 256], F32, name="y_bank%d_%d" % (h, u), tag="bank%d" % (4 + 2 * h + u)) for u in range(2)] for h in range(2)]
+        y_bank = [[psum.tile([P, 2, 256], F32, name="y_bank%d_%d" % (h, u), tag="bank%d" % (2 * h + u)) for u in range(2)] for h in range(2)]
         for g in range(PASSES):
             x_cd = keep.tile([P, S], U32, name="x_cd%d" % g, align_bytes=64)
             if g < PASSES - 1:
@@ -121,7 +126,7 @@ def tile_picked_anc8_relu_p_kernel(tc, x_words, x_scales, w1, emb, w2, offs, up1
                 half = slice(h * 256, (h + 1) * 256)
                 if g == PASSES - 1:
                     nc.vector.tensor_copy(out=x_cd[:, half], in_=x_word_table[g][:].bitcast(U32).indirect(picks[:, h * 16 : (h + 1) * 16]))
-                for t in range(PACK):
+                for t in (2, 3, 0, 1):
                     nc.tensor.matmul_mx(
                         out=y_bank[h][t // 2][:, t % 2, :],
                         lhsT=w1_codes[g][:, t * P : (t + 1) * P].bitcast(FP8X4),
@@ -132,51 +137,47 @@ def tile_picked_anc8_relu_p_kernel(tc, x_words, x_scales, w1, emb, w2, offs, up1
                         stop=(g == PASSES - 1 and t % 2 == 1),
                     )
 
-        out_view = out.rearrange("(t p) s -> p t s", p=P)
-        for h in range(2):
-            y_pair = [keep.tile([P, 2, 256], F32, name="y_pair%d_%d" % (u, h)) for u in range(2)]
-            for u in range(2):
-                nc.scalar.copy(out=y_pair[u][:], in_=y_bank[h][u][:])
-            y_sb = [y_pair[t // 2][:, t % 2, :] for t in range(PACK)]
-            for e in range(2):
-                for c in range(2):
-                    add_turned(pre0[h][:, c, e, :], y_sb[e][:, c * P : (c + 1) * P], False, e == 1 and c == 1)
-            z_turned = keep.tile([P, 2, P, 2], BF16, name="z_turned0_%d" % h)
-            nc.scalar.activation(out=z_turned[:], in_=pre0[h][:].rearrange("s c e p -> s c p e"), func=RELU)
-            back = psum.tile([P, 2, 2, P], F32, name="back%d" % h, tag="bank%d" % h)
-            for c in range(2):
-                add_turned(back[:, c, 0, :], z_turned[:, c].rearrange("s p e -> s (p e)").bitcast(F32), True, True)
+        early[1] = keep.tile([P, 2, 256], F32, name="early1", tag="x_word_table1")
+        for e in range(2):
+            nc.vector.tensor_tensor(out=early[1][:, e, :], in0=looked_up(e, 2, 256, 256), in1=held[e], op=ADD)
 
-            for c in range(2):
-                chunk = 2 * h + c
-                tok = slice(chunk * P, (chunk + 1) * P)
-                pre1 = psum.tile([P, 2, P], F32, name="pre1_%d" % chunk, tag="bank%d" % (2 + c))
-                y_first = h > 0
-                if y_first:
-                    for e in range(2):
-                        add_turned(pre1[:, e, :], y_sb[2 + e][:, c * P : (c + 1) * P], e == 0, False)
+        out_view = out.rearrange("(t p) s -> p t s", p=P)
+        y_late = [keep.tile([P, 2, 256], F32, name="y_late%d" % h) for h in range(2)]
+        for h in range(2):
+            nc.scalar.copy(out=y_late[h][:], in_=y_bank[h][1][:])
+        banks_used = 4
+        for i, (first, count) in enumerate(PIECES):
+            h = first // 256
+            cols = slice(first - 256 * h, first - 256 * h + count)
+            last = i == len(PIECES) - 1
+            pre = keep.tile([P, PACK, count], F32, name="pre%d" % i)
+            nc.vector.tensor_tensor(out=pre[:, 0:2, :], in0=y_bank[h][0][:, :, cols], in1=early[h][:, :, cols], op=ADD)
+            part = [y_late[h][:, e, cols] for e in range(2)]
+            for l in range(3):
                 for e in range(2):
-                    for l in range(3):
-                        g = gather_emb(2 + e, l, chunk * P, P, "late_%d_%d" % (e, l))
-                        add_turned(pre1[:, e, :], g[:], not y_first and e == 0 and l == 0, y_first and e == 1 and l == 2)
-                if not y_first:
-                    for e in range(2):
-                        add_turned(pre1[:, e, :], y_sb[2 + e][:, c * P : (c + 1) * P], False, e == 1)
-                z_turned = keep.tile([P, P, 2], BF16, name="z_turned1_%d" % chunk)
-                nc.scalar.activation(out=z_turned[:], in_=pre1[:].rearrange("s e p -> s p e"), func=RELU)
-                add_turned(back[:, c, 1, :], z_turned[:].rearrange("s p e -> s (p e)").bitcast(F32), True, True)
-                z_grouped = keep.tile([P, PACK * P], BF16, name="z_grouped%d" % chunk, align_bytes=64)
-                nc.scalar.copy(
-                    out=z_grouped[:].bitcast(F32).rearrange("p (s u) -> p s u", u=2),
-                    in_=back[:, c].rearrange("p u s -> p s u"),
-                )
-                z_codes = keep.tile([P, P], U32, name="z_codes%d" % chunk, align_bytes=64)
-                z_scales = keep.tile([P, P], U8, name="z_scales%d" % chunk, align_bytes=64)
-                nc.vector.quantize_mx(out=z_codes[:].bitcast(FP8X4), scales=z_scales[:], in_=z_grouped[:])
-                acc = psum.tile([P, PACK, P], F32, name="acc%d" % chunk, tag="bank%d" % (4 + chunk))
-                for t in range(PACK):
+                    if l == 2:
+                        dst = pre[:, 2 + e, :]
+                    else:
+                        dst = keep.tile([P, count], F32, name="late_part%d_%d_%d" % (i, l, e), tag="z_grouped0" if last and l + e == 0 else "", align_bytes=64)[:]
+                    nc.vector.tensor_tensor(out=dst, in0=looked_up(2 + e, l, first, count), in1=part[e], op=ADD)
+                    part[e] = dst
+            z_grouped = keep.tile([P, PACK * count], BF16, name="z_grouped%d" % i, tag="z_grouped%d" % i, align_bytes=64)
+            z_out = z_grouped[:].rearrange("p (c i t) -> p c t i", i=4, t=PACK)
+            z_in = pre[:].rearrange("p t (c i) -> p c t i", i=4)
+            if last:
+                nc.vector.tensor_scalar_max(z_out, z_in, 0.0)
+            else:
+                nc.scalar.activation(out=z_out, in_=z_in, func=RELU)
+            z_codes = keep.tile([P, count], U32, name="z_codes%d" % i, align_bytes=64)
+            z_scales = keep.tile([P, count], U8, name="z_scales%d" % i, align_bytes=64)
+            nc.vector.quantize_mx(out=z_codes[:].bitcast(FP8X4), scales=z_scales[:], in_=z_grouped[:])
+            per_bank = 2 if last else 512 // count
+            for t0 in range(0, PACK, per_bank):
+                acc = psum.tile([P, per_bank, count], F32, name="acc%d_%d" % (i, t0), tag="bank%d" % (banks_used % 8))
+                banks_used = banks_used + 1
+                for t in range(t0, t0 + per_bank):
                     nc.tensor.matmul_mx(
-                        out=acc[:, t, :],
+                        out=acc[:, t - t0, :],
                         lhsT=w2_codes[:, t * P : (t + 1) * P].bitcast(FP8X4),
                         lhsT_scale=w2_scales[:, t * P : (t + 1) * P],
                         rhs=z_codes[:].bitcast(FP8X4),
@@ -184,9 +185,9 @@ def tile_picked_anc8_relu_p_kernel(tc, x_words, x_scales, w1, emb, w2, offs, up1
                         start=True,
                         stop=True,
                     )
-                result = keep.tile([P, PACK, P], F32, name="result%d" % chunk)
-                if chunk == CHUNKS - 1:
+                result = keep.tile([P, per_bank, count], F32, name="result%d_%d" % (i, t0))
+                if last and t0 > 0:
                     nc.vector.tensor_copy(out=result[:], in_=acc[:])
                 else:
                     nc.scalar.copy(out=result[:], in_=acc[:])
-                nc.sync.dma_start(out=out_view[:, :, tok], in_=result[:])
+                nc.sync.dma_start(out=out_view[:, t0 : t0 + per_bank, first : first + count], in_=result[:])

@@ -15,7 +15,8 @@ FP8X4 = mybir.dt.float8_e4m3fn_x4
 COPY = mybir.ActivationFunctionType.Copy
 RELU = mybir.ActivationFunctionType.Relu
 ADD = mybir.AluOpType.add
-PIECES = ((0, 256), (256, 128), (384, 128))
+HALF = S // 2
+PIECES = (1, 2)
 
 P = 128
 PACK = 4
@@ -31,23 +32,21 @@ def tile_picked_anc8_relu_p_kernel(tc, x_words, x_scales, w1, emb, w2, offs, up1
         psum = ctx.enter_context(tc.psum_pool(name="psum", bufs=1))
 
         x_scale_table = keep.tile([P, T], U8, name="x_scale_table", align_bytes=64)
-        nc.gpsimd.memset(x_scale_table[:].bitcast(I32), 0)
-        for q in range(4):
-            nc.scalar.dma_start(
-                out=x_scale_table[32 * q : 32 * q + 4 * PASSES, :].bitcast(I32),
-                in_=x_scales[:, 4 * q : 4 * q + 4, :].bitcast(I32),
-            )
 
         emb_planes = emb.rearrange("(p t) u -> p t u", t=PACK)
         ups = [keep.tile([P, S // 16], U16, name="up_list%d" % l) for l in range(3)]
         picks = keep.tile([P, S // 16], U16, name="picks")
-        emb_table = [keep.tile([P, U], F32, name="emb_table%d" % t) for t in range(PACK)]
+        emb_table = [keep.tile([P, 2 * U if t < 2 else U], F32, name="emb_table%d" % t) for t in range(PACK)]
         w1_raw = [keep.tile([P, PACK, H], F32, name="w1_raw%d" % g) for g in range(PASSES)]
-        w2_raw = keep.tile([P, PACK, N], F32, name="w2_raw", tag="z_grouped0", align_bytes=64)
+        w2_raw = keep.tile([P, PACK, N], F32, name="w2_raw", tag="w2_raw", align_bytes=64)
         x_word_table = [keep.tile([P, T], I32, name="x_word_table%d" % g, tag="x_word_table%d" % g) for g in range(PASSES)]
 
+        for t in range(2):
+            nc.gpsimd.memset(emb_table[t][:, U : 2 * U], 0.0)
+        nc.gpsimd.memset(x_scale_table[:].bitcast(I32), 0)
+
         def load_emb(t):
-            nc.sync.dma_start(out=emb_table[t][:], in_=emb_planes[:, t, :])
+            nc.sync.dma_start(out=emb_table[t][:, 0:U], in_=emb_planes[:, t, :])
 
         def load_w1(g):
             nc.sync.dma_start(out=w1_raw[g][:], in_=w1[g * 512 : (g + 1) * 512, :].rearrange("(p j) c -> p j c", j=PACK))
@@ -57,12 +56,17 @@ def tile_picked_anc8_relu_p_kernel(tc, x_words, x_scales, w1, emb, w2, offs, up1
 
         nc.sync.dma_start(ups[0][:], up1)
         load_emb(0)
+        load_emb(1)
         nc.sync.dma_start(ups[1][:], up2)
         nc.sync.dma_start(ups[2][:], up3)
-        load_emb(1)
         load_w1(0)
-        load_w1(1)
+        for q in range(4):
+            nc.sync.dma_start(
+                out=x_scale_table[32 * q : 32 * q + 4 * PASSES, :].bitcast(I32),
+                in_=x_scales[:, 4 * q : 4 * q + 4, :].bitcast(I32),
+            )
         nc.sync.dma_start(picks[:], offs)
+        load_w1(1)
         load_x(0)
         load_x(1)
         load_emb(2)
@@ -72,24 +76,17 @@ def tile_picked_anc8_relu_p_kernel(tc, x_words, x_scales, w1, emb, w2, offs, up1
         def looked_up(t, l, first, count):
             return emb_table[t][:].indirect(ups[l][:, first // 16 : (first + count) // 16])
 
-        early = [keep.tile([P, 2, 256], F32, name="early0"), None]
-        held = []
-        for e in range(2):
-            part = [None, None]
-            for l in range(3):
-                for h in range(2):
-                    if l == 2 and h == 1:
-                        held.append(part[h])
-                        continue
-                    if l == 2:
-                        dst = early[h][:, e, :]
-                    else:
-                        dst = keep.tile([P, 256], F32, name="early_part%d_%d_%d" % (e, l, h))[:]
-                    if l == 0:
-                        nc.vector.tensor_copy(out=dst, in_=looked_up(e, l, h * 256, 256))
-                    else:
-                        nc.vector.tensor_tensor(out=dst, in0=looked_up(e, l, h * 256, 256), in1=part[h], op=ADD)
-                    part[h] = dst
+        part = [None, None]
+        for l in range(2):
+            for e in range(2):
+                dst = keep.tile([P, S], F32, name="early_part%d_%d" % (e, l))
+                if l == 0:
+                    nc.vector.tensor_copy(out=dst[:], in_=looked_up(e, l, 0, S))
+                else:
+                    nc.vector.tensor_tensor(out=dst[:], in0=looked_up(e, l, 0, S), in1=part[e][:], op=ADD)
+                part[e] = dst
+        early = [keep.tile([P, S], F32, name="early0"), None]
+        nc.vector.tensor_tensor(out=early[0][:], in0=looked_up(0, 2, 0, S), in1=part[0][:], op=ADD)
 
         w1_codes = []
         w1_scales = []
@@ -117,77 +114,100 @@ def tile_picked_anc8_relu_p_kernel(tc, x_words, x_scales, w1, emb, w2, offs, up1
 
         x_sc = keep.tile([P, S], U8, name="x_sc", align_bytes=64)
         nc.vector.tensor_copy(out=x_sc[:], in_=x_scale_table[:].indirect(picks[:]))
-        y_bank = [[psum.tile([P, 2, 256], F32, name="y_bank%d_%d" % (h, u), tag="bank%d" % (2 * h + u)) for u in range(2)] for h in range(2)]
+        x_cd = [keep.tile([P, S], U32, name="x_cd%d" % g, align_bytes=64) for g in range(PASSES)]
         for g in range(PASSES):
-            x_cd = keep.tile([P, S], U32, name="x_cd%d" % g, align_bytes=64)
-            if g < PASSES - 1:
-                nc.vector.tensor_copy(out=x_cd[:], in_=x_word_table[g][:].bitcast(U32).indirect(picks[:]))
-            for h in range(2):
-                half = slice(h * 256, (h + 1) * 256)
-                if g == PASSES - 1:
-                    nc.vector.tensor_copy(out=x_cd[:, half], in_=x_word_table[g][:].bitcast(U32).indirect(picks[:, h * 16 : (h + 1) * 16]))
-                for t in (2, 3, 0, 1):
+            nc.vector.tensor_copy(out=x_cd[g][:], in_=x_word_table[g][:].bitcast(U32).indirect(picks[:]))
+        early[1] = keep.tile([P, S], F32, name="early1", tag="x_word_table1")
+        nc.vector.tensor_tensor(out=early[1][:], in0=looked_up(1, 2, 0, S), in1=part[1][:], op=ADD)
+
+        def first_layer(h, u):
+            bank = psum.tile([P, 2, HALF], F32, name="y_bank%d_%d" % (h, u), tag="bank%d" % h)
+            cols = slice(h * HALF, (h + 1) * HALF)
+            for g in range(PASSES):
+                for e in range(2):
+                    t = 2 * u + e
                     nc.tensor.matmul_mx(
-                        out=y_bank[h][t // 2][:, t % 2, :],
+                        out=bank[:, e, :],
                         lhsT=w1_codes[g][:, t * P : (t + 1) * P].bitcast(FP8X4),
                         lhsT_scale=w1_scales[g][:, t * P : (t + 1) * P],
-                        rhs=x_cd[:, half].bitcast(FP8X4),
-                        rhs_scale=x_sc[4 * g : P, half],
-                        start=(g == 0 and t % 2 == 0),
-                        stop=(g == PASSES - 1 and t % 2 == 1),
+                        rhs=x_cd[g][:, cols].bitcast(FP8X4),
+                        rhs_scale=x_sc[4 * g : P, cols],
+                        start=(g == 0 and e == 0),
+                        stop=(g == PASSES - 1 and e == 1),
                     )
+            return bank
 
-        early[1] = keep.tile([P, 2, 256], F32, name="early1", tag="x_word_table1")
-        for e in range(2):
-            nc.vector.tensor_tensor(out=early[1][:, e, :], in0=looked_up(e, 2, 256, 256), in1=held[e], op=ADD)
+        y_late = []
+        for h in range(2):
+            bank = first_layer(h, 1)
+            y_sb = keep.tile([P, 2, HALF], F32, name="y_late%d" % h)
+            nc.scalar.copy(out=y_sb[:], in_=bank[:])
+            y_late.append(y_sb)
+        y_early_bank = [first_layer(h, 0) for h in range(2)]
 
         out_view = out.rearrange("(t p) s -> p t s", p=P)
-        y_late = [keep.tile([P, 2, 256], F32, name="y_late%d" % h) for h in range(2)]
+        banks_used = 2
         for h in range(2):
-            nc.scalar.copy(out=y_late[h][:], in_=y_bank[h][1][:])
-        banks_used = 4
-        for i, (first, count) in enumerate(PIECES):
-            h = first // 256
-            cols = slice(first - 256 * h, first - 256 * h + count)
-            last = i == len(PIECES) - 1
-            pre = keep.tile([P, PACK, count], F32, name="pre%d" % i)
-            nc.vector.tensor_tensor(out=pre[:, 0:2, :], in0=y_bank[h][0][:, :, cols], in1=early[h][:, :, cols], op=ADD)
-            part = [y_late[h][:, e, cols] for e in range(2)]
-            for l in range(3):
+            half = slice(h * HALF, (h + 1) * HALF)
+            pieces = PIECES[h]
+            count = HALF // pieces
+            second = y_late[h]
+            for l in range(2):
+                before = second
+                second = keep.tile([P, 2, HALF], F32, name="late_part%d_%d" % (h, l))
                 for e in range(2):
-                    if l == 2:
-                        dst = pre[:, 2 + e, :]
-                    else:
-                        dst = keep.tile([P, count], F32, name="late_part%d_%d_%d" % (i, l, e), tag="z_grouped0" if last and l + e == 0 else "", align_bytes=64)[:]
-                    nc.vector.tensor_tensor(out=dst, in0=looked_up(2 + e, l, first, count), in1=part[e], op=ADD)
-                    part[e] = dst
-            z_grouped = keep.tile([P, PACK * count], BF16, name="z_grouped%d" % i, tag="z_grouped%d" % i, align_bytes=64)
-            z_out = z_grouped[:].rearrange("p (c i t) -> p c t i", i=4, t=PACK)
-            z_in = pre[:].rearrange("p t (c i) -> p c t i", i=4)
-            if last:
-                nc.vector.tensor_scalar_max(z_out, z_in, 0.0)
-            else:
-                nc.scalar.activation(out=z_out, in_=z_in, func=RELU)
-            z_codes = keep.tile([P, count], U32, name="z_codes%d" % i, align_bytes=64)
-            z_scales = keep.tile([P, count], U8, name="z_scales%d" % i, align_bytes=64)
-            nc.vector.quantize_mx(out=z_codes[:].bitcast(FP8X4), scales=z_scales[:], in_=z_grouped[:])
-            per_bank = 2 if last else 512 // count
-            for t0 in range(0, PACK, per_bank):
-                acc = psum.tile([P, per_bank, count], F32, name="acc%d_%d" % (i, t0), tag="bank%d" % (banks_used % 8))
-                banks_used = banks_used + 1
-                for t in range(t0, t0 + per_bank):
-                    nc.tensor.matmul_mx(
-                        out=acc[:, t - t0, :],
-                        lhsT=w2_codes[:, t * P : (t + 1) * P].bitcast(FP8X4),
-                        lhsT_scale=w2_scales[:, t * P : (t + 1) * P],
-                        rhs=z_codes[:].bitcast(FP8X4),
-                        rhs_scale=z_scales[:],
-                        start=True,
-                        stop=True,
+                    nc.vector.tensor_tensor(out=second[:, e, :], in0=looked_up(2 + e, l, h * HALF, HALF), in1=before[:, e, :], op=ADD)
+            pre = keep.tile([P, pieces, PACK, count], F32, name="pre%d" % h, tag="w2_raw" if h == 1 else "", align_bytes=64)
+            for e in range(2):
+                nc.vector.tensor_tensor(
+                    out=pre[:, :, e, :],
+                    in0=y_early_bank[h][:, e, :].rearrange("p (i s) -> p i s", i=pieces),
+                    in1=early[e][:, half].rearrange("p (i s) -> p i s", i=pieces),
+                    op=ADD,
+                )
+            z_grouped = []
+            for i in range(pieces):
+                for e in range(2):
+                    nc.vector.tensor_tensor(
+                        out=pre[:, i, 2 + e, :],
+                        in0=looked_up(2 + e, 2, h * HALF + i * count, count),
+                        in1=second[:, e, i * count : (i + 1) * count],
+                        op=ADD,
                     )
-                result = keep.tile([P, per_bank, count], F32, name="result%d_%d" % (i, t0))
-                if last and t0 > 0:
-                    nc.vector.tensor_copy(out=result[:], in_=acc[:])
+                if h == 0:
+                    grouped = w2_raw[:, 0, :].bitcast(BF16)
                 else:
-                    nc.scalar.copy(out=result[:], in_=acc[:])
-                nc.sync.dma_start(out=out_view[:, t0 : t0 + per_bank, first : first + count], in_=result[:])
+                    grouped = keep.tile([P, PACK * count], BF16, name="z_grouped%d" % i, align_bytes=64)[:]
+                z_out = grouped.rearrange("p (c i t) -> p c t i", i=4, t=PACK)
+                z_in = pre[:, i].rearrange("p t (c i) -> p c t i", i=4)
+                if h == 1 and i == pieces - 1:
+                    nc.vector.tensor_scalar_max(z_out, z_in, 0.0)
+                else:
+                    nc.scalar.activation(out=z_out, in_=z_in, func=RELU)
+                z_grouped.append(grouped)
+            for i in range(pieces):
+                last = h == 1 and i == pieces - 1
+                z_codes = keep.tile([P, count], U32, name="z_codes%d_%d" % (h, i), align_bytes=64)
+                z_scales = keep.tile([P, count], U8, name="z_scales%d_%d" % (h, i), align_bytes=64)
+                nc.vector.quantize_mx(out=z_codes[:].bitcast(FP8X4), scales=z_scales[:], in_=z_grouped[i])
+                per_bank = 2 if last else 512 // count
+                for t0 in range(0, PACK, per_bank):
+                    acc = psum.tile([P, per_bank, count], F32, name="acc%d" % banks_used, tag="bank%d" % (banks_used % 8))
+                    banks_used = banks_used + 1
+                    for t in range(t0, t0 + per_bank):
+                        nc.tensor.matmul_mx(
+                            out=acc[:, t - t0, :],
+                            lhsT=w2_codes[:, t * P : (t + 1) * P].bitcast(FP8X4),
+                            lhsT_scale=w2_scales[:, t * P : (t + 1) * P],
+                            rhs=z_codes[:].bitcast(FP8X4),
+                            rhs_scale=z_scales[:],
+                            start=True,
+                            stop=True,
+                        )
+                    result = keep.tile([P, per_bank, count], F32, name="result%d" % banks_used)
+                    if last:
+                        nc.vector.tensor_copy(out=result[:], in_=acc[:])
+                    else:
+                        nc.scalar.copy(out=result[:], in_=acc[:])
+                    first = h * HALF + i * count
+                    nc.sync.dma_start(out=out_view[:, t0 : t0 + per_bank, first : first + count], in_=result[:])

@@ -15,14 +15,12 @@ FP8X4 = mybir.dt.float8_e4m3fn_x4
 COPY = mybir.ActivationFunctionType.Copy
 RELU = mybir.ActivationFunctionType.Relu
 ADD = mybir.AluOpType.add
-HALF = S // 2
-PIECES = (1, 2)
 
 P = 128
 PACK = 4
 PASSES = K // (P * PACK)
-CHUNK = 128
-CHUNKS = S // CHUNK
+HALF = S // 2
+QUARTER = S // 4
 
 
 def tile_picked_anc8_relu_p_kernel(tc, x_words, x_scales, w1, emb, w2, offs, up1, up2, up3, out):
@@ -32,21 +30,23 @@ def tile_picked_anc8_relu_p_kernel(tc, x_words, x_scales, w1, emb, w2, offs, up1
         psum = ctx.enter_context(tc.psum_pool(name="psum", bufs=1))
 
         x_scale_table = keep.tile([P, T], U8, name="x_scale_table", align_bytes=64)
-
         emb_planes = emb.rearrange("(p t) u -> p t u", t=PACK)
         ups = [keep.tile([P, S // 16], U16, name="up_list%d" % l) for l in range(3)]
         picks = keep.tile([P, S // 16], U16, name="picks")
-        emb_table = [keep.tile([P, 2 * U if t < 2 else U], F32, name="emb_table%d" % t) for t in range(PACK)]
+        emb_wide = [keep.tile([P, 2 * U], F32, name="emb_wide%d" % t) for t in range(PACK)]
+        emb_narrow = [keep.tile([P, U], F32, name="emb_narrow%d" % e) for e in range(2)]
         w1_raw = [keep.tile([P, PACK, H], F32, name="w1_raw%d" % g) for g in range(PASSES)]
         w2_raw = keep.tile([P, PACK, N], F32, name="w2_raw", tag="w2_raw", align_bytes=64)
         x_word_table = [keep.tile([P, T], I32, name="x_word_table%d" % g, tag="x_word_table%d" % g) for g in range(PASSES)]
 
         for t in range(2):
-            nc.gpsimd.memset(emb_table[t][:, U : 2 * U], 0.0)
+            nc.vector.memset(emb_wide[t][:, U : 2 * U], 0.0)
         nc.gpsimd.memset(x_scale_table[:].bitcast(I32), 0)
+        for t in range(2, PACK):
+            nc.gpsimd.memset(emb_wide[t][:, U : 2 * U], 0.0)
 
-        def load_emb(t):
-            nc.sync.dma_start(out=emb_table[t][:, 0:U], in_=emb_planes[:, t, :])
+        def load_emb(table, t):
+            nc.sync.dma_start(out=table[:, 0:U], in_=emb_planes[:, t, :])
 
         def load_w1(g):
             nc.sync.dma_start(out=w1_raw[g][:], in_=w1[g * 512 : (g + 1) * 512, :].rearrange("(p j) c -> p j c", j=PACK))
@@ -55,8 +55,8 @@ def tile_picked_anc8_relu_p_kernel(tc, x_words, x_scales, w1, emb, w2, offs, up1
             nc.sync.dma_start(out=x_word_table[g][:], in_=x_words[g].rearrange("p n t -> p (n t)").bitcast(I32))
 
         nc.sync.dma_start(ups[0][:], up1)
-        load_emb(0)
-        load_emb(1)
+        load_emb(emb_wide[0], 0)
+        load_emb(emb_wide[1], 1)
         nc.sync.dma_start(ups[1][:], up2)
         nc.sync.dma_start(ups[2][:], up3)
         load_w1(0)
@@ -69,24 +69,31 @@ def tile_picked_anc8_relu_p_kernel(tc, x_words, x_scales, w1, emb, w2, offs, up1
         load_w1(1)
         load_x(0)
         load_x(1)
-        load_emb(2)
-        load_emb(3)
+        load_emb(emb_wide[2], 2)
+        load_emb(emb_wide[3], 3)
         nc.sync.dma_start(out=w2_raw[:], in_=w2.rearrange("(p j) c -> p j c", j=PACK))
+        for e in range(2):
+            load_emb(emb_narrow[e], 2 + e)
 
-        def looked_up(t, l, first, count):
-            return emb_table[t][:].indirect(ups[l][:, first // 16 : (first + count) // 16])
+        def looked_up(table, l, first, count):
+            return table[:].indirect(ups[l][:, first // 16 : (first + count) // 16])
 
         part = [None, None]
         for l in range(2):
             for e in range(2):
                 dst = keep.tile([P, S], F32, name="early_part%d_%d" % (e, l))
                 if l == 0:
-                    nc.vector.tensor_copy(out=dst[:], in_=looked_up(e, l, 0, S))
+                    nc.vector.tensor_copy(out=dst[:], in_=looked_up(emb_wide[e], l, 0, S))
                 else:
-                    nc.vector.tensor_tensor(out=dst[:], in0=looked_up(e, l, 0, S), in1=part[e][:], op=ADD)
+                    nc.vector.tensor_tensor(out=dst[:], in0=looked_up(emb_wide[e], l, 0, S), in1=part[e][:], op=ADD)
                 part[e] = dst
-        early = [keep.tile([P, S], F32, name="early0"), None]
-        nc.vector.tensor_tensor(out=early[0][:], in0=looked_up(0, 2, 0, S), in1=part[0][:], op=ADD)
+
+        def early_sum(e, tag):
+            total = keep.tile([P, S], F32, name="early%d" % e, tag=tag)
+            nc.vector.tensor_tensor(out=total[:], in0=looked_up(emb_wide[e], 2, 0, S), in1=part[e][:], op=ADD)
+            return total
+
+        early = [early_sum(0, "early0"), None]
 
         w1_codes = []
         w1_scales = []
@@ -102,112 +109,119 @@ def tile_picked_anc8_relu_p_kernel(tc, x_words, x_scales, w1, emb, w2, offs, up1
             nc.vector.quantize_mx(out=codes[:].bitcast(FP8X4), scales=scales[:], in_=grouped[:])
             w1_codes.append(codes)
             w1_scales.append(scales)
-        w2_grouped = keep.tile([P, PACK * N], BF16, name="w2_grouped", align_bytes=64)
-        nc.scalar.activation(
-            out=w2_grouped[:].rearrange("p (c i j) -> p c j i", i=4, j=PACK),
-            in_=w2_raw[:].rearrange("p j (c i) -> p c j i", i=4),
-            func=COPY,
-        )
-        w2_codes = keep.tile([P, N], U32, name="w2_codes", align_bytes=64)
-        w2_scales = keep.tile([P, N], U8, name="w2_scales", align_bytes=64)
-        nc.vector.quantize_mx(out=w2_codes[:].bitcast(FP8X4), scales=w2_scales[:], in_=w2_grouped[:])
 
         x_sc = keep.tile([P, S], U8, name="x_sc", align_bytes=64)
         nc.vector.tensor_copy(out=x_sc[:], in_=x_scale_table[:].indirect(picks[:]))
         x_cd = [keep.tile([P, S], U32, name="x_cd%d" % g, align_bytes=64) for g in range(PASSES)]
         for g in range(PASSES):
             nc.vector.tensor_copy(out=x_cd[g][:], in_=x_word_table[g][:].bitcast(U32).indirect(picks[:]))
-        early[1] = keep.tile([P, S], F32, name="early1", tag="x_word_table1")
-        nc.vector.tensor_tensor(out=early[1][:], in0=looked_up(1, 2, 0, S), in1=part[1][:], op=ADD)
+        early[1] = early_sum(1, "x_word_table1")
 
-        def first_layer(h, u):
-            bank = psum.tile([P, 2, HALF], F32, name="y_bank%d_%d" % (h, u), tag="bank%d" % h)
-            cols = slice(h * HALF, (h + 1) * HALF)
+        def first_layer(t):
+            bank = psum.tile([P, S], F32, name="y_bank%d" % t, tag="bank%d" % (t % 2))
             for g in range(PASSES):
-                for e in range(2):
-                    t = 2 * u + e
-                    nc.tensor.matmul_mx(
-                        out=bank[:, e, :],
-                        lhsT=w1_codes[g][:, t * P : (t + 1) * P].bitcast(FP8X4),
-                        lhsT_scale=w1_scales[g][:, t * P : (t + 1) * P],
-                        rhs=x_cd[g][:, cols].bitcast(FP8X4),
-                        rhs_scale=x_sc[4 * g : P, cols],
-                        start=(g == 0 and e == 0),
-                        stop=(g == PASSES - 1 and e == 1),
-                    )
+                nc.tensor.matmul_mx(
+                    out=bank[:],
+                    lhsT=w1_codes[g][:, t * P : (t + 1) * P].bitcast(FP8X4),
+                    lhsT_scale=w1_scales[g][:, t * P : (t + 1) * P],
+                    rhs=x_cd[g][:].bitcast(FP8X4),
+                    rhs_scale=x_sc[4 * g : P, :],
+                    start=(g == 0),
+                    stop=(g == PASSES - 1),
+                )
             return bank
 
-        y_late = []
-        for h in range(2):
-            bank = first_layer(h, 1)
-            y_sb = keep.tile([P, 2, HALF], F32, name="y_late%d" % h)
-            nc.scalar.copy(out=y_sb[:], in_=bank[:])
-            y_late.append(y_sb)
-        y_early_bank = [first_layer(h, 0) for h in range(2)]
+        y_late = keep.tile([P, 2, S], F32, name="y_late", tag="sums", align_bytes=64)
+        for e in range(2):
+            nc.scalar.copy(out=y_late[:, e, :], in_=first_layer(2 + e)[:])
+        y_early_bank = [first_layer(e) for e in range(2)]
+
+        w2_grouped = keep.tile([P, PACK * N], BF16, name="w2_grouped", align_bytes=64)
+        nc.scalar.activation(
+            out=w2_grouped[:].rearrange("p (c i j) -> p c j i", i=4, j=PACK),
+            in_=w2_raw[:].rearrange("p j (c i) -> p c j i", i=4),
+            func=COPY,
+        )
+
+        late = y_late
+        for l in range(2):
+            before = late
+            late = keep.tile([P, 2, S], F32, name="late_part%d" % l)
+            for e in range(2):
+                nc.vector.tensor_tensor(out=late[:, e, :], in0=looked_up(emb_wide[2 + e], l, 0, S), in1=before[:, e, :], op=ADD)
 
         out_view = out.rearrange("(t p) s -> p t s", p=P)
-        banks_used = 2
-        for h in range(2):
-            half = slice(h * HALF, (h + 1) * HALF)
-            pieces = PIECES[h]
-            count = HALF // pieces
-            second = y_late[h]
-            for l in range(2):
-                before = second
-                second = keep.tile([P, 2, HALF], F32, name="late_part%d_%d" % (h, l))
-                for e in range(2):
-                    nc.vector.tensor_tensor(out=second[:, e, :], in0=looked_up(2 + e, l, h * HALF, HALF), in1=before[:, e, :], op=ADD)
-            pre = keep.tile([P, pieces, PACK, count], F32, name="pre%d" % h, tag="w2_raw" if h == 1 else "", align_bytes=64)
+        overlap = 2 * QUARTER
+        pre = keep.tile([P, 2 * PACK * HALF - overlap], F32, name="pre", tag="sums", align_bytes=64)
+        half_planes = pre[:, PACK * HALF - overlap :].rearrange("p (t s) -> p t s", t=PACK)
+        quarters = pre[:, 0 : PACK * HALF].rearrange("p (i t s) -> p i t s", i=2, t=PACK)
+
+        def last_step(tables, planes, first, count):
             for e in range(2):
-                nc.vector.tensor_tensor(
-                    out=pre[:, :, e, :],
-                    in0=y_early_bank[h][:, e, :].rearrange("p (i s) -> p i s", i=pieces),
-                    in1=early[e][:, half].rearrange("p (i s) -> p i s", i=pieces),
-                    op=ADD,
+                nc.vector.tensor_tensor(out=planes[:, 2 + e, :], in0=looked_up(tables[e], 2, first, count), in1=late[:, e, first : first + count], op=ADD)
+
+        def views(planes, grouped):
+            return grouped.rearrange("p (c i t) -> p c t i", i=4, t=PACK), planes.rearrange("p t (c i) -> p c t i", i=4)
+
+        def quantised(name, grouped, count):
+            codes = keep.tile([P, count], U32, name=name + "_codes", align_bytes=64)
+            scales = keep.tile([P, count], U8, name=name + "_scales", align_bytes=64)
+            nc.vector.quantize_mx(out=codes[:].bitcast(FP8X4), scales=scales[:], in_=grouped)
+            return codes, scales
+
+        def second_layer(z, first, count, t0, tiles, bank_number):
+            acc = psum.tile([P, tiles, count], F32, name="acc%d_%d" % (first, t0), tag="bank%d" % bank_number)
+            for t in range(t0, t0 + tiles):
+                nc.tensor.matmul_mx(
+                    out=acc[:, t - t0, :],
+                    lhsT=w2_codes[:, t * P : (t + 1) * P].bitcast(FP8X4),
+                    lhsT_scale=w2_scales[:, t * P : (t + 1) * P],
+                    rhs=z[0][:].bitcast(FP8X4),
+                    rhs_scale=z[1][:],
+                    start=True,
+                    stop=True,
                 )
-            z_grouped = []
-            for i in range(pieces):
-                for e in range(2):
-                    nc.vector.tensor_tensor(
-                        out=pre[:, i, 2 + e, :],
-                        in0=looked_up(2 + e, 2, h * HALF + i * count, count),
-                        in1=second[:, e, i * count : (i + 1) * count],
-                        op=ADD,
-                    )
-                if h == 0:
-                    grouped = w2_raw[:, 0, :].bitcast(BF16)
-                else:
-                    grouped = keep.tile([P, PACK * count], BF16, name="z_grouped%d" % i, align_bytes=64)[:]
-                z_out = grouped.rearrange("p (c i t) -> p c t i", i=4, t=PACK)
-                z_in = pre[:, i].rearrange("p t (c i) -> p c t i", i=4)
-                if h == 1 and i == pieces - 1:
-                    nc.vector.tensor_scalar_max(z_out, z_in, 0.0)
-                else:
-                    nc.scalar.activation(out=z_out, in_=z_in, func=RELU)
-                z_grouped.append(grouped)
-            for i in range(pieces):
-                last = h == 1 and i == pieces - 1
-                z_codes = keep.tile([P, count], U32, name="z_codes%d_%d" % (h, i), align_bytes=64)
-                z_scales = keep.tile([P, count], U8, name="z_scales%d_%d" % (h, i), align_bytes=64)
-                nc.vector.quantize_mx(out=z_codes[:].bitcast(FP8X4), scales=z_scales[:], in_=z_grouped[i])
-                per_bank = 2 if last else 512 // count
-                for t0 in range(0, PACK, per_bank):
-                    acc = psum.tile([P, per_bank, count], F32, name="acc%d" % banks_used, tag="bank%d" % (banks_used % 8))
-                    banks_used = banks_used + 1
-                    for t in range(t0, t0 + per_bank):
-                        nc.tensor.matmul_mx(
-                            out=acc[:, t - t0, :],
-                            lhsT=w2_codes[:, t * P : (t + 1) * P].bitcast(FP8X4),
-                            lhsT_scale=w2_scales[:, t * P : (t + 1) * P],
-                            rhs=z_codes[:].bitcast(FP8X4),
-                            rhs_scale=z_scales[:],
-                            start=True,
-                            stop=True,
-                        )
-                    result = keep.tile([P, per_bank, count], F32, name="result%d" % banks_used)
-                    if last:
-                        nc.vector.tensor_copy(out=result[:], in_=acc[:])
-                    else:
-                        nc.scalar.copy(out=result[:], in_=acc[:])
-                    first = h * HALF + i * count
-                    nc.sync.dma_start(out=out_view[:, t0 : t0 + per_bank, first : first + count], in_=result[:])
+            result = keep.tile([P, tiles, count], F32, name="result%d_%d" % (first, t0))
+            return acc, result, out_view[:, t0 : t0 + tiles, first : first + count]
+
+        for e in range(2):
+            nc.vector.tensor_tensor(out=half_planes[:, e, :], in0=y_early_bank[e][:, 0:HALF], in1=early[e][:, 0:HALF], op=ADD)
+        last_step(emb_wide[2:], half_planes, 0, HALF)
+        half_grouped = keep.tile([P, PACK * HALF], BF16, name="z_grouped0", tag="w2_raw", align_bytes=64)
+        z_out, z_in = views(half_planes, half_grouped[:])
+        nc.scalar.activation(out=z_out, in_=z_in, func=RELU)
+
+        for e in range(2):
+            nc.vector.tensor_tensor(
+                out=quarters[:, :, e, :],
+                in0=y_early_bank[e][:, HALF:S].rearrange("p (i s) -> p i s", i=2),
+                in1=early[e][:, HALF:S].rearrange("p (i s) -> p i s", i=2),
+                op=ADD,
+            )
+        w2_codes, w2_scales = quantised("w2", w2_grouped[:], N)
+        last_step(emb_narrow, quarters[:, 0], HALF, QUARTER)
+        z = quantised("z0", half_grouped[:], HALF)
+        third_grouped = pre[:, 2 * PACK * HALF - overlap - 2 * QUARTER :].bitcast(BF16)
+        z_out, z_in = views(quarters[:, 0], third_grouped)
+        nc.scalar.activation(out=z_out, in_=z_in, func=RELU)
+        for t0 in (0, 2):
+            acc, result, target = second_layer(z, 0, HALF, t0, 2, 4 + t0 // 2)
+            nc.scalar.copy(out=result[:], in_=acc[:])
+            nc.sync.dma_start(out=target, in_=result[:])
+
+        last_step(emb_narrow, quarters[:, 1], HALF + QUARTER, QUARTER)
+        z = quantised("z1", third_grouped, QUARTER)
+        acc, result, target = second_layer(z, HALF, QUARTER, 0, 4, 6)
+        nc.scalar.copy(out=result[:], in_=acc[:])
+        nc.sync.dma_start(out=target, in_=result[:])
+
+        last_grouped = pre[:, 0 : 2 * QUARTER].bitcast(BF16)
+        z_out, z_in = views(quarters[:, 1], last_grouped)
+        nc.vector.tensor_scalar_max(z_out, z_in, 0.0)
+        z = quantised("z2", last_grouped, QUARTER)
+        acc, result, target = second_layer(z, HALF + QUARTER, QUARTER, 0, 2, 7)
+        nc.vector.tensor_copy(out=result[:], in_=acc[:])
+        nc.sync.dma_start(out=target, in_=result[:])
+        acc, result, target = second_layer(z, HALF + QUARTER, QUARTER, 2, 2, 2)
+        nc.vector.tensor_copy(out=result[:], in_=acc[:])
+        nc.sync.dma_start(out=target, in_=result[:])

@@ -1,6 +1,7 @@
 from contextlib import ExitStack
 
 import concourse.mybir as mybir
+from concourse.masks import make_identity
 
 K, T, S, H, N, U = 1024, 2048, 512, 512, 512, 512
 FLOPS = 2 * K * H * S + 2 * H * N * S
@@ -39,14 +40,16 @@ def tile_picked_anc8_relu_p_kernel(tc, x_words, x_scales, w1, emb, w2, offs, up1
         w2_raw = keep.tile([P, PACK, N], F32, name="w2_raw", tag="w2_raw", align_bytes=64)
         x_word_table = [keep.tile([P, T], I32, name="x_word_table%d" % g, tag="x_word_table%d" % g) for g in range(PASSES)]
 
+        identity = keep.tile([P, P], F32, name="identity")
+        make_identity(nc, identity[:])
         for t in range(2):
             nc.vector.memset(emb_wide[t][:, U : 2 * U], 0.0)
         nc.gpsimd.memset(x_scale_table[:].bitcast(I32), 0)
         for t in range(2, PACK):
             nc.gpsimd.memset(emb_wide[t][:, U : 2 * U], 0.0)
 
-        def load_emb(table, t):
-            nc.sync.dma_start(out=table[:, 0:U], in_=emb_planes[:, t, :])
+        def load_emb(table, t, queue=nc.sync):
+            queue.dma_start(out=table[:, 0:U], in_=emb_planes[:, t, :])
 
         def load_w1(g):
             nc.sync.dma_start(out=w1_raw[g][:], in_=w1[g * 512 : (g + 1) * 512, :].rearrange("(p j) c -> p j c", j=PACK))
@@ -55,7 +58,7 @@ def tile_picked_anc8_relu_p_kernel(tc, x_words, x_scales, w1, emb, w2, offs, up1
             nc.sync.dma_start(out=x_word_table[g][:], in_=x_words[g].rearrange("p n t -> p (n t)").bitcast(I32))
 
         nc.sync.dma_start(ups[0][:], up1)
-        load_emb(emb_wide[0], 0)
+        load_emb(emb_wide[0], 0, nc.scalar)
         load_emb(emb_wide[1], 1)
         nc.sync.dma_start(ups[1][:], up2)
         nc.sync.dma_start(ups[2][:], up3)
@@ -117,24 +120,28 @@ def tile_picked_anc8_relu_p_kernel(tc, x_words, x_scales, w1, emb, w2, offs, up1
             nc.vector.tensor_copy(out=x_cd[g][:], in_=x_word_table[g][:].bitcast(U32).indirect(picks[:]))
         early[1] = early_sum(1, "x_word_table1")
 
-        def first_layer(t):
-            bank = psum.tile([P, S], F32, name="y_bank%d" % t, tag="bank%d" % (t % 2))
+        def first_layer(t, first, count, bank_number):
+            bank = psum.tile([P, count], F32, name="y_bank%d_%d" % (t, first), tag="bank%d" % bank_number)
+            cols = slice(first, first + count)
             for g in range(PASSES):
                 nc.tensor.matmul_mx(
                     out=bank[:],
                     lhsT=w1_codes[g][:, t * P : (t + 1) * P].bitcast(FP8X4),
                     lhsT_scale=w1_scales[g][:, t * P : (t + 1) * P],
-                    rhs=x_cd[g][:].bitcast(FP8X4),
-                    rhs_scale=x_sc[4 * g : P, :],
+                    rhs=x_cd[g][:, cols].bitcast(FP8X4),
+                    rhs_scale=x_sc[4 * g : P, cols],
                     start=(g == 0),
                     stop=(g == PASSES - 1),
                 )
             return bank
 
         y_late = keep.tile([P, 2, S], F32, name="y_late", tag="sums", align_bytes=64)
+        for h in range(2):
+            nc.scalar.copy(out=y_late[:, 0, h * HALF : (h + 1) * HALF], in_=first_layer(2, h * HALF, HALF, h)[:])
+        nc.scalar.copy(out=y_late[:, 1, :], in_=first_layer(3, 0, S, 3)[:])
+        y_early = keep.tile([P, 2, S], F32, name="y_early")
         for e in range(2):
-            nc.scalar.copy(out=y_late[:, e, :], in_=first_layer(2 + e)[:])
-        y_early_bank = [first_layer(e) for e in range(2)]
+            nc.scalar.copy(out=y_early[:, e, :], in_=first_layer(e, 0, S, e)[:])
 
         w2_grouped = keep.tile([P, PACK * N], BF16, name="w2_grouped", align_bytes=64)
         nc.scalar.activation(
@@ -143,12 +150,39 @@ def tile_picked_anc8_relu_p_kernel(tc, x_words, x_scales, w1, emb, w2, offs, up1
             func=COPY,
         )
 
-        late = y_late
-        for l in range(2):
-            before = late
-            late = keep.tile([P, 2, S], F32, name="late_part%d" % l)
+        def late_step(after, before, l, e, first, count):
+            cols = slice(first, first + count)
+            nc.vector.tensor_tensor(out=after[:, e, cols], in0=looked_up(emb_wide[2 + e], l, first, count), in1=before[:, e, cols], op=ADD)
+
+        late_first = keep.tile([P, 2, S], F32, name="late_first")
+        late = keep.tile([P, 2, S], F32, name="late")
+        for e in range(2):
+            late_step(late_first, y_late, 0, e, 0, S)
+        late_step(late, late_first, 1, 0, 0, S)
+        late_step(late, late_first, 1, 1, 0, HALF)
+
+        back = []
+        for h in range(2):
+            sums = psum.tile([P, 2, 2, P], F32, name="sums%d" % h, tag="bank%d" % (4 + h))
+            terms = [(early[e][:], e) for e in range(2)] + [(y_early[:, e, :], e) for e in range(2)]
+            for i, (term, e) in enumerate(terms):
+                for b in range(2):
+                    cols = slice(h * HALF + b * P, h * HALF + (b + 1) * P)
+                    nc.tensor.matmul(
+                        out=sums[:, e, b, :],
+                        lhsT=term[:, cols],
+                        rhs=identity[:],
+                        is_transpose=True,
+                        start=(i == 0 and b == 0),
+                        stop=(i == len(terms) - 1 and b == 1),
+                    )
+            turned = keep.tile([P, 2, 2, P], F32, name="turned%d" % h)
+            nc.scalar.copy(out=turned[:], in_=sums[:])
+            bank = psum.tile([P, 2, 2, P], F32, name="back%d" % h, tag="bank%d" % (3 - h))
             for e in range(2):
-                nc.vector.tensor_tensor(out=late[:, e, :], in0=looked_up(emb_wide[2 + e], l, 0, S), in1=before[:, e, :], op=ADD)
+                for b in range(2):
+                    nc.tensor.transpose(bank[:, e, b, :], turned[:, e, b, :], identity[:])
+            back.append(bank)
 
         out_view = out.rearrange("(t p) s -> p t s", p=P)
         overlap = 2 * QUARTER
@@ -184,20 +218,14 @@ def tile_picked_anc8_relu_p_kernel(tc, x_words, x_scales, w1, emb, w2, offs, up1
             result = keep.tile([P, tiles, count], F32, name="result%d_%d" % (first, t0))
             return acc, result, out_view[:, t0 : t0 + tiles, first : first + count]
 
-        for e in range(2):
-            nc.vector.tensor_tensor(out=half_planes[:, e, :], in0=y_early_bank[e][:, 0:HALF], in1=early[e][:, 0:HALF], op=ADD)
+        nc.scalar.copy(out=half_planes[:, 0:2, :], in_=back[0][:].rearrange("p e b s -> p e (b s)"))
+        nc.scalar.copy(out=quarters[:, :, 0:2, :], in_=back[1][:].rearrange("p e b s -> p b e s"))
         last_step(emb_wide[2:], half_planes, 0, HALF)
         half_grouped = keep.tile([P, PACK * HALF], BF16, name="z_grouped0", tag="w2_raw", align_bytes=64)
         z_out, z_in = views(half_planes, half_grouped[:])
         nc.scalar.activation(out=z_out, in_=z_in, func=RELU)
 
-        for e in range(2):
-            nc.vector.tensor_tensor(
-                out=quarters[:, :, e, :],
-                in0=y_early_bank[e][:, HALF:S].rearrange("p (i s) -> p i s", i=2),
-                in1=early[e][:, HALF:S].rearrange("p (i s) -> p i s", i=2),
-                op=ADD,
-            )
+        late_step(late, late_first, 1, 1, HALF, HALF)
         w2_codes, w2_scales = quantised("w2", w2_grouped[:], N)
         last_step(emb_narrow, quarters[:, 0], HALF, QUARTER)
         z = quantised("z0", half_grouped[:], HALF)

@@ -232,24 +232,25 @@ def tile_picked_anc8_relu_p_kernel(tc, x_words, x_scales, w1, emb, w2, offs, up1
         third_grouped = pre[:, 2 * PACK * HALF - overlap - 2 * QUARTER :].bitcast(BF16)
         z_out, z_in = views(quarters[:, 0], third_grouped)
         nc.scalar.activation(out=z_out, in_=z_in, func=RELU)
-        for t0 in (0, 2):
-            acc, result, target = second_layer(z, 0, HALF, t0, 2, 4 + t0 // 2)
+        for t in range(PACK):
+            acc, result, target = second_layer(z, 0, HALF, t, 1, 4 + t)
             nc.scalar.copy(out=result[:], in_=acc[:])
             nc.sync.dma_start(out=target, in_=result[:])
 
         last_step(emb_narrow, quarters[:, 1], HALF + QUARTER, QUARTER)
         z = quantised("z1", third_grouped, QUARTER)
-        acc, result, target = second_layer(z, HALF, QUARTER, 0, 4, 6)
-        nc.scalar.copy(out=result[:], in_=acc[:])
-        nc.sync.dma_start(out=target, in_=result[:])
+        for t0 in (0, 2):
+            acc, result, target = second_layer(z, HALF, QUARTER, t0, 2, 2 + t0 // 2)
+            nc.scalar.copy(out=result[:], in_=acc[:])
+            nc.sync.dma_start(out=target, in_=result[:])
 
         last_grouped = pre[:, 0 : 2 * QUARTER].bitcast(BF16)
         z_out, z_in = views(quarters[:, 1], last_grouped)
         nc.vector.tensor_scalar_max(z_out, z_in, 0.0)
         z = quantised("z2", last_grouped, QUARTER)
-        acc, result, target = second_layer(z, HALF + QUARTER, QUARTER, 0, 2, 7)
+        acc, result, target = second_layer(z, HALF + QUARTER, QUARTER, 0, 2, 0)
         nc.vector.tensor_copy(out=result[:], in_=acc[:])
         nc.sync.dma_start(out=target, in_=result[:])
-        acc, result, target = second_layer(z, HALF + QUARTER, QUARTER, 2, 2, 2)
+        acc, result, target = second_layer(z, HALF + QUARTER, QUARTER, 2, 2, 1)
         nc.vector.tensor_copy(out=result[:], in_=acc[:])
         nc.sync.dma_start(out=target, in_=result[:])

@@ -36,7 +36,7 @@ def tile_picked_anc8_relu_p_kernel(tc, x_words, x_scales, w1, emb, w2, offs, up1
         picks = keep.tile([P, S // 16], U16, name="picks")
         emb_wide = [keep.tile([P, 2 * U], F32, name="emb_wide%d" % t) for t in range(PACK)]
         emb_narrow = [keep.tile([P, U], F32, name="emb_narrow%d" % e) for e in range(2)]
-        w1_raw = [keep.tile([P, PACK, H], F32, name="w1_raw%d" % g) for g in range(PASSES)]
+        w1_raw = [keep.tile([P, PACK, H], F32, name="w1_raw%d" % g, tag="w1_raw%d" % g) for g in range(PASSES)]
         w2_raw = keep.tile([P, PACK, N], F32, name="w2_raw", tag="w2_raw", align_bytes=64)
         x_word_table = [keep.tile([P, T], I32, name="x_word_table%d" % g, tag="x_word_table%d" % g) for g in range(PASSES)]
 
@@ -139,9 +139,28 @@ def tile_picked_anc8_relu_p_kernel(tc, x_words, x_scales, w1, emb, w2, offs, up1
         for h in range(2):
             nc.scalar.copy(out=y_late[:, 0, h * HALF : (h + 1) * HALF], in_=first_layer(2, h * HALF, HALF, h)[:])
         nc.scalar.copy(out=y_late[:, 1, :], in_=first_layer(3, 0, S, 3)[:])
-        y_early = keep.tile([P, 2, S], F32, name="y_early")
+        early_turned = keep.tile([P, 2, PACK, P], F32, name="early_turned", tag="w1_raw1")
         for e in range(2):
-            nc.scalar.copy(out=y_early[:, e, :], in_=first_layer(e, 0, S, e)[:])
+            bank = psum.tile([P, PACK, P], F32, name="early_bank%d" % e, tag="bank%d" % (4 + e))
+            for b in range(PACK):
+                nc.tensor.transpose(bank[:, b, :], early[e][:, b * P : (b + 1) * P], identity[:])
+            nc.scalar.copy(out=early_turned[:, e], in_=bank[:])
+        y_turned = keep.tile([P, PACK, 2 * P], F32, name="y_turned")
+        for h in range(2):
+            bank = psum.tile([P, 2, 2 * P], F32, name="y_turned_bank%d" % h, tag="bank%d" % h)
+            for b in range(2):
+                cols = slice((2 * h + b) * P, (2 * h + b + 1) * P)
+                for g in range(PASSES):
+                    nc.tensor.matmul_mx(
+                        out=bank[:, b, :],
+                        lhsT=x_cd[g][:, cols].bitcast(FP8X4),
+                        lhsT_scale=x_sc[4 * g : P, cols],
+                        rhs=w1_codes[g][:, 0 : 2 * P].bitcast(FP8X4),
+                        rhs_scale=w1_scales[g][:, 0 : 2 * P],
+                        start=(g == 0),
+                        stop=(g == PASSES - 1),
+                    )
+            nc.scalar.copy(out=y_turned[:, 2 * h : 2 * h + 2, :], in_=bank[:])
 
         w2_grouped = keep.tile([P, PACK * N], BF16, name="w2_grouped", align_bytes=64)
         nc.scalar.activation(
@@ -163,25 +182,19 @@ def tile_picked_anc8_relu_p_kernel(tc, x_words, x_scales, w1, emb, w2, offs, up1
 
         back = []
         for h in range(2):
-            sums = psum.tile([P, 2, 2, P], F32, name="sums%d" % h, tag="bank%d" % (4 + h))
-            terms = [(early[e][:], e) for e in range(2)] + [(y_early[:, e, :], e) for e in range(2)]
-            for i, (term, e) in enumerate(terms):
-                for b in range(2):
-                    cols = slice(h * HALF + b * P, h * HALF + (b + 1) * P)
-                    nc.tensor.matmul(
-                        out=sums[:, e, b, :],
-                        lhsT=term[:, cols],
-                        rhs=identity[:],
-                        is_transpose=True,
-                        start=(i == 0 and b == 0),
-                        stop=(i == len(terms) - 1 and b == 1),
-                    )
-            turned = keep.tile([P, 2, 2, P], F32, name="turned%d" % h)
-            nc.scalar.copy(out=turned[:], in_=sums[:])
             bank = psum.tile([P, 2, 2, P], F32, name="back%d" % h, tag="bank%d" % (3 - h))
-            for e in range(2):
-                for b in range(2):
-                    nc.tensor.transpose(bank[:, e, b, :], turned[:, e, b, :], identity[:])
+            for term in range(2):
+                for e in range(2):
+                    for b in range(2):
+                        block = 2 * h + b
+                        nc.tensor.matmul(
+                            out=bank[:, e, b, :],
+                            lhsT=early_turned[:, e, block, :] if term == 0 else y_turned[:, block, e * P : (e + 1) * P],
+                            rhs=identity[:],
+                            is_transpose=True,
+                            start=(term == 0 and e == 0 and b == 0),
+                            stop=(term == 1 and e == 1 and b == 1),
+                        )
             back.append(bank)
 
         out_view = out.rearrange("(t p) s -> p t s", p=P)
@@ -248,9 +261,18 @@ def tile_picked_anc8_relu_p_kernel(tc, x_words, x_scales, w1, emb, w2, offs, up1
         z_out, z_in = views(quarters[:, 1], last_grouped)
         nc.vector.tensor_scalar_max(z_out, z_in, 0.0)
         z = quantised("z2", last_grouped, QUARTER)
-        acc, result, target = second_layer(z, HALF + QUARTER, QUARTER, 0, 2, 0)
-        nc.vector.tensor_copy(out=result[:], in_=acc[:])
-        nc.sync.dma_start(out=target, in_=result[:])
-        acc, result, target = second_layer(z, HALF + QUARTER, QUARTER, 2, 2, 1)
-        nc.vector.tensor_copy(out=result[:], in_=acc[:])
-        nc.sync.dma_start(out=target, in_=result[:])
+        for t0 in (0, 2):
+            pair = keep.tile([P, 2, QUARTER], F32, name="last_result%d" % t0)
+            for t in (t0, t0 + 1):
+                acc = psum.tile([P, QUARTER], F32, name="last_acc%d" % t, tag="bank%d" % (0, 1, 4, 5)[t])
+                nc.tensor.matmul_mx(
+                    out=acc[:],
+                    lhsT=w2_codes[:, t * P : (t + 1) * P].bitcast(FP8X4),
+                    lhsT_scale=w2_scales[:, t * P : (t + 1) * P],
+                    rhs=z[0][:].bitcast(FP8X4),
+                    rhs_scale=z[1][:],
+                    start=True,
+                    stop=True,
+                )
+                nc.vector.tensor_copy(out=pair[:, t - t0, :], in_=acc[:])
+            nc.sync.dma_start(out=out_view[:, t0 : t0 + 2, HALF + QUARTER : S], in_=pair[:])

@@ -20,8 +20,12 @@ ADD = mybir.AluOpType.add
 P = 128
 PACK = 4
 PASSES = K // (P * PACK)
+LISTS = 3
+GROUP = 16
+QUADRANT = 32
 HALF = S // 2
 QUARTER = S // 4
+RUN = 4
 
 
 def tile_picked_anc8_relu_p_kernel(tc, x_words, x_scales, w1, emb, w2, offs, up1, up2, up3, out):
@@ -32,8 +36,8 @@ def tile_picked_anc8_relu_p_kernel(tc, x_words, x_scales, w1, emb, w2, offs, up1
 
         x_scale_table = keep.tile([P, T], U8, name="x_scale_table", align_bytes=64)
         emb_planes = emb.rearrange("(p t) u -> p t u", t=PACK)
-        ups = [keep.tile([P, S // 16], U16, name="up_list%d" % l) for l in range(3)]
-        picks = keep.tile([P, S // 16], U16, name="picks")
+        ups = [keep.tile([P, S // GROUP], U16, name="up_list%d" % l) for l in range(LISTS)]
+        picks = keep.tile([P, S // GROUP], U16, name="picks")
         emb_wide = [keep.tile([P, 2 * U], F32, name="emb_wide%d" % t) for t in range(PACK)]
         emb_narrow = [keep.tile([P, U], F32, name="emb_narrow%d" % e) for e in range(2)]
         w1_raw = [keep.tile([P, PACK, H], F32, name="w1_raw%d" % g, tag="w1_raw%d" % g) for g in range(PASSES)]
@@ -42,94 +46,91 @@ def tile_picked_anc8_relu_p_kernel(tc, x_words, x_scales, w1, emb, w2, offs, up1
 
         identity = keep.tile([P, P], F32, name="identity")
         make_identity(nc, identity[:])
-        for t in range(2):
-            nc.vector.memset(emb_wide[t][:, U : 2 * U], 0.0)
         nc.gpsimd.memset(x_scale_table[:].bitcast(I32), 0)
-        for t in range(2, PACK):
-            nc.gpsimd.memset(emb_wide[t][:, U : 2 * U], 0.0)
+        for t in range(PACK):
+            nc.vector.memset(emb_wide[t][:, U : 2 * U], 0.0)
 
-        def load_emb(table, t, queue=nc.sync):
+        def load_emb(table, t, queue):
             queue.dma_start(out=table[:, 0:U], in_=emb_planes[:, t, :])
 
         def load_w1(g):
-            nc.sync.dma_start(out=w1_raw[g][:], in_=w1[g * 512 : (g + 1) * 512, :].rearrange("(p j) c -> p j c", j=PACK))
+            rows = w1[g * P * PACK : (g + 1) * P * PACK, :]
+            nc.sync.dma_start(out=w1_raw[g][:], in_=rows.rearrange("(p j) c -> p j c", j=PACK))
 
         def load_x(g):
             nc.sync.dma_start(out=x_word_table[g][:], in_=x_words[g].rearrange("p n t -> p (n t)").bitcast(I32))
 
         nc.sync.dma_start(ups[0][:], up1)
         load_emb(emb_wide[0], 0, nc.scalar)
-        load_emb(emb_wide[1], 1)
+        load_emb(emb_wide[1], 1, nc.sync)
         nc.sync.dma_start(ups[1][:], up2)
         nc.sync.dma_start(ups[2][:], up3)
         load_w1(0)
-        for q in range(4):
+        for q in range(P // QUADRANT):
             nc.sync.dma_start(
-                out=x_scale_table[32 * q : 32 * q + 4 * PASSES, :].bitcast(I32),
+                out=x_scale_table[QUADRANT * q : QUADRANT * q + 4 * PASSES, :].bitcast(I32),
                 in_=x_scales[:, 4 * q : 4 * q + 4, :].bitcast(I32),
             )
         nc.sync.dma_start(picks[:], offs)
         load_w1(1)
         load_x(0)
         load_x(1)
-        load_emb(emb_wide[2], 2)
-        load_emb(emb_wide[3], 3)
+        load_emb(emb_wide[2], 2, nc.sync)
+        load_emb(emb_wide[3], 3, nc.sync)
         nc.sync.dma_start(out=w2_raw[:], in_=w2.rearrange("(p j) c -> p j c", j=PACK))
         for e in range(2):
-            load_emb(emb_narrow[e], 2 + e)
+            load_emb(emb_narrow[e], 2 + e, nc.sync)
 
         def looked_up(table, l, first, count):
-            return table[:].indirect(ups[l][:, first // 16 : (first + count) // 16])
+            return table[:].indirect(ups[l][:, first // GROUP : (first + count) // GROUP])
 
-        part = [None, None]
-        for l in range(2):
-            for e in range(2):
-                dst = keep.tile([P, S], F32, name="early_part%d_%d" % (e, l))
-                if l == 0:
-                    nc.vector.tensor_copy(out=dst[:], in_=looked_up(emb_wide[e], l, 0, S))
-                else:
-                    nc.vector.tensor_tensor(out=dst[:], in0=looked_up(emb_wide[e], l, 0, S), in1=part[e][:], op=ADD)
-                part[e] = dst
+        def quantised(name, grouped, count):
+            codes = keep.tile([P, count], U32, name=name + "_codes", align_bytes=64)
+            scales = keep.tile([P, count], U8, name=name + "_scales", align_bytes=64)
+            nc.vector.quantize_mx(out=codes[:].bitcast(FP8X4), scales=scales[:], in_=grouped)
+            return codes, scales
+
+        part = [keep.tile([P, S], F32, name="early_first%d" % e) for e in range(2)]
+        for e in range(2):
+            nc.vector.tensor_copy(out=part[e][:], in_=looked_up(emb_wide[e], 0, 0, S))
+        pair_sum = [keep.tile([P, S], F32, name="early_second%d" % e) for e in range(2)]
+        for e in range(2):
+            nc.vector.tensor_tensor(out=pair_sum[e][:], in0=looked_up(emb_wide[e], 1, 0, S), in1=part[e][:], op=ADD)
 
         def early_sum(e, tag):
             total = keep.tile([P, S], F32, name="early%d" % e, tag=tag)
-            nc.vector.tensor_tensor(out=total[:], in0=looked_up(emb_wide[e], 2, 0, S), in1=part[e][:], op=ADD)
+            nc.vector.tensor_tensor(out=total[:], in0=looked_up(emb_wide[e], 2, 0, S), in1=pair_sum[e][:], op=ADD)
             return total
 
-        early = [early_sum(0, "early0"), None]
+        early = [early_sum(0, "early0")]
 
-        w1_codes = []
-        w1_scales = []
+        w1_mx = []
         for g in range(PASSES):
-            grouped = keep.tile([P, PACK * H], BF16, name="w1_grouped%d" % g, align_bytes=64)
+            w1_grouped = keep.tile([P, PACK * H], BF16, name="w1_grouped%d" % g, align_bytes=64)
             nc.scalar.activation(
-                out=grouped[:].rearrange("p (t m j) -> p m j t", t=PACK, j=PACK),
+                out=w1_grouped[:].rearrange("p (t m j) -> p m j t", t=PACK, j=PACK),
                 in_=w1_raw[g][:].rearrange("p j (m t) -> p m j t", t=PACK),
                 func=COPY,
             )
-            codes = keep.tile([P, H], U32, name="w1_codes%d" % g, align_bytes=64)
-            scales = keep.tile([P, H], U8, name="w1_scales%d" % g, align_bytes=64)
-            nc.vector.quantize_mx(out=codes[:].bitcast(FP8X4), scales=scales[:], in_=grouped[:])
-            w1_codes.append(codes)
-            w1_scales.append(scales)
+            w1_mx.append(quantised("w1_%d" % g, w1_grouped[:], H))
 
-        x_sc = keep.tile([P, S], U8, name="x_sc", align_bytes=64)
-        nc.vector.tensor_copy(out=x_sc[:], in_=x_scale_table[:].indirect(picks[:]))
-        x_cd = [keep.tile([P, S], U32, name="x_cd%d" % g, align_bytes=64) for g in range(PASSES)]
+        x_scale = keep.tile([P, S], U8, name="x_scale", align_bytes=64)
+        nc.vector.tensor_copy(out=x_scale[:], in_=x_scale_table[:].indirect(picks[:]))
+        x_codes = [keep.tile([P, S], U32, name="x_codes%d" % g, align_bytes=64) for g in range(PASSES)]
         for g in range(PASSES):
-            nc.vector.tensor_copy(out=x_cd[g][:], in_=x_word_table[g][:].bitcast(U32).indirect(picks[:]))
-        early[1] = early_sum(1, "x_word_table1")
+            nc.vector.tensor_copy(out=x_codes[g][:], in_=x_word_table[g][:].bitcast(U32).indirect(picks[:]))
+        early.append(early_sum(1, "x_word_table%d" % (PASSES - 1)))
 
-        def first_layer(t, first, count, bank_number):
+        def late_y(t, first, count, bank_number):
             bank = psum.tile([P, count], F32, name="y_bank%d_%d" % (t, first), tag="bank%d" % bank_number)
             cols = slice(first, first + count)
             for g in range(PASSES):
                 nc.tensor.matmul_mx(
                     out=bank[:],
-                    lhsT=w1_codes[g][:, t * P : (t + 1) * P].bitcast(FP8X4),
-                    lhsT_scale=w1_scales[g][:, t * P : (t + 1) * P],
-                    rhs=x_cd[g][:, cols].bitcast(FP8X4),
-                    rhs_scale=x_sc[4 * g : P, cols],
+                    lhsT=w1_mx[g][0][:, t * P : (t + 1) * P].bitcast(FP8X4),
+                    lhsT_scale=w1_mx[g][1][:, t * P : (t + 1) * P],
+                    rhs=x_codes[g][:, cols].bitcast(FP8X4),
+                    rhs_scale=x_scale[4 * g : P, cols],
                     start=(g == 0),
                     stop=(g == PASSES - 1),
                 )
@@ -137,14 +138,16 @@ def tile_picked_anc8_relu_p_kernel(tc, x_words, x_scales, w1, emb, w2, offs, up1
 
         y_late = keep.tile([P, 2, S], F32, name="y_late", tag="sums", align_bytes=64)
         for h in range(2):
-            nc.scalar.copy(out=y_late[:, 0, h * HALF : (h + 1) * HALF], in_=first_layer(2, h * HALF, HALF, h)[:])
-        nc.scalar.copy(out=y_late[:, 1, :], in_=first_layer(3, 0, S, 3)[:])
-        early_turned = keep.tile([P, 2, PACK, P], F32, name="early_turned", tag="w1_raw1")
+            nc.scalar.copy(out=y_late[:, 0, h * HALF : (h + 1) * HALF], in_=late_y(2, h * HALF, HALF, h)[:])
+        nc.scalar.copy(out=y_late[:, 1, :], in_=late_y(3, 0, S, 3)[:])
+
+        early_turned = keep.tile([P, 2, PACK, P], F32, name="early_turned", tag="w1_raw%d" % (PASSES - 1))
         for e in range(2):
             bank = psum.tile([P, PACK, P], F32, name="early_bank%d" % e, tag="bank%d" % (4 + e))
-            for b in range(PACK):
-                nc.tensor.transpose(bank[:, b, :], early[e][:, b * P : (b + 1) * P], identity[:])
+            for block in range(PACK):
+                nc.tensor.transpose(bank[:, block, :], early[e][:, block * P : (block + 1) * P], identity[:])
             nc.scalar.copy(out=early_turned[:, e], in_=bank[:])
+
         y_turned = keep.tile([P, PACK, 2 * P], F32, name="y_turned")
         for h in range(2):
             bank = psum.tile([P, 2, 2 * P], F32, name="y_turned_bank%d" % h, tag="bank%d" % h)
@@ -153,10 +156,10 @@ def tile_picked_anc8_relu_p_kernel(tc, x_words, x_scales, w1, emb, w2, offs, up1
                 for g in range(PASSES):
                     nc.tensor.matmul_mx(
                         out=bank[:, b, :],
-                        lhsT=x_cd[g][:, cols].bitcast(FP8X4),
-                        lhsT_scale=x_sc[4 * g : P, cols],
-                        rhs=w1_codes[g][:, 0 : 2 * P].bitcast(FP8X4),
-                        rhs_scale=w1_scales[g][:, 0 : 2 * P],
+                        lhsT=x_codes[g][:, cols].bitcast(FP8X4),
+                        lhsT_scale=x_scale[4 * g : P, cols],
+                        rhs=w1_mx[g][0][:, 0 : 2 * P].bitcast(FP8X4),
+                        rhs_scale=w1_mx[g][1][:, 0 : 2 * P],
                         start=(g == 0),
                         stop=(g == PASSES - 1),
                     )
@@ -164,8 +167,8 @@ def tile_picked_anc8_relu_p_kernel(tc, x_words, x_scales, w1, emb, w2, offs, up1
 
         w2_grouped = keep.tile([P, PACK * N], BF16, name="w2_grouped", align_bytes=64)
         nc.scalar.activation(
-            out=w2_grouped[:].rearrange("p (c i j) -> p c j i", i=4, j=PACK),
-            in_=w2_raw[:].rearrange("p j (c i) -> p c j i", i=4),
+            out=w2_grouped[:].rearrange("p (c i j) -> p c j i", i=RUN, j=PACK),
+            in_=w2_raw[:].rearrange("p j (c i) -> p c j i", i=RUN),
             func=COPY,
         )
 
@@ -174,11 +177,11 @@ def tile_picked_anc8_relu_p_kernel(tc, x_words, x_scales, w1, emb, w2, offs, up1
             nc.vector.tensor_tensor(out=after[:, e, cols], in0=looked_up(emb_wide[2 + e], l, first, count), in1=before[:, e, cols], op=ADD)
 
         late_first = keep.tile([P, 2, S], F32, name="late_first")
-        late = keep.tile([P, 2, S], F32, name="late")
+        late_second = keep.tile([P, 2, S], F32, name="late_second")
         for e in range(2):
             late_step(late_first, y_late, 0, e, 0, S)
-        late_step(late, late_first, 1, 0, 0, S)
-        late_step(late, late_first, 1, 1, 0, HALF)
+        late_step(late_second, late_first, 1, 0, 0, S)
+        late_step(late_second, late_first, 1, 1, 0, HALF)
 
         back = []
         for h in range(2):
@@ -197,82 +200,73 @@ def tile_picked_anc8_relu_p_kernel(tc, x_words, x_scales, w1, emb, w2, offs, up1
                         )
             back.append(bank)
 
-        out_view = out.rearrange("(t p) s -> p t s", p=P)
+        out_tiles = out.rearrange("(t p) s -> p t s", p=P)
         overlap = 2 * QUARTER
         pre = keep.tile([P, 2 * PACK * HALF - overlap], F32, name="pre", tag="sums", align_bytes=64)
         half_planes = pre[:, PACK * HALF - overlap :].rearrange("p (t s) -> p t s", t=PACK)
         quarters = pre[:, 0 : PACK * HALF].rearrange("p (i t s) -> p i t s", i=2, t=PACK)
+        quarter_words = PACK * QUARTER // 2
 
         def last_step(tables, planes, first, count):
             for e in range(2):
-                nc.vector.tensor_tensor(out=planes[:, 2 + e, :], in0=looked_up(tables[e], 2, first, count), in1=late[:, e, first : first + count], op=ADD)
+                nc.vector.tensor_tensor(
+                    out=planes[:, 2 + e, :], in0=looked_up(tables[e], 2, first, count), in1=late_second[:, e, first : first + count], op=ADD
+                )
 
-        def views(planes, grouped):
-            return grouped.rearrange("p (c i t) -> p c t i", i=4, t=PACK), planes.rearrange("p t (c i) -> p c t i", i=4)
+        def interleaved(planes, grouped):
+            return grouped.rearrange("p (c i t) -> p c t i", i=RUN, t=PACK), planes.rearrange("p t (c i) -> p c t i", i=RUN)
 
-        def quantised(name, grouped, count):
-            codes = keep.tile([P, count], U32, name=name + "_codes", align_bytes=64)
-            scales = keep.tile([P, count], U8, name=name + "_scales", align_bytes=64)
-            nc.vector.quantize_mx(out=codes[:].bitcast(FP8X4), scales=scales[:], in_=grouped)
-            return codes, scales
+        def second_layer(acc, z, t):
+            nc.tensor.matmul_mx(
+                out=acc,
+                lhsT=w2_codes[:, t * P : (t + 1) * P].bitcast(FP8X4),
+                lhsT_scale=w2_scales[:, t * P : (t + 1) * P],
+                rhs=z[0][:].bitcast(FP8X4),
+                rhs_scale=z[1][:],
+                start=True,
+                stop=True,
+            )
 
-        def second_layer(z, first, count, t0, tiles, bank_number):
+        def leave_by_scalar(z, first, count, t0, tiles, bank_number):
             acc = psum.tile([P, tiles, count], F32, name="acc%d_%d" % (first, t0), tag="bank%d" % bank_number)
             for t in range(t0, t0 + tiles):
-                nc.tensor.matmul_mx(
-                    out=acc[:, t - t0, :],
-                    lhsT=w2_codes[:, t * P : (t + 1) * P].bitcast(FP8X4),
-                    lhsT_scale=w2_scales[:, t * P : (t + 1) * P],
-                    rhs=z[0][:].bitcast(FP8X4),
-                    rhs_scale=z[1][:],
-                    start=True,
-                    stop=True,
-                )
+                second_layer(acc[:, t - t0, :], z, t)
             result = keep.tile([P, tiles, count], F32, name="result%d_%d" % (first, t0))
-            return acc, result, out_view[:, t0 : t0 + tiles, first : first + count]
+            nc.scalar.copy(out=result[:], in_=acc[:])
+            nc.sync.dma_start(out=out_tiles[:, t0 : t0 + tiles, first : first + count], in_=result[:])
 
         nc.scalar.copy(out=half_planes[:, 0:2, :], in_=back[0][:].rearrange("p e b s -> p e (b s)"))
         nc.scalar.copy(out=quarters[:, :, 0:2, :], in_=back[1][:].rearrange("p e b s -> p b e s"))
         last_step(emb_wide[2:], half_planes, 0, HALF)
-        half_grouped = keep.tile([P, PACK * HALF], BF16, name="z_grouped0", tag="w2_raw", align_bytes=64)
-        z_out, z_in = views(half_planes, half_grouped[:])
+        half_grouped = keep.tile([P, PACK * HALF], BF16, name="half_grouped", tag="w2_raw", align_bytes=64)
+        z_out, z_in = interleaved(half_planes, half_grouped[:])
         nc.scalar.activation(out=z_out, in_=z_in, func=RELU)
 
-        late_step(late, late_first, 1, 1, HALF, HALF)
+        late_step(late_second, late_first, 1, 1, HALF, HALF)
         w2_codes, w2_scales = quantised("w2", w2_grouped[:], N)
         last_step(emb_narrow, quarters[:, 0], HALF, QUARTER)
-        z = quantised("z0", half_grouped[:], HALF)
-        third_grouped = pre[:, 2 * PACK * HALF - overlap - 2 * QUARTER :].bitcast(BF16)
-        z_out, z_in = views(quarters[:, 0], third_grouped)
+        z_half = quantised("z_half", half_grouped[:], HALF)
+
+        third_grouped = pre[:, 2 * PACK * HALF - overlap - quarter_words :].bitcast(BF16)
+        z_out, z_in = interleaved(quarters[:, 0], third_grouped)
         nc.scalar.activation(out=z_out, in_=z_in, func=RELU)
         for t in range(PACK):
-            acc, result, target = second_layer(z, 0, HALF, t, 1, 4 + t)
-            nc.scalar.copy(out=result[:], in_=acc[:])
-            nc.sync.dma_start(out=target, in_=result[:])
+            leave_by_scalar(z_half, 0, HALF, t, 1, 4 + t)
 
         last_step(emb_narrow, quarters[:, 1], HALF + QUARTER, QUARTER)
-        z = quantised("z1", third_grouped, QUARTER)
+        z_third = quantised("z_third", third_grouped, QUARTER)
         for t0 in (0, 2):
-            acc, result, target = second_layer(z, HALF, QUARTER, t0, 2, 2 + t0 // 2)
-            nc.scalar.copy(out=result[:], in_=acc[:])
-            nc.sync.dma_start(out=target, in_=result[:])
+            leave_by_scalar(z_third, HALF, QUARTER, t0, 2, 2 + t0 // 2)
 
-        last_grouped = pre[:, 0 : 2 * QUARTER].bitcast(BF16)
-        z_out, z_in = views(quarters[:, 1], last_grouped)
+        last_grouped = pre[:, 0:quarter_words].bitcast(BF16)
+        z_out, z_in = interleaved(quarters[:, 1], last_grouped)
         nc.vector.tensor_scalar_max(z_out, z_in, 0.0)
-        z = quantised("z2", last_grouped, QUARTER)
+        z_last = quantised("z_last", last_grouped, QUARTER)
+        last_banks = (0, 1, 4, 5)
         for t0 in (0, 2):
             pair = keep.tile([P, 2, QUARTER], F32, name="last_result%d" % t0)
             for t in (t0, t0 + 1):
-                acc = psum.tile([P, QUARTER], F32, name="last_acc%d" % t, tag="bank%d" % (0, 1, 4, 5)[t])
-                nc.tensor.matmul_mx(
-                    out=acc[:],
-                    lhsT=w2_codes[:, t * P : (t + 1) * P].bitcast(FP8X4),
-                    lhsT_scale=w2_scales[:, t * P : (t + 1) * P],
-                    rhs=z[0][:].bitcast(FP8X4),
-                    rhs_scale=z[1][:],
-                    start=True,
-                    stop=True,
-                )
+                acc = psum.tile([P, QUARTER], F32, name="last_acc%d" % t, tag="bank%d" % last_banks[t])
+                second_layer(acc[:], z_last, t)
                 nc.vector.tensor_copy(out=pair[:, t - t0, :], in_=acc[:])
-            nc.sync.dma_start(out=out_view[:, t0 : t0 + 2, HALF + QUARTER : S], in_=pair[:])
+            nc.sync.dma_start(out=out_tiles[:, t0 : t0 + 2, HALF + QUARTER : S], in_=pair[:])

@@ -46,7 +46,7 @@ def tile_picked_anc8_relu_p_kernel(tc, x_words, x_scales, w1, emb, w2, offs, up1
 
         identity = keep.tile([P, P], F32, name="identity")
         make_identity(nc, identity[:])
-        nc.gpsimd.memset(x_scale_table[:].bitcast(I32), 0)
+        nc.vector.memset(x_scale_table[:].bitcast(I32), 0)
         for t in range(PACK):
             nc.vector.memset(emb_wide[t][:, U : 2 * U], 0.0)
 
@@ -60,8 +60,8 @@ def tile_picked_anc8_relu_p_kernel(tc, x_words, x_scales, w1, emb, w2, offs, up1
         def load_x(g):
             nc.sync.dma_start(out=x_word_table[g][:], in_=x_words[g].rearrange("p n t -> p (n t)").bitcast(I32))
 
+        load_emb(emb_wide[0], 0, nc.sync)
         nc.sync.dma_start(ups[0][:], up1)
-        load_emb(emb_wide[0], 0, nc.scalar)
         load_emb(emb_wide[1], 1, nc.sync)
         nc.sync.dma_start(ups[1][:], up2)
         nc.sync.dma_start(ups[2][:], up3)

@@ -25,6 +25,7 @@ GROUP = 16
 QUADRANT = 32
 HALF = S // 2
 QUARTER = S // 4
+MAIN = S - QUARTER
 RUN = 4
 
 
@@ -41,14 +42,16 @@ def tile_picked_anc8_relu_p_kernel(tc, x_words, x_scales, w1, emb, w2, offs, up1
         emb_wide = [keep.tile([P, 2 * U], F32, name="emb_wide%d" % t) for t in range(PACK)]
         emb_narrow = [keep.tile([P, U], F32, name="emb_narrow%d" % e) for e in range(2)]
         w1_raw = [keep.tile([P, PACK, H], F32, name="w1_raw%d" % g, tag="w1_raw%d" % g) for g in range(PASSES)]
-        w2_raw = keep.tile([P, PACK, N], F32, name="w2_raw", tag="w2_raw", align_bytes=64)
+        w2_raw = [keep.tile([P, PACK, N // 2], F32, name="w2_raw%d" % h, tag="w2_raw%d" % h, align_bytes=64) for h in range(2)]
         x_word_table = [keep.tile([P, T], I32, name="x_word_table%d" % g, tag="x_word_table%d" % g) for g in range(PASSES)]
 
         identity = keep.tile([P, P], F32, name="identity")
         make_identity(nc, identity[:])
-        nc.vector.memset(x_scale_table[:].bitcast(I32), 0)
+        nc.gpsimd.memset(x_scale_table[:].bitcast(I32), 0)
+        emb_again = keep.tile([P, 2 * U], F32, name="emb_again")
         for t in range(PACK):
             nc.vector.memset(emb_wide[t][:, U : 2 * U], 0.0)
+        nc.vector.memset(emb_again[:, U : 2 * U], 0.0)
 
         def load_emb(table, t, queue):
             queue.dma_start(out=table[:, 0:U], in_=emb_planes[:, t, :])
@@ -75,9 +78,11 @@ def tile_picked_anc8_relu_p_kernel(tc, x_words, x_scales, w1, emb, w2, offs, up1
         load_w1(1)
         load_x(0)
         load_x(1)
+        load_emb(emb_again, 1, nc.sync)
         load_emb(emb_wide[2], 2, nc.sync)
         load_emb(emb_wide[3], 3, nc.sync)
-        nc.sync.dma_start(out=w2_raw[:], in_=w2.rearrange("(p j) c -> p j c", j=PACK))
+        for h in range(2):
+            nc.sync.dma_start(out=w2_raw[h][:], in_=w2.rearrange("(p j) c -> p j c", j=PACK)[:, :, h * N // 2 : (h + 1) * N // 2])
         for e in range(2):
             load_emb(emb_narrow[e], 2 + e, nc.sync)
 
@@ -97,12 +102,12 @@ def tile_picked_anc8_relu_p_kernel(tc, x_words, x_scales, w1, emb, w2, offs, up1
         for e in range(2):
             nc.vector.tensor_tensor(out=pair_sum[e][:], in0=looked_up(emb_wide[e], 1, 0, S), in1=part[e][:], op=ADD)
 
-        def early_sum(e, tag):
-            total = keep.tile([P, S], F32, name="early%d" % e, tag=tag)
-            nc.vector.tensor_tensor(out=total[:], in0=looked_up(emb_wide[e], 2, 0, S), in1=pair_sum[e][:], op=ADD)
+        def early_sum(e, table):
+            total = keep.tile([P, S], F32, name="early%d" % e)
+            nc.vector.tensor_tensor(out=total[:], in0=looked_up(table, 2, 0, S), in1=pair_sum[e][:], op=ADD)
             return total
 
-        early = [early_sum(0, "early0")]
+        early = [early_sum(0, emb_wide[0])]
 
         w1_mx = []
         for g in range(PASSES):
@@ -117,9 +122,11 @@ def tile_picked_anc8_relu_p_kernel(tc, x_words, x_scales, w1, emb, w2, offs, up1
         x_scale = keep.tile([P, S], U8, name="x_scale", align_bytes=64)
         nc.vector.tensor_copy(out=x_scale[:], in_=x_scale_table[:].indirect(picks[:]))
         x_codes = [keep.tile([P, S], U32, name="x_codes%d" % g, align_bytes=64) for g in range(PASSES)]
-        for g in range(PASSES):
-            nc.vector.tensor_copy(out=x_codes[g][:], in_=x_word_table[g][:].bitcast(U32).indirect(picks[:]))
-        early.append(early_sum(1, "x_word_table%d" % (PASSES - 1)))
+        nc.vector.tensor_copy(out=x_codes[0][:], in_=x_word_table[0][:].bitcast(U32).indirect(picks[:]))
+        for first in (0, HALF):
+            entries = picks[:, first // GROUP : (first + HALF) // GROUP]
+            nc.vector.tensor_copy(out=x_codes[1][:, first : first + HALF], in_=x_word_table[1][:].bitcast(U32).indirect(entries))
+        early.append(early_sum(1, emb_again))
 
         def late_y(t, first, count, bank_number):
             bank = psum.tile([P, count], F32, name="y_bank%d_%d" % (t, first), tag="bank%d" % bank_number)
@@ -137,9 +144,8 @@ def tile_picked_anc8_relu_p_kernel(tc, x_words, x_scales, w1, emb, w2, offs, up1
             return bank
 
         y_late = keep.tile([P, 2, S], F32, name="y_late", tag="sums", align_bytes=64)
-        for h in range(2):
-            nc.scalar.copy(out=y_late[:, 0, h * HALF : (h + 1) * HALF], in_=late_y(2, h * HALF, HALF, h)[:])
-        nc.scalar.copy(out=y_late[:, 1, :], in_=late_y(3, 0, S, 3)[:])
+        for e, first, bank_number in ((0, 0, 0), (0, HALF, 1), (1, 0, 3), (1, HALF, 6)):
+            nc.scalar.copy(out=y_late[:, e, first : first + HALF], in_=late_y(2 + e, first, HALF, bank_number)[:])
 
         early_turned = keep.tile([P, 2, PACK, P], F32, name="early_turned", tag="w1_raw%d" % (PASSES - 1))
         for e in range(2):
@@ -166,11 +172,12 @@ def tile_picked_anc8_relu_p_kernel(tc, x_words, x_scales, w1, emb, w2, offs, up1
             nc.scalar.copy(out=y_turned[:, 2 * h : 2 * h + 2, :], in_=bank[:])
 
         w2_grouped = keep.tile([P, PACK * N], BF16, name="w2_grouped", align_bytes=64)
-        nc.scalar.activation(
-            out=w2_grouped[:].rearrange("p (c i j) -> p c j i", i=RUN, j=PACK),
-            in_=w2_raw[:].rearrange("p j (c i) -> p c j i", i=RUN),
-            func=COPY,
-        )
+        for h in range(2):
+            nc.scalar.activation(
+                out=w2_grouped[:, h * PACK * N // 2 : (h + 1) * PACK * N // 2].rearrange("p (c i j) -> p c j i", i=RUN, j=PACK),
+                in_=w2_raw[h][:].rearrange("p j (c i) -> p c j i", i=RUN),
+                func=COPY,
+            )
 
         def late_step(after, before, l, e, first, count):
             cols = slice(first, first + count)
@@ -178,10 +185,11 @@ def tile_picked_anc8_relu_p_kernel(tc, x_words, x_scales, w1, emb, w2, offs, up1
 
         late_first = keep.tile([P, 2, S], F32, name="late_first")
         late_second = keep.tile([P, 2, S], F32, name="late_second")
+        late_step(late_first, y_late, 0, 0, 0, HALF)
+        late_step(late_first, y_late, 0, 0, HALF, HALF)
+        late_step(late_first, y_late, 0, 1, 0, S)
         for e in range(2):
-            late_step(late_first, y_late, 0, e, 0, S)
-        late_step(late_second, late_first, 1, 0, 0, S)
-        late_step(late_second, late_first, 1, 1, 0, HALF)
+            late_step(late_second, late_first, 1, e, 0, MAIN)
 
         back = []
         for h in range(2):
@@ -189,7 +197,7 @@ def tile_picked_anc8_relu_p_kernel(tc, x_words, x_scales, w1, emb, w2, offs, up1
             for term in range(2):
                 for e in range(2):
                     for b in range(2):
-                        block = 2 * h + b
+                        block = (0, 1, 3, 2)[2 * h + b]
                         nc.tensor.matmul(
                             out=bank[:, e, b, :],
                             lhsT=early_turned[:, e, block, :] if term == 0 else y_turned[:, block, e * P : (e + 1) * P],
@@ -201,17 +209,11 @@ def tile_picked_anc8_relu_p_kernel(tc, x_words, x_scales, w1, emb, w2, offs, up1
             back.append(bank)
 
         out_tiles = out.rearrange("(t p) s -> p t s", p=P)
-        overlap = 2 * QUARTER
-        pre = keep.tile([P, 2 * PACK * HALF - overlap], F32, name="pre", tag="sums", align_bytes=64)
-        half_planes = pre[:, PACK * HALF - overlap :].rearrange("p (t s) -> p t s", t=PACK)
-        quarters = pre[:, 0 : PACK * HALF].rearrange("p (i t s) -> p i t s", i=2, t=PACK)
-        quarter_words = PACK * QUARTER // 2
-
-        def last_step(tables, planes, first, count):
-            for e in range(2):
-                nc.vector.tensor_tensor(
-                    out=planes[:, 2 + e, :], in0=looked_up(tables[e], 2, first, count), in1=late_second[:, e, first : first + count], op=ADD
-                )
+        lead = 2 * MAIN - QUARTER
+        pre = keep.tile([P, lead + PACK * MAIN], F32, name="pre", tag="sums", align_bytes=64)
+        main = pre[:, lead:].rearrange("p (t s) -> p t s", t=PACK)
+        last = pre[:, 0 : PACK * MAIN].rearrange("p (t s) -> p t s", t=PACK)[:, :, 0:QUARTER]
+        fourth = slice(MAIN, S)
 
         def interleaved(planes, grouped):
             return grouped.rearrange("p (c i t) -> p c t i", i=RUN, t=PACK), planes.rearrange("p t (c i) -> p c t i", i=RUN)
@@ -235,31 +237,37 @@ def tile_picked_anc8_relu_p_kernel(tc, x_words, x_scales, w1, emb, w2, offs, up1
             nc.scalar.copy(out=result[:], in_=acc[:])
             nc.sync.dma_start(out=out_tiles[:, t0 : t0 + tiles, first : first + count], in_=result[:])
 
-        nc.scalar.copy(out=half_planes[:, 0:2, :], in_=back[0][:].rearrange("p e b s -> p e (b s)"))
-        nc.scalar.copy(out=quarters[:, :, 0:2, :], in_=back[1][:].rearrange("p e b s -> p b e s"))
-        last_step(emb_wide[2:], half_planes, 0, HALF)
-        half_grouped = keep.tile([P, PACK * HALF], BF16, name="half_grouped", tag="w2_raw", align_bytes=64)
-        z_out, z_in = interleaved(half_planes, half_grouped[:])
-        nc.scalar.activation(out=z_out, in_=z_in, func=RELU)
+        nc.scalar.copy(out=main[:, 0:2, 0:HALF], in_=back[0][:].rearrange("p e b s -> p e (b s)"))
+        apart = lead + HALF
+        both = pre[:, 0 : 2 * apart].rearrange("p (b r) -> p b r", b=2)[:, :, 0 : 2 * MAIN]
+        nc.scalar.copy(out=both.rearrange("p b (e s) -> p b e s", e=2)[:, :, :, 0:QUARTER], in_=back[1][:].rearrange("p e b s -> p b e s"))
+        for e in range(2):
+            nc.vector.tensor_tensor(out=main[:, 2 + e, :], in0=looked_up(emb_wide[2 + e], 2, 0, MAIN), in1=late_second[:, e, 0:MAIN], op=ADD)
+        grouped = keep.tile([P, PACK * MAIN], BF16, name="grouped", tag="w2_raw1", align_bytes=64)
+        pieces = [grouped[:, i * PACK * QUARTER : (i + 1) * PACK * QUARTER] for i in range(3)]
+        for i in range(3):
+            z_out, z_in = interleaved(main[:, :, i * QUARTER : (i + 1) * QUARTER], pieces[i])
+            nc.scalar.activation(out=z_out, in_=z_in, func=RELU)
 
-        late_step(late_second, late_first, 1, 1, HALF, HALF)
+        def last_gather(after, before, l, e):
+            nc.vector.tensor_tensor(out=after, in0=looked_up(emb_narrow[e], l, MAIN, QUARTER), in1=before, op=ADD)
+
+        def leave(i, banks):
+            z = quantised("z%d" % i, pieces[i], QUARTER)
+            for t0 in (0, 2):
+                leave_by_scalar(z, i * QUARTER, QUARTER, t0, 2, banks[t0 // 2])
+
+        last_gather(late_second[:, 0, fourth], late_first[:, 0, fourth], 1, 0)
         w2_codes, w2_scales = quantised("w2", w2_grouped[:], N)
-        last_step(emb_narrow, quarters[:, 0], HALF, QUARTER)
-        z_half = quantised("z_half", half_grouped[:], HALF)
+        leave(0, (4, 5))
+        last_gather(main[:, 0, 0:QUARTER], late_first[:, 1, fourth], 1, 1)
+        leave(1, (6, 7))
+        last_gather(last[:, 2, :], late_second[:, 0, fourth], 2, 0)
+        last_gather(last[:, 3, :], main[:, 0, 0:QUARTER], 2, 1)
+        leave(2, (2, 3))
 
-        third_grouped = pre[:, 2 * PACK * HALF - overlap - quarter_words :].bitcast(BF16)
-        z_out, z_in = interleaved(quarters[:, 0], third_grouped)
-        nc.scalar.activation(out=z_out, in_=z_in, func=RELU)
-        for t in range(PACK):
-            leave_by_scalar(z_half, 0, HALF, t, 1, 4 + t)
-
-        last_step(emb_narrow, quarters[:, 1], HALF + QUARTER, QUARTER)
-        z_third = quantised("z_third", third_grouped, QUARTER)
-        for t0 in (0, 2):
-            leave_by_scalar(z_third, HALF, QUARTER, t0, 2, 2 + t0 // 2)
-
-        last_grouped = pre[:, 0:quarter_words].bitcast(BF16)
-        z_out, z_in = interleaved(quarters[:, 1], last_grouped)
+        last_grouped = main[:, 3, QUARTER:MAIN].bitcast(BF16)
+        z_out, z_in = interleaved(last, last_grouped)
         nc.vector.tensor_scalar_max(z_out, z_in, 0.0)
         z_last = quantised("z_last", last_grouped, QUARTER)
         last_banks = (0, 1, 4, 5)
@@ -268,5 +276,8 @@ def tile_picked_anc8_relu_p_kernel(tc, x_words, x_scales, w1, emb, w2, offs, up1
             for t in (t0, t0 + 1):
                 acc = psum.tile([P, QUARTER], F32, name="last_acc%d" % t, tag="bank%d" % last_banks[t])
                 second_layer(acc[:], z_last, t)
-                nc.vector.tensor_copy(out=pair[:, t - t0, :], in_=acc[:])
+                if t == t0:
+                    nc.vector.tensor_copy(out=pair[:, 0, :], in_=acc[:])
+                else:
+                    nc.scalar.copy(out=pair[:, 1, :], in_=acc[:])
             nc.sync.dma_start(out=out_tiles[:, t0 : t0 + 2, HALF + QUARTER : S], in_=pair[:])

@@ -47,11 +47,12 @@ def tile_picked_anc8_relu_p_kernel(tc, x_words, x_scales, w1, emb, w2, offs, up1
 
         identity = keep.tile([P, P], F32, name="identity")
         make_identity(nc, identity[:])
-        nc.gpsimd.memset(x_scale_table[:].bitcast(I32), 0)
+        nc.vector.memset(x_scale_table[:].bitcast(I32), 0)
         emb_again = keep.tile([P, 2 * U], F32, name="emb_again")
-        for t in range(PACK):
+        for t in range(2):
             nc.vector.memset(emb_wide[t][:, U : 2 * U], 0.0)
-        nc.vector.memset(emb_again[:, U : 2 * U], 0.0)
+        for table in (emb_again, emb_wide[2], emb_wide[3]):
+            nc.scalar.copy(out=table[:, U : 2 * U], in_=emb_wide[0][:, U : 2 * U])
 
         def load_emb(table, t, queue):
             queue.dma_start(out=table[:, 0:U], in_=emb_planes[:, t, :])
@@ -69,13 +70,19 @@ def tile_picked_anc8_relu_p_kernel(tc, x_words, x_scales, w1, emb, w2, offs, up1
         nc.sync.dma_start(ups[1][:], up2)
         nc.sync.dma_start(ups[2][:], up3)
         load_w1(0)
-        for q in range(P // QUADRANT):
+        def load_scales(number):
+            g, r = number % PASSES, number // PASSES
             nc.sync.dma_start(
-                out=x_scale_table[QUADRANT * q : QUADRANT * q + 4 * PASSES, :].bitcast(I32),
-                in_=x_scales[:, 4 * q : 4 * q + 4, :].bitcast(I32),
+                out=x_scale_table[4 * g + r : P : QUADRANT, :].bitcast(I32),
+                in_=x_scales[g, r : 16 : 4, :].bitcast(I32),
             )
+
+        for number in range(5):
+            load_scales(number)
         nc.sync.dma_start(picks[:], offs)
         load_w1(1)
+        for number in range(5, 8):
+            load_scales(number)
         load_x(0)
         load_x(1)
         load_emb(emb_again, 1, nc.sync)

@@ -46,7 +46,8 @@ def tile_picked_anc8_relu_p_kernel(tc, x_words, x_scales, w1, emb, w2, offs, up1
         x_word_table = [keep.tile([P, T], I32, name="x_word_table%d" % g, tag="x_word_table%d" % g) for g in range(PASSES)]
 
         identity = keep.tile([P, P], F32, name="identity")
-        make_identity(nc, identity[:])
+        nc.vector.memset(identity[:], 0.0)
+        make_identity(nc, identity[:], nomemset=True)
         nc.vector.memset(x_scale_table[:].bitcast(I32), 0)
         emb_again = keep.tile([P, 2 * U], F32, name="emb_again")
         for t in range(2):
@@ -201,18 +202,18 @@ def tile_picked_anc8_relu_p_kernel(tc, x_words, x_scales, w1, emb, w2, offs, up1
         back = []
         for h in range(2):
             bank = psum.tile([P, 2, 2, P], F32, name="back%d" % h, tag="bank%d" % (3 - h))
-            for term in range(2):
-                for e in range(2):
-                    for b in range(2):
-                        block = (0, 1, 3, 2)[2 * h + b]
-                        nc.tensor.matmul(
-                            out=bank[:, e, b, :],
-                            lhsT=early_turned[:, e, block, :] if term == 0 else y_turned[:, block, e * P : (e + 1) * P],
-                            rhs=identity[:],
-                            is_transpose=True,
-                            start=(term == 0 and e == 0 and b == 0),
-                            stop=(term == 1 and e == 1 and b == 1),
-                        )
+            terms = ((0, True), (0, False), (1, False), (1, True))
+            for n, (e, is_sum) in enumerate(terms):
+                for b in range(2):
+                    block = (0, 1, 3, 2)[2 * h + b]
+                    nc.tensor.matmul(
+                        out=bank[:, e, b, :],
+                        lhsT=early_turned[:, e, block, :] if is_sum else y_turned[:, block, e * P : (e + 1) * P],
+                        rhs=identity[:],
+                        is_transpose=True,
+                        start=(n == 0 and b == 0),
+                        stop=(n == len(terms) - 1 and b == 1),
+                    )
             back.append(bank)
 
         out_tiles = out.rearrange("(t p) s -> p t s", p=P)
@@ -259,32 +260,44 @@ def tile_picked_anc8_relu_p_kernel(tc, x_words, x_scales, w1, emb, w2, offs, up1
         def last_gather(after, before, l, e):
             nc.vector.tensor_tensor(out=after, in0=looked_up(emb_narrow[e], l, MAIN, QUARTER), in1=before, op=ADD)
 
-        def leave(i, banks):
-            z = quantised("z%d" % i, pieces[i], QUARTER)
-            for t0 in (0, 2):
-                leave_by_scalar(z, i * QUARTER, QUARTER, t0, 2, banks[t0 // 2])
-
         last_gather(late_second[:, 0, fourth], late_first[:, 0, fourth], 1, 0)
         w2_codes, w2_scales = quantised("w2", w2_grouped[:], N)
-        leave(0, (4, 5))
+        z_first = quantised("z0", pieces[0], QUARTER)
+        leave_by_scalar(z_first, 0, QUARTER, 0, 2, 4)
+        wide_acc = [psum.tile([P, HALF], F32, name="wide_acc%d" % t, tag="bank%d" % (6 + t)) for t in range(2)]
+        for t in range(2):
+            second_layer(wide_acc[t][:, 0:QUARTER], z_first, 2 + t)
         last_gather(main[:, 0, 0:QUARTER], late_first[:, 1, fourth], 1, 1)
-        leave(1, (6, 7))
+        z_second = quantised("z1", pieces[1], QUARTER)
+        leave_by_scalar(z_second, QUARTER, QUARTER, 0, 2, 5)
+        for t in range(2):
+            second_layer(wide_acc[t][:, QUARTER:HALF], z_second, 2 + t)
+            wide_result = keep.tile([P, HALF], F32, name="wide_result%d" % t)
+            nc.scalar.copy(out=wide_result[:], in_=wide_acc[t][:])
+            nc.sync.dma_start(out=out_tiles[:, 2 + t, 0:HALF], in_=wide_result[:])
         last_gather(last[:, 2, :], late_second[:, 0, fourth], 2, 0)
         last_gather(last[:, 3, :], main[:, 0, 0:QUARTER], 2, 1)
-        leave(2, (2, 3))
+        z_third = quantised("z2", pieces[2], QUARTER)
+        leave_by_scalar(z_third, HALF, QUARTER, 0, 2, 2)
+        late_tiles = pre[:, lead + PACK * MAIN - 2 * HALF :].rearrange("p (t s) -> p t s", t=2)
+        third_acc = psum.tile([P, 2, QUARTER], F32, name="third_acc", tag="bank3")
+        for t in range(2):
+            second_layer(third_acc[:, t, :], z_third, 2 + t)
 
         last_grouped = main[:, 3, QUARTER:MAIN].bitcast(BF16)
         z_out, z_in = interleaved(last, last_grouped)
         nc.vector.tensor_scalar_max(z_out, z_in, 0.0)
         z_last = quantised("z_last", last_grouped, QUARTER)
-        last_banks = (0, 1, 4, 5)
-        for t0 in (0, 2):
-            pair = keep.tile([P, 2, QUARTER], F32, name="last_result%d" % t0)
-            for t in (t0, t0 + 1):
-                acc = psum.tile([P, QUARTER], F32, name="last_acc%d" % t, tag="bank%d" % last_banks[t])
-                second_layer(acc[:], z_last, t)
-                if t == t0:
-                    nc.vector.tensor_copy(out=pair[:, 0, :], in_=acc[:])
-                else:
-                    nc.scalar.copy(out=pair[:, 1, :], in_=acc[:])
-            nc.sync.dma_start(out=out_tiles[:, t0 : t0 + 2, HALF + QUARTER : S], in_=pair[:])
+        nc.vector.tensor_copy(out=late_tiles[:, :, 0:QUARTER], in_=third_acc[:])
+        copies = (nc.scalar.copy, nc.vector.tensor_copy)
+        for t, copy in enumerate(copies):
+            acc = psum.tile([P, QUARTER], F32, name="last_acc%d" % (2 + t), tag="bank%d" % t)
+            second_layer(acc[:], z_last, 2 + t)
+            copy(out=late_tiles[:, t, QUARTER:HALF], in_=acc[:])
+            nc.sync.dma_start(out=out_tiles[:, 2 + t, HALF:S], in_=late_tiles[:, t, :])
+        pair = keep.tile([P, 2, QUARTER], F32, name="last_pair")
+        for t, copy in enumerate(copies):
+            acc = psum.tile([P, QUARTER], F32, name="last_acc%d" % t, tag="bank%d" % (4 + t))
+            second_layer(acc[:], z_last, t)
+            copy(out=pair[:, t, :], in_=acc[:])
+        nc.sync.dma_start(out=out_tiles[:, 0:2, fourth], in_=pair[:])

@@ -89,10 +89,11 @@ def tile_picked_anc8_relu_p_kernel(tc, x_words, x_scales, w1, emb, w2, offs, up1
         load_emb(emb_again, 1, nc.sync)
         load_emb(emb_wide[2], 2, nc.sync)
         load_emb(emb_wide[3], 3, nc.sync)
-        for h in range(2):
-            nc.sync.dma_start(out=w2_raw[h][:], in_=w2.rearrange("(p j) c -> p j c", j=PACK)[:, :, h * N // 2 : (h + 1) * N // 2])
+        w2_rows = w2.rearrange("(p j) c -> p j c", j=PACK)
+        nc.sync.dma_start(out=w2_raw[0][:], in_=w2_rows[:, :, 0 : N // 2])
         for e in range(2):
             load_emb(emb_narrow[e], 2 + e, nc.sync)
+        nc.sync.dma_start(out=w2_raw[1][:], in_=w2_rows[:, :, N // 2 : N])
 
         def looked_up(table, l, first, count):
             return table[:].indirect(ups[l][:, first // GROUP : (first + count) // GROUP])
@@ -155,14 +156,25 @@ def tile_picked_anc8_relu_p_kernel(tc, x_words, x_scales, w1, emb, w2, offs, up1
         for e, first, bank_number in ((0, 0, 0), (0, HALF, 1), (1, 0, 3), (1, HALF, 6)):
             nc.scalar.copy(out=y_late[:, e, first : first + HALF], in_=late_y(2 + e, first, HALF, bank_number)[:])
 
-        early_turned = keep.tile([P, 2, PACK, P], F32, name="early_turned", tag="w1_raw%d" % (PASSES - 1))
-        for e in range(2):
-            bank = psum.tile([P, PACK, P], F32, name="early_bank%d" % e, tag="bank%d" % (4 + e))
-            for block in range(PACK):
-                nc.tensor.transpose(bank[:, block, :], early[e][:, block * P : (block + 1) * P], identity[:])
-            nc.scalar.copy(out=early_turned[:, e], in_=bank[:])
+        w2_grouped = keep.tile([P, PACK * N], BF16, name="w2_grouped", align_bytes=64)
 
-        y_turned = keep.tile([P, PACK, 2 * P], F32, name="y_turned")
+        def cast_w2(h):
+            nc.scalar.activation(
+                out=w2_grouped[:, h * PACK * N // 2 : (h + 1) * PACK * N // 2].rearrange("p (c i j) -> p c j i", i=RUN, j=PACK),
+                in_=w2_raw[h][:].rearrange("p j (c i) -> p c j i", i=RUN),
+                func=COPY,
+            )
+
+        cast_w2(0)
+        turned = keep.tile([P, 3 * S], F32, name="turned", tag="w2_raw0", align_bytes=64)
+        early_turned = [keep.tile([P, S], F32, name="early_turned0", tag="w1_raw%d" % (PASSES - 1))[:], turned[:, 0:S]]
+        for e in range(2):
+            bank = psum.tile([P, S], F32, name="early_bank%d" % e, tag="bank%d" % (4 + e))
+            for block in range(PACK):
+                nc.tensor.transpose(bank[:, block * P : (block + 1) * P], early[e][:, block * P : (block + 1) * P], identity[:])
+            nc.scalar.copy(out=early_turned[e], in_=bank[:])
+
+        y_turned = turned[:, S:].rearrange("p (b c) -> p b c", b=PACK)
         for h in range(2):
             bank = psum.tile([P, 2, 2 * P], F32, name="y_turned_bank%d" % h, tag="bank%d" % h)
             for b in range(2):
@@ -179,13 +191,7 @@ def tile_picked_anc8_relu_p_kernel(tc, x_words, x_scales, w1, emb, w2, offs, up1
                     )
             nc.scalar.copy(out=y_turned[:, 2 * h : 2 * h + 2, :], in_=bank[:])
 
-        w2_grouped = keep.tile([P, PACK * N], BF16, name="w2_grouped", align_bytes=64)
-        for h in range(2):
-            nc.scalar.activation(
-                out=w2_grouped[:, h * PACK * N // 2 : (h + 1) * PACK * N // 2].rearrange("p (c i j) -> p c j i", i=RUN, j=PACK),
-                in_=w2_raw[h][:].rearrange("p j (c i) -> p c j i", i=RUN),
-                func=COPY,
-            )
+        cast_w2(1)
 
         def late_step(after, before, l, e, first, count):
             cols = slice(first, first + count)
@@ -201,14 +207,14 @@ def tile_picked_anc8_relu_p_kernel(tc, x_words, x_scales, w1, emb, w2, offs, up1
 
         back = []
         for h in range(2):
-            bank = psum.tile([P, 2, 2, P], F32, name="back%d" % h, tag="bank%d" % (3 - h))
+            bank = psum.tile([P, 2, 2, P], F32, name="back%d" % h, tag="bank%d" % (4, 2)[h])
             terms = ((0, True), (0, False), (1, False), (1, True))
             for n, (e, is_sum) in enumerate(terms):
                 for b in range(2):
                     block = (0, 1, 3, 2)[2 * h + b]
                     nc.tensor.matmul(
                         out=bank[:, e, b, :],
-                        lhsT=early_turned[:, e, block, :] if is_sum else y_turned[:, block, e * P : (e + 1) * P],
+                        lhsT=early_turned[e][:, block * P : (block + 1) * P] if is_sum else y_turned[:, block, e * P : (e + 1) * P],
                         rhs=identity[:],
                         is_transpose=True,
                         start=(n == 0 and b == 0),

@@ -1,7 +1,6 @@
 from contextlib import ExitStack
 
 import concourse.mybir as mybir
-from concourse.masks import make_identity
 
 K, T, S, H, N, U = 1024, 2048, 512, 512, 512, 512
 FLOPS = 2 * K * H * S + 2 * H * N * S
@@ -24,8 +23,7 @@ LISTS = 3
 GROUP = 16
 QUADRANT = 32
 HALF = S // 2
-QUARTER = S // 4
-MAIN = S - QUARTER
+PIECE = S // 4
 RUN = 4
 
 
@@ -40,23 +38,17 @@ def tile_picked_anc8_relu_p_kernel(tc, x_words, x_scales, w1, emb, w2, offs, up1
         ups = [keep.tile([P, S // GROUP], U16, name="up_list%d" % l) for l in range(LISTS)]
         picks = keep.tile([P, S // GROUP], U16, name="picks")
         emb_wide = [keep.tile([P, 2 * U], F32, name="emb_wide%d" % t) for t in range(PACK)]
-        emb_narrow = [keep.tile([P, U], F32, name="emb_narrow%d" % e) for e in range(2)]
-        w1_raw = [keep.tile([P, PACK, H], F32, name="w1_raw%d" % g, tag="w1_raw%d" % g) for g in range(PASSES)]
+        w1_raw = [keep.tile([P, PACK, H], F32, name="w1_raw%d" % g) for g in range(PASSES)]
         w2_raw = [keep.tile([P, PACK, N // 2], F32, name="w2_raw%d" % h, tag="w2_raw%d" % h, align_bytes=64) for h in range(2)]
-        x_word_table = [keep.tile([P, T], I32, name="x_word_table%d" % g, tag="x_word_table%d" % g) for g in range(PASSES)]
+        x_word_table = [keep.tile([P, T], I32, name="x_word_table%d" % g) for g in range(PASSES)]
 
-        identity = keep.tile([P, P], F32, name="identity")
-        nc.vector.memset(identity[:], 0.0)
-        make_identity(nc, identity[:], nomemset=True)
         nc.vector.memset(x_scale_table[:].bitcast(I32), 0)
-        emb_again = keep.tile([P, 2 * U], F32, name="emb_again")
-        for t in range(2):
+        for t in range(PACK - 1):
             nc.vector.memset(emb_wide[t][:, U : 2 * U], 0.0)
-        for table in (emb_again, emb_wide[2], emb_wide[3]):
-            nc.scalar.copy(out=table[:, U : 2 * U], in_=emb_wide[0][:, U : 2 * U])
+        nc.scalar.activation(out=emb_wide[PACK - 1][:, U : 2 * U], in_=emb_wide[0][:, U : 2 * U], func=COPY)
 
-        def load_emb(table, t, queue):
-            queue.dma_start(out=table[:, 0:U], in_=emb_planes[:, t, :])
+        def load_emb(t):
+            nc.sync.dma_start(out=emb_wide[t][:, 0:U], in_=emb_planes[:, t, :])
 
         def load_w1(g):
             rows = w1[g * P * PACK : (g + 1) * P * PACK, :]
@@ -65,12 +57,6 @@ def tile_picked_anc8_relu_p_kernel(tc, x_words, x_scales, w1, emb, w2, offs, up1
         def load_x(g):
             nc.sync.dma_start(out=x_word_table[g][:], in_=x_words[g].rearrange("p n t -> p (n t)").bitcast(I32))
 
-        load_emb(emb_wide[0], 0, nc.sync)
-        nc.sync.dma_start(ups[0][:], up1)
-        load_emb(emb_wide[1], 1, nc.sync)
-        nc.sync.dma_start(ups[1][:], up2)
-        nc.sync.dma_start(ups[2][:], up3)
-        load_w1(0)
         def load_scales(number):
             g, r = number % PASSES, number // PASSES
             nc.sync.dma_start(
@@ -78,25 +64,28 @@ def tile_picked_anc8_relu_p_kernel(tc, x_words, x_scales, w1, emb, w2, offs, up1
                 in_=x_scales[g, r : 16 : 4, :].bitcast(I32),
             )
 
+        load_emb(0)
+        nc.sync.dma_start(ups[0][:], up1)
+        load_emb(1)
+        nc.sync.dma_start(ups[1][:], up2)
+        nc.sync.dma_start(ups[2][:], up3)
+        load_emb(2)
+        load_x(0)
+        nc.sync.dma_start(picks[:], offs)
         for number in range(5):
             load_scales(number)
-        nc.sync.dma_start(picks[:], offs)
-        load_w1(1)
+        load_w1(0)
         for number in range(5, 8):
             load_scales(number)
-        load_x(0)
+        load_emb(3)
+        load_w1(1)
         load_x(1)
-        load_emb(emb_again, 1, nc.sync)
-        load_emb(emb_wide[2], 2, nc.sync)
-        load_emb(emb_wide[3], 3, nc.sync)
         w2_rows = w2.rearrange("(p j) c -> p j c", j=PACK)
-        nc.sync.dma_start(out=w2_raw[0][:], in_=w2_rows[:, :, 0 : N // 2])
-        for e in range(2):
-            load_emb(emb_narrow[e], 2 + e, nc.sync)
-        nc.sync.dma_start(out=w2_raw[1][:], in_=w2_rows[:, :, N // 2 : N])
+        for h in range(2):
+            nc.sync.dma_start(out=w2_raw[h][:], in_=w2_rows[:, :, h * N // 2 : (h + 1) * N // 2])
 
-        def looked_up(table, l, first, count):
-            return table[:].indirect(ups[l][:, first // GROUP : (first + count) // GROUP])
+        def looked_up(t, l, first, count):
+            return emb_wide[t][:].indirect(ups[l][:, first // GROUP : (first + count) // GROUP])
 
         def quantised(name, grouped, count):
             codes = keep.tile([P, count], U32, name=name + "_codes", align_bytes=64)
@@ -104,206 +93,105 @@ def tile_picked_anc8_relu_p_kernel(tc, x_words, x_scales, w1, emb, w2, offs, up1
             nc.vector.quantize_mx(out=codes[:].bitcast(FP8X4), scales=scales[:], in_=grouped)
             return codes, scales
 
-        part = [keep.tile([P, S], F32, name="early_first%d" % e) for e in range(2)]
-        for e in range(2):
-            nc.vector.tensor_copy(out=part[e][:], in_=looked_up(emb_wide[e], 0, 0, S))
-        pair_sum = [keep.tile([P, S], F32, name="early_second%d" % e) for e in range(2)]
-        for e in range(2):
-            nc.vector.tensor_tensor(out=pair_sum[e][:], in0=looked_up(emb_wide[e], 1, 0, S), in1=part[e][:], op=ADD)
+        def fetch(values, t, l, first, count):
+            nc.scalar.activation(out=values[:, first : first + count], in_=looked_up(t, l, first, count), func=COPY)
 
-        def early_sum(e, table):
-            total = keep.tile([P, S], F32, name="early%d" % e)
-            nc.vector.tensor_tensor(out=total[:], in0=looked_up(table, 2, 0, S), in1=pair_sum[e][:], op=ADD)
-            return total
-
-        early = [early_sum(0, emb_wide[0])]
-
-        w1_mx = []
-        for g in range(PASSES):
-            w1_grouped = keep.tile([P, PACK * H], BF16, name="w1_grouped%d" % g, align_bytes=64)
-            nc.scalar.activation(
-                out=w1_grouped[:].rearrange("p (t m j) -> p m j t", t=PACK, j=PACK),
-                in_=w1_raw[g][:].rearrange("p j (m t) -> p m j t", t=PACK),
-                func=COPY,
-            )
-            w1_mx.append(quantised("w1_%d" % g, w1_grouped[:], H))
+        sums = keep.tile([P, PACK, S], F32, name="sums", align_bytes=64)
+        firsts = [keep.tile([P, S], F32, name="first%d" % t) for t in range(PACK)]
+        pairs = [keep.tile([P, S], F32, name="pair%d" % t) for t in range(PACK)]
+        thirds = [keep.tile([P, S], F32, name="third%d" % t) for t in range(1, PACK)]
+        nc.vector.tensor_copy(out=firsts[0][:, 0:HALF], in_=looked_up(0, 0, 0, HALF))
+        fetch(firsts[0], 0, 0, HALF, HALF)
+        for t in range(1, PACK):
+            fetch(firsts[t], t, 0, 0, S)
+        for t in range(1, PACK):
+            fetch(thirds[t - 1], t, 2, 0, S)
+        for t in range(PACK):
+            nc.vector.tensor_tensor(out=pairs[t][:], in0=looked_up(t, 1, 0, S), in1=firsts[t][:], op=ADD)
+        for t in range(PACK):
+            third = thirds[t - 1][:] if t else looked_up(t, 2, 0, S)
+            nc.vector.tensor_tensor(out=sums[:, t, :], in0=third, in1=pairs[t][:], op=ADD)
 
         x_scale = keep.tile([P, S], U8, name="x_scale", align_bytes=64)
-        nc.vector.tensor_copy(out=x_scale[:], in_=x_scale_table[:].indirect(picks[:]))
         x_codes = [keep.tile([P, S], U32, name="x_codes%d" % g, align_bytes=64) for g in range(PASSES)]
-        nc.vector.tensor_copy(out=x_codes[0][:], in_=x_word_table[0][:].bitcast(U32).indirect(picks[:]))
-        for first in (0, HALF):
-            entries = picks[:, first // GROUP : (first + HALF) // GROUP]
-            nc.vector.tensor_copy(out=x_codes[1][:, first : first + HALF], in_=x_word_table[1][:].bitcast(U32).indirect(entries))
-        early.append(early_sum(1, emb_again))
+        nc.vector.tensor_copy(out=x_scale[:], in_=x_scale_table[:].indirect(picks[:]))
+        for g, first, count in ((0, 0, S), (1, 0, PIECE), (1, PIECE, S - PIECE)):
+            entries = picks[:, first // GROUP : (first + count) // GROUP]
+            nc.vector.tensor_copy(out=x_codes[g][:, first : first + count], in_=x_word_table[g][:].bitcast(U32).indirect(entries))
 
-        def late_y(t, first, count, bank_number):
-            bank = psum.tile([P, count], F32, name="y_bank%d_%d" % (t, first), tag="bank%d" % bank_number)
-            cols = slice(first, first + count)
-            for g in range(PASSES):
-                nc.tensor.matmul_mx(
-                    out=bank[:],
-                    lhsT=w1_mx[g][0][:, t * P : (t + 1) * P].bitcast(FP8X4),
-                    lhsT_scale=w1_mx[g][1][:, t * P : (t + 1) * P],
-                    rhs=x_codes[g][:, cols].bitcast(FP8X4),
-                    rhs_scale=x_scale[4 * g : P, cols],
-                    start=(g == 0),
-                    stop=(g == PASSES - 1),
-                )
-            return bank
-
-        y_late = keep.tile([P, 2, S], F32, name="y_late", tag="sums", align_bytes=64)
-        for e, first, bank_number in ((0, 0, 0), (0, HALF, 1), (1, 0, 3), (1, HALF, 6)):
-            nc.scalar.copy(out=y_late[:, e, first : first + HALF], in_=late_y(2 + e, first, HALF, bank_number)[:])
-
-        w2_grouped = keep.tile([P, PACK * N], BF16, name="w2_grouped", align_bytes=64)
-
-        def cast_w2(h):
+        w1_mx = {}
+        for g, t0, planes in ((0, 0, 4), (1, 0, 2), (1, 2, 2)):
+            w1_grouped = keep.tile([P, planes * H], BF16, name="w1_grouped%d_%d" % (g, t0), align_bytes=64)
             nc.scalar.activation(
-                out=w2_grouped[:, h * PACK * N // 2 : (h + 1) * PACK * N // 2].rearrange("p (c i j) -> p c j i", i=RUN, j=PACK),
+                out=w1_grouped[:].rearrange("p (t m j) -> p m j t", t=planes, j=PACK),
+                in_=w1_raw[g][:].rearrange("p j (m t) -> p m j t", t=PACK)[:, :, :, t0 : t0 + planes],
+                func=COPY,
+            )
+            codes, scales = quantised("w1_%d_%d" % (g, t0), w1_grouped[:], planes * P)
+            for t in range(planes):
+                w1_mx[g, t0 + t] = (codes[:, t * P : (t + 1) * P], scales[:, t * P : (t + 1) * P])
+
+        y_banks = [psum.tile([P, PACK, PIECE], F32, name="y_bank%d" % q, tag="bank%d" % q) for q in range(PACK)]
+        for g in range(PASSES):
+            for q in range(PACK):
+                cols = slice(q * PIECE, (q + 1) * PIECE)
+                for t in range(PACK):
+                    nc.tensor.matmul_mx(
+                        out=y_banks[q][:, t, :],
+                        lhsT=w1_mx[g, t][0].bitcast(FP8X4),
+                        lhsT_scale=w1_mx[g, t][1],
+                        rhs=x_codes[g][:, cols].bitcast(FP8X4),
+                        rhs_scale=x_scale[4 * g : P, cols],
+                        start=(g == 0 and t == 0),
+                        stop=(g == PASSES - 1 and t == PACK - 1),
+                    )
+
+        w2_mx = []
+        for h in range(2):
+            w2_grouped = keep.tile([P, PACK * N // 2], BF16, name="w2_grouped%d" % h, align_bytes=64)
+            nc.scalar.activation(
+                out=w2_grouped[:].rearrange("p (c i j) -> p c j i", i=RUN, j=PACK),
                 in_=w2_raw[h][:].rearrange("p j (c i) -> p c j i", i=RUN),
                 func=COPY,
             )
-
-        cast_w2(0)
-        turned = keep.tile([P, 3 * S], F32, name="turned", tag="w2_raw0", align_bytes=64)
-        early_turned = [keep.tile([P, S], F32, name="early_turned0", tag="w1_raw%d" % (PASSES - 1))[:], turned[:, 0:S]]
-        for e in range(2):
-            bank = psum.tile([P, S], F32, name="early_bank%d" % e, tag="bank%d" % (4 + e))
-            for block in range(PACK):
-                nc.tensor.transpose(bank[:, block * P : (block + 1) * P], early[e][:, block * P : (block + 1) * P], identity[:])
-            nc.scalar.copy(out=early_turned[e], in_=bank[:])
-
-        y_turned = turned[:, S:].rearrange("p (b c) -> p b c", b=PACK)
-        for h in range(2):
-            bank = psum.tile([P, 2, 2 * P], F32, name="y_turned_bank%d" % h, tag="bank%d" % h)
-            for b in range(2):
-                cols = slice((2 * h + b) * P, (2 * h + b + 1) * P)
-                for g in range(PASSES):
-                    nc.tensor.matmul_mx(
-                        out=bank[:, b, :],
-                        lhsT=x_codes[g][:, cols].bitcast(FP8X4),
-                        lhsT_scale=x_scale[4 * g : P, cols],
-                        rhs=w1_mx[g][0][:, 0 : 2 * P].bitcast(FP8X4),
-                        rhs_scale=w1_mx[g][1][:, 0 : 2 * P],
-                        start=(g == 0),
-                        stop=(g == PASSES - 1),
-                    )
-            nc.scalar.copy(out=y_turned[:, 2 * h : 2 * h + 2, :], in_=bank[:])
-
-        cast_w2(1)
-
-        def late_step(after, before, l, e, first, count):
-            cols = slice(first, first + count)
-            nc.vector.tensor_tensor(out=after[:, e, cols], in0=looked_up(emb_wide[2 + e], l, first, count), in1=before[:, e, cols], op=ADD)
-
-        late_first = keep.tile([P, 2, S], F32, name="late_first")
-        late_second = keep.tile([P, 2, S], F32, name="late_second")
-        late_step(late_first, y_late, 0, 0, 0, HALF)
-        late_step(late_first, y_late, 0, 0, HALF, HALF)
-        late_step(late_first, y_late, 0, 1, 0, S)
-        for e in range(2):
-            late_step(late_second, late_first, 1, e, 0, MAIN)
-
-        back = []
-        for h in range(2):
-            bank = psum.tile([P, 2, 2, P], F32, name="back%d" % h, tag="bank%d" % (4, 2)[h])
-            terms = ((0, True), (0, False), (1, False), (1, True))
-            for n, (e, is_sum) in enumerate(terms):
-                for b in range(2):
-                    block = (0, 1, 3, 2)[2 * h + b]
-                    nc.tensor.matmul(
-                        out=bank[:, e, b, :],
-                        lhsT=early_turned[e][:, block * P : (block + 1) * P] if is_sum else y_turned[:, block, e * P : (e + 1) * P],
-                        rhs=identity[:],
-                        is_transpose=True,
-                        start=(n == 0 and b == 0),
-                        stop=(n == len(terms) - 1 and b == 1),
-                    )
-            back.append(bank)
+            w2_mx.append(quantised("w2_%d" % h, w2_grouped[:], N // 2))
 
         out_tiles = out.rearrange("(t p) s -> p t s", p=P)
-        lead = 2 * MAIN - QUARTER
-        pre = keep.tile([P, lead + PACK * MAIN], F32, name="pre", tag="sums", align_bytes=64)
-        main = pre[:, lead:].rearrange("p (t s) -> p t s", t=PACK)
-        last = pre[:, 0 : PACK * MAIN].rearrange("p (t s) -> p t s", t=PACK)[:, :, 0:QUARTER]
-        fourth = slice(MAIN, S)
 
-        def interleaved(planes, grouped):
-            return grouped.rearrange("p (c i t) -> p c t i", i=RUN, t=PACK), planes.rearrange("p t (c i) -> p c t i", i=RUN)
+        def interleaved(grouped):
+            return grouped.rearrange("p (c i t) -> p c t i", i=RUN, t=PACK)
 
-        def second_layer(acc, z, t):
-            nc.tensor.matmul_mx(
-                out=acc,
-                lhsT=w2_codes[:, t * P : (t + 1) * P].bitcast(FP8X4),
-                lhsT_scale=w2_scales[:, t * P : (t + 1) * P],
-                rhs=z[0][:].bitcast(FP8X4),
-                rhs_scale=z[1][:],
-                start=True,
-                stop=True,
-            )
+        def by_runs(planes):
+            return planes.rearrange("p t (c i) -> p c t i", i=RUN)
 
-        def leave_by_scalar(z, first, count, t0, tiles, bank_number):
-            acc = psum.tile([P, tiles, count], F32, name="acc%d_%d" % (first, t0), tag="bank%d" % bank_number)
-            for t in range(t0, t0 + tiles):
-                second_layer(acc[:, t - t0, :], z, t)
-            result = keep.tile([P, tiles, count], F32, name="result%d_%d" % (first, t0))
-            nc.scalar.copy(out=result[:], in_=acc[:])
-            nc.sync.dma_start(out=out_tiles[:, t0 : t0 + tiles, first : first + count], in_=result[:])
-
-        nc.scalar.copy(out=main[:, 0:2, 0:HALF], in_=back[0][:].rearrange("p e b s -> p e (b s)"))
-        apart = lead + HALF
-        both = pre[:, 0 : 2 * apart].rearrange("p (b r) -> p b r", b=2)[:, :, 0 : 2 * MAIN]
-        nc.scalar.copy(out=both.rearrange("p b (e s) -> p b e s", e=2)[:, :, :, 0:QUARTER], in_=back[1][:].rearrange("p e b s -> p b e s"))
-        for e in range(2):
-            nc.vector.tensor_tensor(out=main[:, 2 + e, :], in0=looked_up(emb_wide[2 + e], 2, 0, MAIN), in1=late_second[:, e, 0:MAIN], op=ADD)
-        grouped = keep.tile([P, PACK * MAIN], BF16, name="grouped", tag="w2_raw1", align_bytes=64)
-        pieces = [grouped[:, i * PACK * QUARTER : (i + 1) * PACK * QUARTER] for i in range(3)]
-        for i in range(3):
-            z_out, z_in = interleaved(main[:, :, i * QUARTER : (i + 1) * QUARTER], pieces[i])
-            nc.scalar.activation(out=z_out, in_=z_in, func=RELU)
-
-        def last_gather(after, before, l, e):
-            nc.vector.tensor_tensor(out=after, in0=looked_up(emb_narrow[e], l, MAIN, QUARTER), in1=before, op=ADD)
-
-        last_gather(late_second[:, 0, fourth], late_first[:, 0, fourth], 1, 0)
-        w2_codes, w2_scales = quantised("w2", w2_grouped[:], N)
-        z_first = quantised("z0", pieces[0], QUARTER)
-        leave_by_scalar(z_first, 0, QUARTER, 0, 2, 4)
-        wide_acc = [psum.tile([P, HALF], F32, name="wide_acc%d" % t, tag="bank%d" % (6 + t)) for t in range(2)]
-        for t in range(2):
-            second_layer(wide_acc[t][:, 0:QUARTER], z_first, 2 + t)
-        last_gather(main[:, 0, 0:QUARTER], late_first[:, 1, fourth], 1, 1)
-        z_second = quantised("z1", pieces[1], QUARTER)
-        leave_by_scalar(z_second, QUARTER, QUARTER, 0, 2, 5)
-        for t in range(2):
-            second_layer(wide_acc[t][:, QUARTER:HALF], z_second, 2 + t)
-            wide_result = keep.tile([P, HALF], F32, name="wide_result%d" % t)
-            nc.scalar.copy(out=wide_result[:], in_=wide_acc[t][:])
-            nc.sync.dma_start(out=out_tiles[:, 2 + t, 0:HALF], in_=wide_result[:])
-        last_gather(last[:, 2, :], late_second[:, 0, fourth], 2, 0)
-        last_gather(last[:, 3, :], main[:, 0, 0:QUARTER], 2, 1)
-        z_third = quantised("z2", pieces[2], QUARTER)
-        leave_by_scalar(z_third, HALF, QUARTER, 0, 2, 2)
-        late_tiles = pre[:, lead + PACK * MAIN - 2 * HALF :].rearrange("p (t s) -> p t s", t=2)
-        third_acc = psum.tile([P, 2, QUARTER], F32, name="third_acc", tag="bank3")
-        for t in range(2):
-            second_layer(third_acc[:, t, :], z_third, 2 + t)
-
-        last_grouped = main[:, 3, QUARTER:MAIN].bitcast(BF16)
-        z_out, z_in = interleaved(last, last_grouped)
-        nc.vector.tensor_scalar_max(z_out, z_in, 0.0)
-        z_last = quantised("z_last", last_grouped, QUARTER)
-        nc.vector.tensor_copy(out=late_tiles[:, :, 0:QUARTER], in_=third_acc[:])
-        copies = (nc.scalar.copy, nc.vector.tensor_copy)
-        for t, copy in enumerate(copies):
-            acc = psum.tile([P, QUARTER], F32, name="last_acc%d" % (2 + t), tag="bank%d" % t)
-            second_layer(acc[:], z_last, 2 + t)
-            copy(out=late_tiles[:, t, QUARTER:HALF], in_=acc[:])
-            nc.sync.dma_start(out=out_tiles[:, 2 + t, HALF:S], in_=late_tiles[:, t, :])
-        pair = keep.tile([P, 2, QUARTER], F32, name="last_pair")
-        for t, copy in enumerate(copies):
-            acc = psum.tile([P, QUARTER], F32, name="last_acc%d" % t, tag="bank%d" % (4 + t))
-            second_layer(acc[:], z_last, t)
-            copy(out=pair[:, t, :], in_=acc[:])
-        nc.sync.dma_start(out=out_tiles[:, 0:2, fourth], in_=pair[:])
+        for q in range(PACK):
+            cols = slice(q * PIECE, (q + 1) * PIECE)
+            last = q == PACK - 1
+            z = keep.tile([P, PACK * PIECE], BF16, name="z%d" % q, align_bytes=64)
+            if last:
+                pre = keep.tile([P, PACK * PIECE], BF16, name="pre%d" % q, tag="w2_raw%d" % (q % 2), align_bytes=64)
+                nc.vector.tensor_tensor(out=interleaved(pre[:]), in0=by_runs(y_banks[q][:]), in1=by_runs(sums[:, :, cols]), op=ADD)
+                nc.vector.tensor_scalar_max(z[:], pre[:], 0.0)
+            else:
+                pre = keep.tile([P, PACK, PIECE], F32, name="pre%d" % q, tag="w2_raw%d" % (q % 2), align_bytes=64)
+                nc.vector.tensor_tensor(out=pre[:], in0=y_banks[q][:], in1=sums[:, :, cols], op=ADD)
+                nc.scalar.activation(out=interleaved(z[:]), in_=by_runs(pre[:]), func=RELU)
+            z_codes, z_scales = quantised("z%d" % q, z[:], PIECE)
+            parts = ((0, 2, PACK + q, nc.scalar.copy), (2, 2, 0, nc.vector.tensor_copy)) if last else ((0, PACK, PACK + q, nc.scalar.copy),)
+            for t0, tiles, bank, copy in parts:
+                acc = psum.tile([P, tiles, PIECE], F32, name="acc%d_%d" % (q, t0), tag="bank%d" % bank)
+                for t in range(t0, t0 + tiles):
+                    codes, scales = w2_mx[t // 2]
+                    m = slice(t % 2 * P, (t % 2 + 1) * P)
+                    nc.tensor.matmul_mx(
+                        out=acc[:, t - t0, :],
+                        lhsT=codes[:, m].bitcast(FP8X4),
+                        lhsT_scale=scales[:, m],
+                        rhs=z_codes[:].bitcast(FP8X4),
+                        rhs_scale=z_scales[:],
+                        start=True,
+                        stop=True,
+                    )
+                result = keep.tile([P, tiles, PIECE], F32, name="result%d_%d" % (q, t0))
+                copy(out=result[:], in_=acc[:])
+                nc.sync.dma_start(out=out_tiles[:, t0 : t0 + tiles, cols], in_=result[:])

@@ -38,7 +38,9 @@ def tile_picked_anc8_relu_p_kernel(tc, x_words, x_scales, w1, emb, w2, offs, up1
         ups = [keep.tile([P, S // GROUP], U16, name="up_list%d" % l) for l in range(LISTS)]
         picks = keep.tile([P, S // GROUP], U16, name="picks")
         emb_wide = [keep.tile([P, 2 * U], F32, name="emb_wide%d" % t) for t in range(PACK)]
-        w1_raw = [keep.tile([P, PACK, H], F32, name="w1_raw%d" % g) for g in range(PASSES)]
+        stage = keep.tile([P, PACK * H + (PACK - 1) * S], F32, name="stage", align_bytes=64)
+        w1_raw = [stage[:, 0 : PACK * H].rearrange("p (j c) -> p j c", j=PACK), keep.tile([P, PACK, H], F32, name="w1_raw1")[:]]
+        sums = stage[:, PACK * H - S :].rearrange("p (t s) -> p t s", t=PACK)
         w2_raw = [keep.tile([P, PACK, N // 2], F32, name="w2_raw%d" % h, tag="w2_raw%d" % h, align_bytes=64) for h in range(2)]
         x_word_table = [keep.tile([P, T], I32, name="x_word_table%d" % g) for g in range(PASSES)]
 
@@ -52,7 +54,7 @@ def tile_picked_anc8_relu_p_kernel(tc, x_words, x_scales, w1, emb, w2, offs, up1
 
         def load_w1(g):
             rows = w1[g * P * PACK : (g + 1) * P * PACK, :]
-            nc.sync.dma_start(out=w1_raw[g][:], in_=rows.rearrange("(p j) c -> p j c", j=PACK))
+            nc.sync.dma_start(out=w1_raw[g], in_=rows.rearrange("(p j) c -> p j c", j=PACK))
 
         def load_x(g):
             nc.sync.dma_start(out=x_word_table[g][:], in_=x_words[g].rearrange("p n t -> p (n t)").bitcast(I32))
@@ -68,8 +70,9 @@ def tile_picked_anc8_relu_p_kernel(tc, x_words, x_scales, w1, emb, w2, offs, up1
         nc.sync.dma_start(ups[0][:], up1)
         load_emb(1)
         nc.sync.dma_start(ups[1][:], up2)
-        nc.sync.dma_start(ups[2][:], up3)
         load_emb(2)
+        load_emb(3)
+        nc.sync.dma_start(ups[2][:], up3)
         load_x(0)
         nc.sync.dma_start(picks[:], offs)
         for number in range(5):
@@ -77,7 +80,6 @@ def tile_picked_anc8_relu_p_kernel(tc, x_words, x_scales, w1, emb, w2, offs, up1
         load_w1(0)
         for number in range(5, 8):
             load_scales(number)
-        load_emb(3)
         load_w1(1)
         load_x(1)
         w2_rows = w2.rearrange("(p j) c -> p j c", j=PACK)
@@ -96,21 +98,25 @@ def tile_picked_anc8_relu_p_kernel(tc, x_words, x_scales, w1, emb, w2, offs, up1
         def fetch(values, t, l, first, count):
             nc.scalar.activation(out=values[:, first : first + count], in_=looked_up(t, l, first, count), func=COPY)
 
-        sums = keep.tile([P, PACK, S], F32, name="sums", align_bytes=64)
-        firsts = [keep.tile([P, S], F32, name="first%d" % t) for t in range(PACK)]
+        firsts = [keep.tile([P, S], F32, name="first%d" % t)[:] for t in range(PACK - 1)] + [sums[:, 2, :]]
         pairs = [keep.tile([P, S], F32, name="pair%d" % t) for t in range(PACK)]
-        thirds = [keep.tile([P, S], F32, name="third%d" % t) for t in range(1, PACK)]
+        thirds = {t: keep.tile([P, S], F32, name="third%d" % t) for t in (2, 3)}
         nc.vector.tensor_copy(out=firsts[0][:, 0:HALF], in_=looked_up(0, 0, 0, HALF))
         fetch(firsts[0], 0, 0, HALF, HALF)
         for t in range(1, PACK):
             fetch(firsts[t], t, 0, 0, S)
-        for t in range(1, PACK):
-            fetch(thirds[t - 1], t, 2, 0, S)
-        for t in range(PACK):
-            nc.vector.tensor_tensor(out=pairs[t][:], in0=looked_up(t, 1, 0, S), in1=firsts[t][:], op=ADD)
-        for t in range(PACK):
-            third = thirds[t - 1][:] if t else looked_up(t, 2, 0, S)
-            nc.vector.tensor_tensor(out=sums[:, t, :], in0=third, in1=pairs[t][:], op=ADD)
+        for t in thirds:
+            fetch(thirds[t], t, 2, 0, S)
+
+        def chain(total, t, l, before):
+            nc.vector.tensor_tensor(out=total, in0=looked_up(t, l, 0, S), in1=before, op=ADD)
+
+        for t in range(PACK - 1):
+            chain(pairs[t][:], t, 1, firsts[t])
+        chain(sums[:, 1, :], 1, 2, pairs[1][:])
+        chain(pairs[3][:], 3, 1, firsts[3])
+        for t in thirds:
+            nc.gpsimd.tensor_tensor(out=sums[:, t, :], in0=thirds[t][:], in1=pairs[t][:], op=ADD)
 
         x_scale = keep.tile([P, S], U8, name="x_scale", align_bytes=64)
         x_codes = [keep.tile([P, S], U32, name="x_codes%d" % g, align_bytes=64) for g in range(PASSES)]
@@ -124,12 +130,14 @@ def tile_picked_anc8_relu_p_kernel(tc, x_words, x_scales, w1, emb, w2, offs, up1
             w1_grouped = keep.tile([P, planes * H], BF16, name="w1_grouped%d_%d" % (g, t0), align_bytes=64)
             nc.scalar.activation(
                 out=w1_grouped[:].rearrange("p (t m j) -> p m j t", t=planes, j=PACK),
-                in_=w1_raw[g][:].rearrange("p j (m t) -> p m j t", t=PACK)[:, :, :, t0 : t0 + planes],
+                in_=w1_raw[g].rearrange("p j (m t) -> p m j t", t=PACK)[:, :, :, t0 : t0 + planes],
                 func=COPY,
             )
             codes, scales = quantised("w1_%d_%d" % (g, t0), w1_grouped[:], planes * P)
             for t in range(planes):
                 w1_mx[g, t0 + t] = (codes[:, t * P : (t + 1) * P], scales[:, t * P : (t + 1) * P])
+            if g == 0:
+                chain(sums[:, 0, :], 0, 2, pairs[0][:])
 
         y_banks = [psum.tile([P, PACK, PIECE], F32, name="y_bank%d" % q, tag="bank%d" % q) for q in range(PACK)]
         for g in range(PASSES):

@@ -98,9 +98,11 @@ def tile_picked_anc8_relu_p_kernel(tc, x_words, x_scales, w1, emb, w2, offs, up1
         def fetch(values, t, l, first, count):
             nc.scalar.activation(out=values[:, first : first + count], in_=looked_up(t, l, first, count), func=COPY)
 
-        firsts = [keep.tile([P, S], F32, name="first%d" % t)[:] for t in range(PACK - 1)] + [sums[:, 2, :]]
-        pairs = [keep.tile([P, S], F32, name="pair%d" % t) for t in range(PACK)]
-        thirds = {t: keep.tile([P, S], F32, name="third%d" % t) for t in (2, 3)}
+        firsts = [keep.tile([P, S], F32, name="first%d" % t)[:] for t in range(PACK)]
+        late_pairs = keep.tile([P, 2 * S], F32, name="late_pairs")
+        late_thirds = keep.tile([P, 2 * S], F32, name="late_thirds")
+        pairs = [keep.tile([P, S], F32, name="pair%d" % t)[:] for t in range(2)] + [late_pairs[:, 0:S], late_pairs[:, S:]]
+        thirds = {2: late_thirds[:, 0:S], 3: late_thirds[:, S:]}
         nc.vector.tensor_copy(out=firsts[0][:, 0:HALF], in_=looked_up(0, 0, 0, HALF))
         fetch(firsts[0], 0, 0, HALF, HALF)
         for t in range(1, PACK):
@@ -112,16 +114,15 @@ def tile_picked_anc8_relu_p_kernel(tc, x_words, x_scales, w1, emb, w2, offs, up1
             nc.vector.tensor_tensor(out=total, in0=looked_up(t, l, 0, S), in1=before, op=ADD)
 
         for t in range(PACK - 1):
-            chain(pairs[t][:], t, 1, firsts[t])
-        chain(sums[:, 1, :], 1, 2, pairs[1][:])
-        chain(pairs[3][:], 3, 1, firsts[3])
-        for t in thirds:
-            nc.gpsimd.tensor_tensor(out=sums[:, t, :], in0=thirds[t][:], in1=pairs[t][:], op=ADD)
+            chain(pairs[t], t, 1, firsts[t])
+        chain(sums[:, 1, :], 1, 2, pairs[1])
+        chain(pairs[3], 3, 1, firsts[3])
+        nc.gpsimd.tensor_tensor(out=sums[:, 2:4, :].rearrange("p t s -> p (t s)"), in0=late_thirds[:], in1=late_pairs[:], op=ADD)
 
         x_scale = keep.tile([P, S], U8, name="x_scale", align_bytes=64)
         x_codes = [keep.tile([P, S], U32, name="x_codes%d" % g, align_bytes=64) for g in range(PASSES)]
         nc.vector.tensor_copy(out=x_scale[:], in_=x_scale_table[:].indirect(picks[:]))
-        for g, first, count in ((0, 0, S), (1, 0, PIECE), (1, PIECE, S - PIECE)):
+        for g, first, count in ((0, 0, S), (1, 0, PIECE), (1, PIECE, PIECE), (1, HALF, HALF)):
             entries = picks[:, first // GROUP : (first + count) // GROUP]
             nc.vector.tensor_copy(out=x_codes[g][:, first : first + count], in_=x_word_table[g][:].bitcast(U32).indirect(entries))
 
@@ -137,7 +138,7 @@ def tile_picked_anc8_relu_p_kernel(tc, x_words, x_scales, w1, emb, w2, offs, up1
             for t in range(planes):
                 w1_mx[g, t0 + t] = (codes[:, t * P : (t + 1) * P], scales[:, t * P : (t + 1) * P])
             if g == 0:
-                chain(sums[:, 0, :], 0, 2, pairs[0][:])
+                chain(sums[:, 0, :], 0, 2, pairs[0])
 
         y_banks = [psum.tile([P, PACK, PIECE], F32, name="y_bank%d" % q, tag="bank%d" % q) for q in range(PACK)]
         for g in range(PASSES):
@@ -154,15 +155,13 @@ def tile_picked_anc8_relu_p_kernel(tc, x_words, x_scales, w1, emb, w2, offs, up1
                         stop=(g == PASSES - 1 and t == PACK - 1),
                     )
 
-        w2_mx = []
+        w2_grouped = [keep.tile([P, PACK * N // 2], BF16, name="w2_grouped%d" % h, align_bytes=64) for h in range(2)]
         for h in range(2):
-            w2_grouped = keep.tile([P, PACK * N // 2], BF16, name="w2_grouped%d" % h, align_bytes=64)
             nc.scalar.activation(
-                out=w2_grouped[:].rearrange("p (c i j) -> p c j i", i=RUN, j=PACK),
+                out=w2_grouped[h][:].rearrange("p (c i j) -> p c j i", i=RUN, j=PACK),
                 in_=w2_raw[h][:].rearrange("p j (c i) -> p c j i", i=RUN),
                 func=COPY,
             )
-            w2_mx.append(quantised("w2_%d" % h, w2_grouped[:], N // 2))
 
         out_tiles = out.rearrange("(t p) s -> p t s", p=P)
 
@@ -172,34 +171,45 @@ def tile_picked_anc8_relu_p_kernel(tc, x_words, x_scales, w1, emb, w2, offs, up1
         def by_runs(planes):
             return planes.rearrange("p t (c i) -> p c t i", i=RUN)
 
+        z_mx = []
+
+        def leave(q, t0, tiles, bank, copy, result):
+            acc = psum.tile([P, tiles, PIECE], F32, name="acc%d_%d" % (q, t0), tag="bank%d" % bank)
+            for t in range(t0, t0 + tiles):
+                codes, scales = w2_mx[t // 2]
+                m = slice(t % 2 * P, (t % 2 + 1) * P)
+                nc.tensor.matmul_mx(
+                    out=acc[:, t - t0, :],
+                    lhsT=codes[:, m].bitcast(FP8X4),
+                    lhsT_scale=scales[:, m],
+                    rhs=z_mx[q][0][:].bitcast(FP8X4),
+                    rhs_scale=z_mx[q][1][:],
+                    start=True,
+                    stop=True,
+                )
+            rows = result.rearrange("p (t s) -> p t s", t=tiles)
+            copy(out=rows, in_=acc[:])
+            nc.sync.dma_start(out=out_tiles[:, t0 : t0 + tiles, q * PIECE : (q + 1) * PIECE], in_=rows)
+
+        width = PACK * PIECE
         for q in range(PACK):
             cols = slice(q * PIECE, (q + 1) * PIECE)
-            last = q == PACK - 1
-            z = keep.tile([P, PACK * PIECE], BF16, name="z%d" % q, align_bytes=64)
-            if last:
-                pre = keep.tile([P, PACK * PIECE], BF16, name="pre%d" % q, tag="w2_raw%d" % (q % 2), align_bytes=64)
-                nc.vector.tensor_tensor(out=interleaved(pre[:]), in0=by_runs(y_banks[q][:]), in1=by_runs(sums[:, :, cols]), op=ADD)
-                nc.vector.tensor_scalar_max(z[:], pre[:], 0.0)
+            z = keep.tile([P, width], BF16, name="z%d" % q, tag="w2_raw%d" % q if q < 2 else "z%d" % q, align_bytes=64)
+            if q in (0, PACK - 1):
+                pre = keep.tile([P, width], BF16, name="pre%d" % q, tag="pre%d" % (q % 2), align_bytes=64)[:]
+                nc.vector.tensor_tensor(out=interleaved(pre), in0=by_runs(y_banks[q][:]), in1=by_runs(sums[:, :, cols]), op=ADD)
+                nc.vector.tensor_scalar_max(z[:], pre, 0.0)
             else:
-                pre = keep.tile([P, PACK, PIECE], F32, name="pre%d" % q, tag="w2_raw%d" % (q % 2), align_bytes=64)
-                nc.vector.tensor_tensor(out=pre[:], in0=y_banks[q][:], in1=sums[:, :, cols], op=ADD)
-                nc.scalar.activation(out=interleaved(z[:]), in_=by_runs(pre[:]), func=RELU)
+                pre = keep.tile([P, PACK, PIECE], F32, name="pre%d" % q, tag="pre%d" % (q % 2), align_bytes=64)[:]
+                nc.vector.tensor_tensor(out=pre, in0=y_banks[q][:], in1=sums[:, :, cols], op=ADD)
+                nc.scalar.activation(out=interleaved(z[:]), in_=by_runs(pre), func=RELU)
+            if q == 0:
+                w2_mx = [quantised("w2_%d" % h, w2_grouped[h][:], N // 2) for h in range(2)]
             z_codes, z_scales = quantised("z%d" % q, z[:], PIECE)
-            parts = ((0, 2, PACK + q, nc.scalar.copy), (2, 2, 0, nc.vector.tensor_copy)) if last else ((0, PACK, PACK + q, nc.scalar.copy),)
-            for t0, tiles, bank, copy in parts:
-                acc = psum.tile([P, tiles, PIECE], F32, name="acc%d_%d" % (q, t0), tag="bank%d" % bank)
-                for t in range(t0, t0 + tiles):
-                    codes, scales = w2_mx[t // 2]
-                    m = slice(t % 2 * P, (t % 2 + 1) * P)
-                    nc.tensor.matmul_mx(
-                        out=acc[:, t - t0, :],
-                        lhsT=codes[:, m].bitcast(FP8X4),
-                        lhsT_scale=scales[:, m],
-                        rhs=z_codes[:].bitcast(FP8X4),
-                        rhs_scale=z_scales[:],
-                        start=True,
-                        stop=True,
-                    )
-                result = keep.tile([P, tiles, PIECE], F32, name="result%d_%d" % (q, t0))
-                copy(out=result[:], in_=acc[:])
-                nc.sync.dma_start(out=out_tiles[:, t0 : t0 + tiles, cols], in_=result[:])
+            z_mx.append((z_codes, z_scales))
+            if q < 2:
+                leave(q, 0, PACK, PACK + q, nc.scalar.copy, keep.tile([P, width], F32, name="result%d" % q)[:])
+            else:
+                leave(q, 0, 2, PACK + q, nc.scalar.copy, keep.tile([P, width // 2], F32, name="result%d" % q)[:])
+        leave(2, 2, 2, 0, nc.vector.tensor_copy, keep.tile([P, width // 2], F32, name="result_held", tag="pre1", align_bytes=64)[:])
+        leave(3, 2, 2, 1, nc.vector.tensor_copy, keep.tile([P, width // 2], F32, name="result_last")[:])

@@ -41,7 +41,8 @@ def tile_picked_anc8_relu_p_kernel(tc, x_words, x_scales, w1, emb, w2, offs, up1
         stage = keep.tile([P, PACK * H + (PACK - 1) * S], F32, name="stage", align_bytes=64)
         w1_raw = [stage[:, 0 : PACK * H].rearrange("p (j c) -> p j c", j=PACK), keep.tile([P, PACK, H], F32, name="w1_raw1")[:]]
         sums = stage[:, PACK * H - S :].rearrange("p (t s) -> p t s", t=PACK)
-        w2_raw = [keep.tile([P, PACK, N // 2], F32, name="w2_raw%d" % h, tag="w2_raw%d" % h, align_bytes=64) for h in range(2)]
+        w2_flat = [keep.tile([P, PACK * N // 2], F32, name="w2_raw%d" % h, align_bytes=64) for h in range(2)]
+        w2_raw = [flat[:].rearrange("p (j c) -> p j c", j=PACK) for flat in w2_flat]
         x_word_table = [keep.tile([P, T], I32, name="x_word_table%d" % g) for g in range(PASSES)]
 
         nc.vector.memset(x_scale_table[:].bitcast(I32), 0)
@@ -84,7 +85,7 @@ def tile_picked_anc8_relu_p_kernel(tc, x_words, x_scales, w1, emb, w2, offs, up1
         load_x(1)
         w2_rows = w2.rearrange("(p j) c -> p j c", j=PACK)
         for h in range(2):
-            nc.sync.dma_start(out=w2_raw[h][:], in_=w2_rows[:, :, h * N // 2 : (h + 1) * N // 2])
+            nc.sync.dma_start(out=w2_raw[h], in_=w2_rows[:, :, h * N // 2 : (h + 1) * N // 2])
 
         def looked_up(t, l, first, count):
             return emb_wide[t][:].indirect(ups[l][:, first // GROUP : (first + count) // GROUP])
@@ -140,26 +141,29 @@ def tile_picked_anc8_relu_p_kernel(tc, x_words, x_scales, w1, emb, w2, offs, up1
             if g == 0:
                 chain(sums[:, 0, :], 0, 2, pairs[0])
 
-        y_banks = [psum.tile([P, PACK, PIECE], F32, name="y_bank%d" % q, tag="bank%d" % q) for q in range(PACK)]
+        def first_layer(bank, q, g):
+            cols = slice(q * PIECE, (q + 1) * PIECE)
+            for t in range(PACK):
+                nc.tensor.matmul_mx(
+                    out=bank[:, t, :],
+                    lhsT=w1_mx[g, t][0].bitcast(FP8X4),
+                    lhsT_scale=w1_mx[g, t][1],
+                    rhs=x_codes[g][:, cols].bitcast(FP8X4),
+                    rhs_scale=x_scale[4 * g : P, cols],
+                    start=(g == 0 and t == 0),
+                    stop=(g == PASSES - 1 and t == PACK - 1),
+                )
+
+        y_banks = [psum.tile([P, PACK, PIECE], F32, name="y_bank%d" % q, tag="bank%d" % q) for q in range(PACK - 1)]
         for g in range(PASSES):
-            for q in range(PACK):
-                cols = slice(q * PIECE, (q + 1) * PIECE)
-                for t in range(PACK):
-                    nc.tensor.matmul_mx(
-                        out=y_banks[q][:, t, :],
-                        lhsT=w1_mx[g, t][0].bitcast(FP8X4),
-                        lhsT_scale=w1_mx[g, t][1],
-                        rhs=x_codes[g][:, cols].bitcast(FP8X4),
-                        rhs_scale=x_scale[4 * g : P, cols],
-                        start=(g == 0 and t == 0),
-                        stop=(g == PASSES - 1 and t == PACK - 1),
-                    )
+            for q in range(PACK - 1):
+                first_layer(y_banks[q], q, g)
 
         w2_grouped = [keep.tile([P, PACK * N // 2], BF16, name="w2_grouped%d" % h, align_bytes=64) for h in range(2)]
         for h in range(2):
             nc.scalar.activation(
                 out=w2_grouped[h][:].rearrange("p (c i j) -> p c j i", i=RUN, j=PACK),
-                in_=w2_raw[h][:].rearrange("p j (c i) -> p c j i", i=RUN),
+                in_=w2_raw[h].rearrange("p j (c i) -> p c j i", i=RUN),
                 func=COPY,
             )
 
@@ -192,24 +196,38 @@ def tile_picked_anc8_relu_p_kernel(tc, x_words, x_scales, w1, emb, w2, offs, up1
             nc.sync.dma_start(out=out_tiles[:, t0 : t0 + tiles, q * PIECE : (q + 1) * PIECE], in_=rows)
 
         width = PACK * PIECE
-        for q in range(PACK):
+
+        def finish(q, pre, by_vector):
             cols = slice(q * PIECE, (q + 1) * PIECE)
-            z = keep.tile([P, width], BF16, name="z%d" % q, tag="w2_raw%d" % q if q < 2 else "z%d" % q, align_bytes=64)
-            if q in (0, PACK - 1):
-                pre = keep.tile([P, width], BF16, name="pre%d" % q, tag="pre%d" % (q % 2), align_bytes=64)[:]
+            z = w2_flat[q][:, 0 : width // 2].bitcast(BF16) if q < 2 else keep.tile([P, width], BF16, name="z%d" % q, align_bytes=64)[:]
+            if by_vector:
                 nc.vector.tensor_tensor(out=interleaved(pre), in0=by_runs(y_banks[q][:]), in1=by_runs(sums[:, :, cols]), op=ADD)
-                nc.vector.tensor_scalar_max(z[:], pre, 0.0)
+                nc.vector.tensor_scalar_max(z, pre, 0.0)
             else:
-                pre = keep.tile([P, PACK, PIECE], F32, name="pre%d" % q, tag="pre%d" % (q % 2), align_bytes=64)[:]
-                nc.vector.tensor_tensor(out=pre, in0=y_banks[q][:], in1=sums[:, :, cols], op=ADD)
-                nc.scalar.activation(out=interleaved(z[:]), in_=by_runs(pre), func=RELU)
-            if q == 0:
-                w2_mx = [quantised("w2_%d" % h, w2_grouped[h][:], N // 2) for h in range(2)]
-            z_codes, z_scales = quantised("z%d" % q, z[:], PIECE)
-            z_mx.append((z_codes, z_scales))
-            if q < 2:
-                leave(q, 0, PACK, PACK + q, nc.scalar.copy, keep.tile([P, width], F32, name="result%d" % q)[:])
-            else:
-                leave(q, 0, 2, PACK + q, nc.scalar.copy, keep.tile([P, width // 2], F32, name="result%d" % q)[:])
-        leave(2, 2, 2, 0, nc.vector.tensor_copy, keep.tile([P, width // 2], F32, name="result_held", tag="pre1", align_bytes=64)[:])
-        leave(3, 2, 2, 1, nc.vector.tensor_copy, keep.tile([P, width // 2], F32, name="result_last")[:])
+                planes = pre.rearrange("p (t s) -> p t s", t=PACK)
+                nc.vector.tensor_tensor(out=planes, in0=y_banks[q][:], in1=sums[:, :, cols], op=ADD)
+                nc.scalar.activation(out=interleaved(z), in_=by_runs(planes), func=RELU)
+            return z
+
+        def result(name, tiles):
+            return keep.tile([P, tiles * PIECE], F32, name=name)[:]
+
+        z = finish(0, keep.tile([P, width], BF16, name="pre0", align_bytes=64)[:], True)
+        w2_mx = [quantised("w2_%d" % h, w2_grouped[h][:], N // 2) for h in range(2)]
+        z_mx.append(quantised("z0", z, PIECE))
+        y_banks.append(psum.tile([P, PACK, PIECE], F32, name="y_bank3", tag="bank0"))
+        for g in range(PASSES):
+            first_layer(y_banks[3], 3, g)
+        z = finish(1, keep.tile([P, width], F32, name="pre1", tag="pre", align_bytes=64)[:], False)
+        leave(0, 0, 2, 4, nc.scalar.copy, w2_flat[1][:, width // 2 : width])
+        leave(0, 2, 2, 5, nc.scalar.copy, result("result0_2", 2))
+        z_mx.append(quantised("z1", z, PIECE))
+        z = finish(2, w2_flat[1][:, width:], False)
+        leave(1, 0, PACK, 2, nc.scalar.copy, result("result1", PACK))
+        z_last = finish(3, keep.tile([P, width], BF16, name="pre3", tag="pre", align_bytes=64)[:], True)
+        z_mx.append(quantised("z2", z, PIECE))
+        leave(2, 0, 2, 6, nc.scalar.copy, result("result2_0", 2))
+        z_mx.append(quantised("z3", z_last, PIECE))
+        leave(3, 0, 2, 7, nc.scalar.copy, result("result3_0", 2))
+        leave(2, 2, 2, 3, nc.vector.tensor_copy, keep.tile([P, width // 2], F32, name="result2_2", tag="pre", align_bytes=64)[:])
+        leave(3, 2, 2, 1, nc.vector.tensor_copy, result("result3_2", 2))

@@ -197,37 +197,38 @@ def tile_picked_anc8_relu_p_kernel(tc, x_words, x_scales, w1, emb, w2, offs, up1
 
         width = PACK * PIECE
 
-        def finish(q, pre, by_vector):
+        def finish(q, pre, z):
             cols = slice(q * PIECE, (q + 1) * PIECE)
-            z = w2_flat[q][:, 0 : width // 2].bitcast(BF16) if q < 2 else keep.tile([P, width], BF16, name="z%d" % q, align_bytes=64)[:]
-            if by_vector:
+            if q != 2:
                 nc.vector.tensor_tensor(out=interleaved(pre), in0=by_runs(y_banks[q][:]), in1=by_runs(sums[:, :, cols]), op=ADD)
                 nc.vector.tensor_scalar_max(z, pre, 0.0)
             else:
                 planes = pre.rearrange("p (t s) -> p t s", t=PACK)
                 nc.vector.tensor_tensor(out=planes, in0=y_banks[q][:], in1=sums[:, :, cols], op=ADD)
                 nc.scalar.activation(out=interleaved(z), in_=by_runs(planes), func=RELU)
-            return z
 
         def result(name, tiles):
             return keep.tile([P, tiles * PIECE], F32, name=name)[:]
 
-        z = finish(0, keep.tile([P, width], BF16, name="pre0", align_bytes=64)[:], True)
+        words = width // 2
+        pre = [keep.tile([P, width], BF16, name="pre%d" % q, align_bytes=64)[:] for q in range(2)]
+        z = [w2_flat[0][:, 0:words].bitcast(BF16), pre[0]] + [keep.tile([P, width], BF16, name="z%d" % q, align_bytes=64)[:] for q in (2, 3)]
+        finish(0, pre[0], z[0])
         w2_mx = [quantised("w2_%d" % h, w2_grouped[h][:], N // 2) for h in range(2)]
-        z_mx.append(quantised("z0", z, PIECE))
+        z_mx.append(quantised("z0", z[0], PIECE))
         y_banks.append(psum.tile([P, PACK, PIECE], F32, name="y_bank3", tag="bank0"))
         for g in range(PASSES):
             first_layer(y_banks[3], 3, g)
-        z = finish(1, keep.tile([P, width], F32, name="pre1", tag="pre", align_bytes=64)[:], False)
-        leave(0, 0, 2, 4, nc.scalar.copy, w2_flat[1][:, width // 2 : width])
+        finish(1, pre[1], z[1])
+        leave(0, 0, 2, 4, nc.scalar.copy, w2_flat[1][:, words:width])
+        finish(2, w2_grouped[0][:].bitcast(F32), z[2])
         leave(0, 2, 2, 5, nc.scalar.copy, result("result0_2", 2))
-        z_mx.append(quantised("z1", z, PIECE))
-        z = finish(2, w2_flat[1][:, width:], False)
+        z_mx.append(quantised("z1", z[1], PIECE))
         leave(1, 0, PACK, 2, nc.scalar.copy, result("result1", PACK))
-        z_last = finish(3, keep.tile([P, width], BF16, name="pre3", tag="pre", align_bytes=64)[:], True)
-        z_mx.append(quantised("z2", z, PIECE))
+        finish(3, w2_flat[1][:, 0:words].bitcast(BF16), z[3])
+        z_mx.append(quantised("z2", z[2], PIECE))
         leave(2, 0, 2, 6, nc.scalar.copy, result("result2_0", 2))
-        z_mx.append(quantised("z3", z_last, PIECE))
+        z_mx.append(quantised("z3", z[3], PIECE))
         leave(3, 0, 2, 7, nc.scalar.copy, result("result3_0", 2))
-        leave(2, 2, 2, 3, nc.vector.tensor_copy, keep.tile([P, width // 2], F32, name="result2_2", tag="pre", align_bytes=64)[:])
+        leave(2, 2, 2, 3, nc.vector.tensor_copy, w2_flat[1][:, 0:words])
         leave(3, 2, 2, 1, nc.vector.tensor_copy, result("result3_2", 2))

@@ -175,10 +175,16 @@ def tile_picked_anc8_relu_p_kernel(tc, x_words, x_scales, w1, emb, w2, offs, up1
         def by_runs(planes):
             return planes.rearrange("p t (c i) -> p c t i", i=RUN)
 
-        z_mx = []
+        z_codes = [keep.tile([P, HALF], U32, name="z_codes%d" % h, align_bytes=64) for h in range(2)]
+        z_scales = [keep.tile([P, HALF], U8, name="z_scales%d" % h, align_bytes=64) for h in range(2)]
 
-        def leave(q, t0, tiles, bank, copy, result):
-            acc = psum.tile([P, tiles, PIECE], F32, name="acc%d_%d" % (q, t0), tag="bank%d" % bank)
+        def quantise_z(q):
+            nodes = slice(q % 2 * PIECE, (q % 2 + 1) * PIECE)
+            nc.vector.quantize_mx(out=z_codes[q // 2][:, nodes].bitcast(FP8X4), scales=z_scales[q // 2][:, nodes], in_=z[q])
+
+        def leave(q, t0, tiles, bank, copy, result, pieces=1):
+            cols = slice(q * PIECE, (q + pieces) * PIECE)
+            acc = psum.tile([P, tiles, pieces * PIECE], F32, name="acc%d_%d" % (q, t0), tag="bank%d" % bank)
             for t in range(t0, t0 + tiles):
                 codes, scales = w2_mx[t // 2]
                 m = slice(t % 2 * P, (t % 2 + 1) * P)
@@ -186,14 +192,14 @@ def tile_picked_anc8_relu_p_kernel(tc, x_words, x_scales, w1, emb, w2, offs, up1
                     out=acc[:, t - t0, :],
                     lhsT=codes[:, m].bitcast(FP8X4),
                     lhsT_scale=scales[:, m],
-                    rhs=z_mx[q][0][:].bitcast(FP8X4),
-                    rhs_scale=z_mx[q][1][:],
+                    rhs=z_codes[q // 2][:, q % 2 * PIECE : (q % 2 + pieces) * PIECE].bitcast(FP8X4),
+                    rhs_scale=z_scales[q // 2][:, q % 2 * PIECE : (q % 2 + pieces) * PIECE],
                     start=True,
                     stop=True,
                 )
             rows = result.rearrange("p (t s) -> p t s", t=tiles)
             copy(out=rows, in_=acc[:])
-            nc.sync.dma_start(out=out_tiles[:, t0 : t0 + tiles, q * PIECE : (q + 1) * PIECE], in_=rows)
+            nc.sync.dma_start(out=out_tiles[:, t0 : t0 + tiles, cols], in_=rows)
 
         width = PACK * PIECE
 
@@ -215,20 +221,20 @@ def tile_picked_anc8_relu_p_kernel(tc, x_words, x_scales, w1, emb, w2, offs, up1
         z = [w2_flat[0][:, 0:words].bitcast(BF16), pre[0]] + [keep.tile([P, width], BF16, name="z%d" % q, align_bytes=64)[:] for q in (2, 3)]
         finish(0, pre[0], z[0])
         w2_mx = [quantised("w2_%d" % h, w2_grouped[h][:], N // 2) for h in range(2)]
-        z_mx.append(quantised("z0", z[0], PIECE))
+        quantise_z(0)
         y_banks.append(psum.tile([P, PACK, PIECE], F32, name="y_bank3", tag="bank0"))
         for g in range(PASSES):
             first_layer(y_banks[3], 3, g)
         finish(1, pre[1], z[1])
         leave(0, 0, 2, 4, nc.scalar.copy, w2_flat[1][:, words:width])
         finish(2, w2_grouped[0][:].bitcast(F32), z[2])
-        leave(0, 2, 2, 5, nc.scalar.copy, result("result0_2", 2))
-        z_mx.append(quantised("z1", z[1], PIECE))
-        leave(1, 0, PACK, 2, nc.scalar.copy, result("result1", PACK))
+        quantise_z(1)
+        leave(1, 0, 2, 2, nc.scalar.copy, result("result1_0", 2))
+        leave(0, 2, 2, 5, nc.scalar.copy, result("result01_2", PACK), 2)
         finish(3, w2_flat[1][:, 0:words].bitcast(BF16), z[3])
-        z_mx.append(quantised("z2", z[2], PIECE))
+        quantise_z(2)
         leave(2, 0, 2, 6, nc.scalar.copy, result("result2_0", 2))
-        z_mx.append(quantised("z3", z[3], PIECE))
+        quantise_z(3)
         leave(3, 0, 2, 7, nc.scalar.copy, result("result3_0", 2))
         leave(2, 2, 2, 3, nc.vector.tensor_copy, w2_flat[1][:, 0:words])
         leave(3, 2, 2, 1, nc.vector.tensor_copy, result("result3_2", 2))

@@ -25,6 +25,7 @@ QUADRANT = 32
 HALF = S // 2
 PIECE = S // 4
 RUN = 4
+DMA_ALIGN = 256
 
 
 def tile_picked_anc8_relu_p_kernel(tc, x_words, x_scales, w1, emb, w2, offs, up1, up2, up3, out):
@@ -33,17 +34,17 @@ def tile_picked_anc8_relu_p_kernel(tc, x_words, x_scales, w1, emb, w2, offs, up1
         keep = ctx.enter_context(tc.tile_pool(name="keep", bufs=1))
         psum = ctx.enter_context(tc.psum_pool(name="psum", bufs=1))
 
-        x_scale_table = keep.tile([P, T], U8, name="x_scale_table", align_bytes=64)
+        x_scale_table = keep.tile([P, T], U8, name="x_scale_table", align_bytes=DMA_ALIGN)
         emb_planes = emb.rearrange("(p t) u -> p t u", t=PACK)
         ups = [keep.tile([P, S // GROUP], U16, name="up_list%d" % l) for l in range(LISTS)]
         picks = keep.tile([P, S // GROUP], U16, name="picks")
-        emb_wide = [keep.tile([P, 2 * U], F32, name="emb_wide%d" % t) for t in range(PACK)]
-        stage = keep.tile([P, PACK * H + (PACK - 1) * S], F32, name="stage", align_bytes=64)
-        w1_raw = [stage[:, 0 : PACK * H].rearrange("p (j c) -> p j c", j=PACK), keep.tile([P, PACK, H], F32, name="w1_raw1")[:]]
-        sums = stage[:, PACK * H - S :].rearrange("p (t s) -> p t s", t=PACK)
-        w2_flat = [keep.tile([P, PACK * N // 2], F32, name="w2_raw%d" % h, align_bytes=64) for h in range(2)]
+        emb_wide = [keep.tile([P, 2 * U], F32, name="emb_wide%d" % t, align_bytes=DMA_ALIGN) for t in range(PACK)]
+        w1_raw = [keep.tile([P, PACK, H], F32, name="w1_raw%d" % g, align_bytes=DMA_ALIGN)[:] for g in range(PASSES)]
+        stage = keep.tile([P, PACK * S], F32, name="stage", align_bytes=DMA_ALIGN)
+        sums = stage[:].rearrange("p (t s) -> p t s", t=PACK)
+        w2_flat = [keep.tile([P, PACK * N // 2], F32, name="w2_raw%d" % h, align_bytes=DMA_ALIGN) for h in range(2)]
         w2_raw = [flat[:].rearrange("p (j c) -> p j c", j=PACK) for flat in w2_flat]
-        x_word_table = [keep.tile([P, T], I32, name="x_word_table%d" % g) for g in range(PASSES)]
+        x_word_table = [keep.tile([P, T], I32, name="x_word_table%d" % g, align_bytes=DMA_ALIGN) for g in range(PASSES)]
 
         nc.vector.memset(x_scale_table[:].bitcast(I32), 0)
         for t in range(PACK - 1):
@@ -74,11 +75,11 @@ def tile_picked_anc8_relu_p_kernel(tc, x_words, x_scales, w1, emb, w2, offs, up1
         load_emb(2)
         load_emb(3)
         nc.sync.dma_start(ups[2][:], up3)
-        load_x(0)
+        load_w1(0)
         nc.sync.dma_start(picks[:], offs)
         for number in range(5):
             load_scales(number)
-        load_w1(0)
+        load_x(0)
         for number in range(5, 8):
             load_scales(number)
         load_w1(1)
@@ -100,46 +101,60 @@ def tile_picked_anc8_relu_p_kernel(tc, x_words, x_scales, w1, emb, w2, offs, up1
             nc.scalar.activation(out=values[:, first : first + count], in_=looked_up(t, l, first, count), func=COPY)
 
         firsts = [keep.tile([P, S], F32, name="first%d" % t)[:] for t in range(PACK)]
-        late_pairs = keep.tile([P, 2 * S], F32, name="late_pairs")
-        late_thirds = keep.tile([P, 2 * S], F32, name="late_thirds")
-        pairs = [keep.tile([P, S], F32, name="pair%d" % t)[:] for t in range(2)] + [late_pairs[:, 0:S], late_pairs[:, S:]]
-        thirds = {2: late_thirds[:, 0:S], 3: late_thirds[:, S:]}
+        thirds = keep.tile([P, PACK, S], F32, name="thirds")
+        early_pairs = keep.tile([P, 2, S], F32, name="early_pairs")
+        late_pairs = keep.tile([P, 2, S], F32, name="late_pairs")
+        pairs = [early_pairs[:, 0, :], early_pairs[:, 1, :], late_pairs[:, 0, :], late_pairs[:, 1, :]]
         nc.vector.tensor_copy(out=firsts[0][:, 0:HALF], in_=looked_up(0, 0, 0, HALF))
         fetch(firsts[0], 0, 0, HALF, HALF)
         for t in range(1, PACK):
             fetch(firsts[t], t, 0, 0, S)
-        for t in thirds:
-            fetch(thirds[t], t, 2, 0, S)
+        for t in range(PACK):
+            fetch(thirds[:, t, :], t, 2, 0, S)
 
-        def chain(total, t, l, before):
-            nc.vector.tensor_tensor(out=total, in0=looked_up(t, l, 0, S), in1=before, op=ADD)
+        def pair(t):
+            nc.vector.tensor_tensor(out=pairs[t], in0=looked_up(t, 1, 0, S), in1=firsts[t], op=ADD)
 
-        for t in range(PACK - 1):
-            chain(pairs[t], t, 1, firsts[t])
-        chain(sums[:, 1, :], 1, 2, pairs[1])
-        chain(pairs[3], 3, 1, firsts[3])
-        nc.gpsimd.tensor_tensor(out=sums[:, 2:4, :].rearrange("p t s -> p (t s)"), in0=late_thirds[:], in1=late_pairs[:], op=ADD)
+        w1_mx = {}
+
+        def w1_views(g, t0, planes):
+            first = (g * PACK + t0) * H // 2
+            grouped = stage[:, first : first + planes * H // 2].bitcast(BF16)
+            dealt = grouped.rearrange("p (t m j) -> p m j t", t=planes, j=PACK)
+            return grouped, dealt, w1_raw[g].rearrange("p j (m t) -> p m j t", t=PACK)[:, :, :, t0 : t0 + planes]
+
+        def quantise_w1(g, t0, planes):
+            codes, scales = quantised("w1_%d_%d" % (g, t0), w1_views(g, t0, planes)[0], planes * P)
+            for t in range(planes):
+                w1_mx[g, t0 + t] = (codes[:, t * P : (t + 1) * P], scales[:, t * P : (t + 1) * P])
+
+        for t in range(PACK):
+            pair(t)
+        for t0 in (0, 2):
+            nc.vector.tensor_copy(out=w1_views(0, t0, 2)[1], in_=w1_views(0, t0, 2)[2])
+        for t0 in (0, 2):
+            quantise_w1(0, t0, 2)
+        nc.gpsimd.tensor_tensor(out=sums[:, 0:2, :], in0=thirds[:, 0:2, :], in1=early_pairs[:], op=ADD)
 
         x_scale = keep.tile([P, S], U8, name="x_scale", align_bytes=64)
         x_codes = [keep.tile([P, S], U32, name="x_codes%d" % g, align_bytes=64) for g in range(PASSES)]
-        nc.vector.tensor_copy(out=x_scale[:], in_=x_scale_table[:].indirect(picks[:]))
-        for g, first, count in ((0, 0, S), (1, 0, PIECE), (1, PIECE, PIECE), (1, HALF, HALF)):
+
+        def gather_words(g, first, count):
             entries = picks[:, first // GROUP : (first + count) // GROUP]
             nc.vector.tensor_copy(out=x_codes[g][:, first : first + count], in_=x_word_table[g][:].bitcast(U32).indirect(entries))
 
-        w1_mx = {}
-        for g, t0, planes in ((0, 0, 4), (1, 0, 2), (1, 2, 2)):
-            w1_grouped = keep.tile([P, planes * H], BF16, name="w1_grouped%d_%d" % (g, t0), align_bytes=64)
-            nc.scalar.activation(
-                out=w1_grouped[:].rearrange("p (t m j) -> p m j t", t=planes, j=PACK),
-                in_=w1_raw[g].rearrange("p j (m t) -> p m j t", t=PACK)[:, :, :, t0 : t0 + planes],
-                func=COPY,
-            )
-            codes, scales = quantised("w1_%d_%d" % (g, t0), w1_grouped[:], planes * P)
-            for t in range(planes):
-                w1_mx[g, t0 + t] = (codes[:, t * P : (t + 1) * P], scales[:, t * P : (t + 1) * P])
-            if g == 0:
-                chain(sums[:, 0, :], 0, 2, pairs[0])
+        gather_words(0, 0, S)
+        nc.vector.tensor_copy(out=x_scale[:], in_=x_scale_table[:].indirect(picks[:]))
+
+        nc.scalar.activation(out=w1_views(1, 0, 2)[1], in_=w1_views(1, 0, 2)[2], func=COPY)
+        nc.vector.tensor_copy(out=w1_views(1, 2, 2)[1], in_=w1_views(1, 2, 2)[2])
+        quantise_w1(1, 2, 2)
+        quantise_w1(1, 0, 2)
+        for h in range(2):
+            nodes = slice(h * HALF, (h + 1) * HALF)
+            nc.gpsimd.tensor_tensor(out=sums[:, 2:4, nodes], in0=thirds[:, 2:4, nodes], in1=late_pairs[:, :, nodes], op=ADD)
+        for first, count in ((0, PIECE), (PIECE, PIECE), (HALF, HALF)):
+            gather_words(1, first, count)
 
         def first_layer(bank, q, g):
             cols = slice(q * PIECE, (q + 1) * PIECE)
@@ -214,7 +229,7 @@ def tile_picked_anc8_relu_p_kernel(tc, x_words, x_scales, w1, emb, w2, offs, up1
                 nc.scalar.activation(out=interleaved(z), in_=by_runs(planes), func=RELU)
 
         def result(name, tiles):
-            return keep.tile([P, tiles * PIECE], F32, name=name)[:]
+            return keep.tile([P, tiles * PIECE], F32, name=name, align_bytes=DMA_ALIGN)[:]
 
         words = width // 2
         pre = [keep.tile([P, width], BF16, name="pre%d" % q, align_bytes=64)[:] for q in range(2)]

@@ -39,9 +39,8 @@ def tile_picked_anc8_relu_p_kernel(tc, x_words, x_scales, w1, emb, w2, offs, up1
         ups = [keep.tile([P, S // GROUP], U16, name="up_list%d" % l) for l in range(LISTS)]
         picks = keep.tile([P, S // GROUP], U16, name="picks")
         emb_wide = [keep.tile([P, 2 * U], F32, name="emb_wide%d" % t, align_bytes=DMA_ALIGN) for t in range(PACK)]
-        w1_raw = [keep.tile([P, PACK, H], F32, name="w1_raw%d" % g, align_bytes=DMA_ALIGN)[:] for g in range(PASSES)]
-        stage = keep.tile([P, PACK * S], F32, name="stage", align_bytes=DMA_ALIGN)
-        sums = stage[:].rearrange("p (t s) -> p t s", t=PACK)
+        w1_raw = [keep.tile([P, PACK, H], F32, name="w1_raw%d" % g, tag="w1_raw%d" % g, align_bytes=DMA_ALIGN)[:] for g in range(PASSES)]
+        stage = keep.tile([P, PACK * H + HALF], F32, name="stage", align_bytes=DMA_ALIGN)
         w2_flat = [keep.tile([P, PACK * N // 2], F32, name="w2_raw%d" % h, align_bytes=DMA_ALIGN) for h in range(2)]
         w2_raw = [flat[:].rearrange("p (j c) -> p j c", j=PACK) for flat in w2_flat]
         x_word_table = [keep.tile([P, T], I32, name="x_word_table%d" % g, align_bytes=DMA_ALIGN) for g in range(PASSES)]
@@ -74,15 +73,15 @@ def tile_picked_anc8_relu_p_kernel(tc, x_words, x_scales, w1, emb, w2, offs, up1
         nc.sync.dma_start(ups[1][:], up2)
         load_emb(2)
         load_emb(3)
-        nc.sync.dma_start(ups[2][:], up3)
         load_w1(0)
+        nc.sync.dma_start(ups[2][:], up3)
         nc.sync.dma_start(picks[:], offs)
-        for number in range(5):
-            load_scales(number)
-        load_x(0)
-        for number in range(5, 8):
+        for number in range(4):
             load_scales(number)
         load_w1(1)
+        for number in range(4, 8):
+            load_scales(number)
+        load_x(0)
         load_x(1)
         w2_rows = w2.rearrange("(p j) c -> p j c", j=PACK)
         for h in range(2):
@@ -91,8 +90,8 @@ def tile_picked_anc8_relu_p_kernel(tc, x_words, x_scales, w1, emb, w2, offs, up1
         def looked_up(t, l, first, count):
             return emb_wide[t][:].indirect(ups[l][:, first // GROUP : (first + count) // GROUP])
 
-        def quantised(name, grouped, count):
-            codes = keep.tile([P, count], U32, name=name + "_codes", align_bytes=64)
+        def quantised(name, grouped, count, tag=None):
+            codes = keep.tile([P, count], U32, name=name + "_codes", tag=tag or name, align_bytes=DMA_ALIGN)
             scales = keep.tile([P, count], U8, name=name + "_scales", align_bytes=64)
             nc.vector.quantize_mx(out=codes[:].bitcast(FP8X4), scales=scales[:], in_=grouped)
             return codes, scales
@@ -102,61 +101,50 @@ def tile_picked_anc8_relu_p_kernel(tc, x_words, x_scales, w1, emb, w2, offs, up1
 
         firsts = [keep.tile([P, S], F32, name="first%d" % t)[:] for t in range(PACK)]
         thirds = keep.tile([P, PACK, S], F32, name="thirds")
-        early_pairs = keep.tile([P, 2, S], F32, name="early_pairs")
-        late_pairs = keep.tile([P, 2, S], F32, name="late_pairs")
-        pairs = [early_pairs[:, 0, :], early_pairs[:, 1, :], late_pairs[:, 0, :], late_pairs[:, 1, :]]
+        pairs = keep.tile([P, PACK, S], F32, name="pairs")
         nc.vector.tensor_copy(out=firsts[0][:, 0:HALF], in_=looked_up(0, 0, 0, HALF))
         fetch(firsts[0], 0, 0, HALF, HALF)
         for t in range(1, PACK):
             fetch(firsts[t], t, 0, 0, S)
-        for t in range(PACK):
-            fetch(thirds[:, t, :], t, 2, 0, S)
-
-        def pair(t):
-            nc.vector.tensor_tensor(out=pairs[t], in0=looked_up(t, 1, 0, S), in1=firsts[t], op=ADD)
-
         w1_mx = {}
 
-        def w1_views(g, t0, planes):
+        def w1_views(g, t0):
             first = (g * PACK + t0) * H // 2
-            grouped = stage[:, first : first + planes * H // 2].bitcast(BF16)
-            dealt = grouped.rearrange("p (t m j) -> p m j t", t=planes, j=PACK)
-            return grouped, dealt, w1_raw[g].rearrange("p j (m t) -> p m j t", t=PACK)[:, :, :, t0 : t0 + planes]
+            grouped = stage[:, first : first + H].bitcast(BF16)
+            dealt = grouped.rearrange("p (t m j) -> p m j t", t=2, j=PACK)
+            return grouped, dealt, w1_raw[g].rearrange("p j (m t) -> p m j t", t=PACK)[:, :, :, t0 : t0 + 2]
 
-        def quantise_w1(g, t0, planes):
-            codes, scales = quantised("w1_%d_%d" % (g, t0), w1_views(g, t0, planes)[0], planes * P)
-            for t in range(planes):
+        def quantise_w1(g, t0, tag=None):
+            codes, scales = quantised("w1_%d_%d" % (g, t0), w1_views(g, t0)[0], 2 * P, tag)
+            for t in range(2):
                 w1_mx[g, t0 + t] = (codes[:, t * P : (t + 1) * P], scales[:, t * P : (t + 1) * P])
 
+        nc.scalar.activation(out=w1_views(0, 0)[1], in_=w1_views(0, 0)[2], func=COPY)
         for t in range(PACK):
-            pair(t)
+            fetch(thirds[:, t, :], t, 2, 0, S)
+        for t in range(PACK):
+            nc.vector.tensor_tensor(out=pairs[:, t, :], in0=looked_up(t, 1, 0, S), in1=firsts[t], op=ADD)
+        nc.vector.tensor_copy(out=w1_views(0, 2)[1], in_=w1_views(0, 2)[2])
+        quantise_w1(0, 0)
+        quantise_w1(0, 2, "w1_raw0")
         for t0 in (0, 2):
-            nc.vector.tensor_copy(out=w1_views(0, t0, 2)[1], in_=w1_views(0, t0, 2)[2])
+            nc.vector.tensor_copy(out=w1_views(1, t0)[1], in_=w1_views(1, t0)[2])
         for t0 in (0, 2):
-            quantise_w1(0, t0, 2)
-        nc.gpsimd.tensor_tensor(out=sums[:, 0:2, :], in0=thirds[:, 0:2, :], in1=early_pairs[:], op=ADD)
+            quantise_w1(1, t0)
+        early = stage[:, PACK * H - 3 * HALF : PACK * H + HALF]
+        sums = [early.rearrange("p (t s) -> p t s", t=PACK), thirds[:, :, 0:HALF]]
+        for h, t0 in ((0, 0), (0, 2), (1, 0), (1, 2)):
+            planes, nodes = slice(t0, t0 + 2), slice(h * HALF, (h + 1) * HALF)
+            nc.gpsimd.tensor_tensor(out=sums[h][:, planes, :], in0=thirds[:, planes, nodes], in1=pairs[:, planes, nodes], op=ADD)
 
         x_scale = keep.tile([P, S], U8, name="x_scale", align_bytes=64)
         x_codes = [keep.tile([P, S], U32, name="x_codes%d" % g, align_bytes=64) for g in range(PASSES)]
-
-        def gather_words(g, first, count):
+        nc.vector.tensor_copy(out=x_scale[:], in_=x_scale_table[:].indirect(picks[:]))
+        for g, first, count in ((0, 0, HALF), (0, HALF, HALF), (1, 0, PIECE), (1, PIECE, PIECE), (1, HALF, HALF)):
             entries = picks[:, first // GROUP : (first + count) // GROUP]
             nc.vector.tensor_copy(out=x_codes[g][:, first : first + count], in_=x_word_table[g][:].bitcast(U32).indirect(entries))
 
-        gather_words(0, 0, S)
-        nc.vector.tensor_copy(out=x_scale[:], in_=x_scale_table[:].indirect(picks[:]))
-
-        nc.scalar.activation(out=w1_views(1, 0, 2)[1], in_=w1_views(1, 0, 2)[2], func=COPY)
-        nc.vector.tensor_copy(out=w1_views(1, 2, 2)[1], in_=w1_views(1, 2, 2)[2])
-        quantise_w1(1, 2, 2)
-        quantise_w1(1, 0, 2)
-        for h in range(2):
-            nodes = slice(h * HALF, (h + 1) * HALF)
-            nc.gpsimd.tensor_tensor(out=sums[:, 2:4, nodes], in0=thirds[:, 2:4, nodes], in1=late_pairs[:, :, nodes], op=ADD)
-        for first, count in ((0, PIECE), (PIECE, PIECE), (HALF, HALF)):
-            gather_words(1, first, count)
-
-        def first_layer(bank, q, g):
+        def first_layer(bank, q, g, opens=0):
             cols = slice(q * PIECE, (q + 1) * PIECE)
             for t in range(PACK):
                 nc.tensor.matmul_mx(
@@ -165,14 +153,16 @@ def tile_picked_anc8_relu_p_kernel(tc, x_words, x_scales, w1, emb, w2, offs, up1
                     lhsT_scale=w1_mx[g, t][1],
                     rhs=x_codes[g][:, cols].bitcast(FP8X4),
                     rhs_scale=x_scale[4 * g : P, cols],
-                    start=(g == 0 and t == 0),
-                    stop=(g == PASSES - 1 and t == PACK - 1),
+                    start=(g == opens and t == 0),
+                    stop=(g != opens and t == PACK - 1),
                 )
 
         y_banks = [psum.tile([P, PACK, PIECE], F32, name="y_bank%d" % q, tag="bank%d" % q) for q in range(PACK - 1)]
         for g in range(PASSES):
-            for q in range(PACK - 1):
+            for q in range(2):
                 first_layer(y_banks[q], q, g)
+        for g in (1, 0):
+            first_layer(y_banks[2], 2, g, 1)
 
         w2_grouped = [keep.tile([P, PACK * N // 2], BF16, name="w2_grouped%d" % h, align_bytes=64) for h in range(2)]
         for h in range(2):
@@ -219,13 +209,13 @@ def tile_picked_anc8_relu_p_kernel(tc, x_words, x_scales, w1, emb, w2, offs, up1
         width = PACK * PIECE
 
         def finish(q, pre, z):
-            cols = slice(q * PIECE, (q + 1) * PIECE)
+            added = sums[q // 2][:, :, q % 2 * PIECE : (q % 2 + 1) * PIECE]
             if q != 2:
-                nc.vector.tensor_tensor(out=interleaved(pre), in0=by_runs(y_banks[q][:]), in1=by_runs(sums[:, :, cols]), op=ADD)
+                nc.vector.tensor_tensor(out=interleaved(pre), in0=by_runs(y_banks[q][:]), in1=by_runs(added), op=ADD)
                 nc.vector.tensor_scalar_max(z, pre, 0.0)
             else:
                 planes = pre.rearrange("p (t s) -> p t s", t=PACK)
-                nc.vector.tensor_tensor(out=planes, in0=y_banks[q][:], in1=sums[:, :, cols], op=ADD)
+                nc.vector.tensor_tensor(out=planes, in0=y_banks[q][:], in1=added, op=ADD)
                 nc.scalar.activation(out=interleaved(z), in_=by_runs(planes), func=RELU)
 
         def result(name, tiles):

@@ -73,13 +73,15 @@ def tile_picked_anc8_relu_p_kernel(tc, x_words, x_scales, w1, emb, w2, offs, up1
         nc.sync.dma_start(ups[1][:], up2)
         load_emb(2)
         load_emb(3)
+        for number in range(2):
+            load_scales(number)
         load_w1(0)
         nc.sync.dma_start(ups[2][:], up3)
-        nc.sync.dma_start(picks[:], offs)
-        for number in range(4):
+        for number in range(2, 6):
             load_scales(number)
+        nc.sync.dma_start(picks[:], offs)
         load_w1(1)
-        for number in range(4, 8):
+        for number in range(6, 8):
             load_scales(number)
         load_x(0)
         load_x(1)

@@ -122,8 +122,11 @@ def tile_picked_anc8_relu_p_kernel(tc, x_words, x_scales, w1, emb, w2, offs, up1
                 w1_mx[g, t0 + t] = (codes[:, t * P : (t + 1) * P], scales[:, t * P : (t + 1) * P])
 
         nc.scalar.activation(out=w1_views(0, 0)[1], in_=w1_views(0, 0)[2], func=COPY)
-        for t in range(PACK):
+        for t in range(2):
             fetch(thirds[:, t, :], t, 2, 0, S)
+        for first in (0, HALF):
+            for t in range(2, PACK):
+                fetch(thirds[:, t, :], t, 2, first, HALF)
         for t in range(PACK):
             nc.vector.tensor_tensor(out=pairs[:, t, :], in0=looked_up(t, 1, 0, S), in1=firsts[t], op=ADD)
         nc.vector.tensor_copy(out=w1_views(0, 2)[1], in_=w1_views(0, 2)[2])

@@ -32,6 +32,7 @@ def tile_picked_anc8_relu_p_kernel(tc, x_words, x_scales, w1, emb, w2, offs, up1
     nc = tc.nc
     with ExitStack() as ctx:
         keep = ctx.enter_context(tc.tile_pool(name="keep", bufs=1))
+        reused = ctx.enter_context(tc.tile_pool(name="reused", bufs=1))
         psum = ctx.enter_context(tc.psum_pool(name="psum", bufs=1))
 
         x_scale_table = keep.tile([P, T], U8, name="x_scale_table", align_bytes=DMA_ALIGN)
@@ -39,7 +40,9 @@ def tile_picked_anc8_relu_p_kernel(tc, x_words, x_scales, w1, emb, w2, offs, up1
         ups = [keep.tile([P, S // GROUP], U16, name="up_list%d" % l) for l in range(LISTS)]
         picks = keep.tile([P, S // GROUP], U16, name="picks")
         emb_wide = [keep.tile([P, 2 * U], F32, name="emb_wide%d" % t, align_bytes=DMA_ALIGN) for t in range(PACK)]
-        w1_raw = [keep.tile([P, PACK, H], F32, name="w1_raw%d" % g, tag="w1_raw%d" % g, align_bytes=DMA_ALIGN)[:] for g in range(PASSES)]
+        w1_first = keep.tile([P, PACK, H], F32, name="w1_raw0", tag="w1_raw0", align_bytes=DMA_ALIGN)
+        w1_second = reused.tile([P, PACK, H], F32, name="w1_raw1", align_bytes=DMA_ALIGN, offset=0)
+        w1_raw = [w1_first[:], w1_second[:]]
         stage = keep.tile([P, PACK * H + HALF], F32, name="stage", align_bytes=DMA_ALIGN)
         w2_flat = [keep.tile([P, PACK * N // 2], F32, name="w2_raw%d" % h, align_bytes=DMA_ALIGN) for h in range(2)]
         w2_raw = [flat[:].rearrange("p (j c) -> p j c", j=PACK) for flat in w2_flat]
@@ -102,7 +105,6 @@ def tile_picked_anc8_relu_p_kernel(tc, x_words, x_scales, w1, emb, w2, offs, up1
             nc.scalar.activation(out=values[:, first : first + count], in_=looked_up(t, l, first, count), func=COPY)
 
         firsts = [keep.tile([P, S], F32, name="first%d" % t)[:] for t in range(PACK)]
-        thirds = keep.tile([P, PACK, S], F32, name="thirds")
         pairs = keep.tile([P, PACK, S], F32, name="pairs")
         nc.vector.tensor_copy(out=firsts[0][:, 0:HALF], in_=looked_up(0, 0, 0, HALF))
         fetch(firsts[0], 0, 0, HALF, HALF)
@@ -111,7 +113,7 @@ def tile_picked_anc8_relu_p_kernel(tc, x_words, x_scales, w1, emb, w2, offs, up1
         w1_mx = {}
 
         def w1_views(g, t0):
-            first = (g * PACK + t0) * H // 2
+            first = (g * PACK + (t0 if g == 0 else 2 - t0)) * H // 2
             grouped = stage[:, first : first + H].bitcast(BF16)
             dealt = grouped.rearrange("p (t m j) -> p m j t", t=2, j=PACK)
             return grouped, dealt, w1_raw[g].rearrange("p j (m t) -> p m j t", t=PACK)[:, :, :, t0 : t0 + 2]
@@ -122,32 +124,40 @@ def tile_picked_anc8_relu_p_kernel(tc, x_words, x_scales, w1, emb, w2, offs, up1
                 w1_mx[g, t0 + t] = (codes[:, t * P : (t + 1) * P], scales[:, t * P : (t + 1) * P])
 
         nc.scalar.activation(out=w1_views(0, 0)[1], in_=w1_views(0, 0)[2], func=COPY)
-        for t in range(2):
-            fetch(thirds[:, t, :], t, 2, 0, S)
-        for first in (0, HALF):
-            for t in range(2, PACK):
-                fetch(thirds[:, t, :], t, 2, first, HALF)
+        early_thirds = keep.tile([P, 2, HALF], F32, name="early_thirds")
+        thirds = {(0, 0): early_thirds[:]}
+
+        def fetch_thirds(h, t0):
+            for t in range(2):
+                nc.scalar.activation(out=thirds[h, t0][:, t, :], in_=looked_up(t0 + t, 2, h * HALF, HALF), func=COPY)
+
+        fetch_thirds(0, 0)
         for t in range(PACK):
             nc.vector.tensor_tensor(out=pairs[:, t, :], in0=looked_up(t, 1, 0, S), in1=firsts[t], op=ADD)
         nc.vector.tensor_copy(out=w1_views(0, 2)[1], in_=w1_views(0, 2)[2])
         quantise_w1(0, 0)
         quantise_w1(0, 2, "w1_raw0")
-        for t0 in (0, 2):
-            nc.vector.tensor_copy(out=w1_views(1, t0)[1], in_=w1_views(1, t0)[2])
-        for t0 in (0, 2):
+        nc.scalar.activation(out=w1_views(1, 0)[1], in_=w1_views(1, 0)[2], func=COPY)
+        nc.vector.tensor_copy(out=w1_views(1, 2)[1], in_=w1_views(1, 2)[2])
+        for t0 in (2, 0):
             quantise_w1(1, t0)
+        late_thirds = reused.tile([P, 3, 2, HALF], F32, name="late_thirds", align_bytes=DMA_ALIGN, offset=0)
+        for place, (h, t0) in enumerate(((0, 2), (1, 0), (1, 2))):
+            thirds[h, t0] = late_thirds[:, place]
+            fetch_thirds(h, t0)
+        x_scale = reused.tile([P, S], U8, name="x_scale", align_bytes=DMA_ALIGN, offset=3 * S * 4)
+        nc.vector.tensor_copy(out=x_scale[:], in_=x_scale_table[:].indirect(picks[:]))
         early = stage[:, PACK * H - 3 * HALF : PACK * H + HALF]
-        sums = [early.rearrange("p (t s) -> p t s", t=PACK), thirds[:, :, 0:HALF]]
+        sums = [early.rearrange("p (t s) -> p t s", t=PACK), keep.tile([P, PACK, HALF], F32, name="late_sums")[:]]
         for h, t0 in ((0, 0), (0, 2), (1, 0), (1, 2)):
             planes, nodes = slice(t0, t0 + 2), slice(h * HALF, (h + 1) * HALF)
-            nc.gpsimd.tensor_tensor(out=sums[h][:, planes, :], in0=thirds[:, planes, nodes], in1=pairs[:, planes, nodes], op=ADD)
+            nc.gpsimd.tensor_tensor(out=sums[h][:, planes, :], in0=thirds[h, t0], in1=pairs[:, planes, nodes], op=ADD)
 
-        x_scale = keep.tile([P, S], U8, name="x_scale", align_bytes=64)
         x_codes = [keep.tile([P, S], U32, name="x_codes%d" % g, align_bytes=64) for g in range(PASSES)]
-        nc.vector.tensor_copy(out=x_scale[:], in_=x_scale_table[:].indirect(picks[:]))
-        for g, first, count in ((0, 0, HALF), (0, HALF, HALF), (1, 0, PIECE), (1, PIECE, PIECE), (1, HALF, HALF)):
-            entries = picks[:, first // GROUP : (first + count) // GROUP]
-            nc.vector.tensor_copy(out=x_codes[g][:, first : first + count], in_=x_word_table[g][:].bitcast(U32).indirect(entries))
+        for g in range(PASSES):
+            for first, count in ((0, PIECE), (PIECE, PIECE), (HALF, HALF)):
+                entries = picks[:, first // GROUP : (first + count) // GROUP]
+                nc.vector.tensor_copy(out=x_codes[g][:, first : first + count], in_=x_word_table[g][:].bitcast(U32).indirect(entries))
 
         def first_layer(bank, q, g, opens=0):
             cols = slice(q * PIECE, (q + 1) * PIECE)

@@ -202,7 +202,7 @@ def tile_picked_anc8_relu_p_kernel(tc, x_words, x_scales, w1, emb, w2, offs, up1
             nodes = slice(q % 2 * PIECE, (q % 2 + 1) * PIECE)
             nc.vector.quantize_mx(out=z_codes[q // 2][:, nodes].bitcast(FP8X4), scales=z_scales[q // 2][:, nodes], in_=z[q])
 
-        def leave(q, t0, tiles, bank, copy, result, pieces=1):
+        def leave(q, t0, tiles, bank, copy, result, pieces=1, stored=True):
             cols = slice(q * PIECE, (q + pieces) * PIECE)
             acc = psum.tile([P, tiles, pieces * PIECE], F32, name="acc%d_%d" % (q, t0), tag="bank%d" % bank)
             for t in range(t0, t0 + tiles):
@@ -219,7 +219,8 @@ def tile_picked_anc8_relu_p_kernel(tc, x_words, x_scales, w1, emb, w2, offs, up1
                 )
             rows = result.rearrange("p (t s) -> p t s", t=tiles)
             copy(out=rows, in_=acc[:])
-            nc.sync.dma_start(out=out_tiles[:, t0 : t0 + tiles, cols], in_=rows)
+            if stored:
+                nc.sync.dma_start(out=out_tiles[:, t0 : t0 + tiles, cols], in_=rows)
 
         width = PACK * PIECE
 
@@ -255,6 +256,9 @@ def tile_picked_anc8_relu_p_kernel(tc, x_words, x_scales, w1, emb, w2, offs, up1
         quantise_z(2)
         leave(2, 0, 2, 6, nc.scalar.copy, result("result2_0", 2))
         quantise_z(3)
-        leave(3, 0, 2, 7, nc.scalar.copy, result("result3_0", 2))
         leave(2, 2, 2, 3, nc.vector.tensor_copy, w2_flat[1][:, 0:words])
-        leave(3, 2, 2, 1, nc.vector.tensor_copy, result("result3_2", 2))
+        for t0, banks in ((0, (7, 1)), (2, (4, 0))):
+            last = result("result3_%d" % t0, 2)
+            leave(3, t0, 1, banks[0], nc.scalar.copy, last[:, 0:PIECE], stored=False)
+            leave(3, t0 + 1, 1, banks[1], nc.vector.tensor_copy, last[:, PIECE:], stored=False)
+            nc.sync.dma_start(out=out_tiles[:, t0 : t0 + 2, 3 * PIECE :], in_=last.rearrange("p (t s) -> p t s", t=2))

@@ -76,15 +76,14 @@ def tile_picked_anc8_relu_p_kernel(tc, x_words, x_scales, w1, emb, w2, offs, up1
         nc.sync.dma_start(ups[1][:], up2)
         load_emb(2)
         load_emb(3)
-        for number in range(2):
-            load_scales(number)
+        load_scales(0)
         load_w1(0)
         nc.sync.dma_start(ups[2][:], up3)
-        for number in range(2, 6):
+        for number in range(1, 5):
             load_scales(number)
         nc.sync.dma_start(picks[:], offs)
         load_w1(1)
-        for number in range(6, 8):
+        for number in range(5, 8):
             load_scales(number)
         load_x(0)
         load_x(1)

@@ -76,14 +76,13 @@ def tile_picked_anc8_relu_p_kernel(tc, x_words, x_scales, w1, emb, w2, offs, up1
         nc.sync.dma_start(ups[1][:], up2)
         load_emb(2)
         load_emb(3)
-        load_scales(0)
+        for number in range(3):
+            load_scales(number)
         load_w1(0)
         nc.sync.dma_start(ups[2][:], up3)
-        for number in range(1, 5):
-            load_scales(number)
-        nc.sync.dma_start(picks[:], offs)
         load_w1(1)
-        for number in range(5, 8):
+        nc.sync.dma_start(picks[:], offs)
+        for number in range(3, 8):
             load_scales(number)
         load_x(0)
         load_x(1)

from contextlib import ExitStack

import concourse.mybir as mybir

K, T, S, H, N, U = 1024, 2048, 512, 512, 512, 512
FLOPS = 2 * K * H * S + 2 * H * N * S

F32 = mybir.dt.float32
BF16 = mybir.dt.bfloat16
I32 = mybir.dt.int32
U32 = mybir.dt.uint32
U16 = mybir.dt.uint16
U8 = mybir.dt.uint8
FP8X4 = mybir.dt.float8_e4m3fn_x4
COPY = mybir.ActivationFunctionType.Copy
RELU = mybir.ActivationFunctionType.Relu
ADD = mybir.AluOpType.add

P = 128
PACK = 4
PASSES = K // (P * PACK)
LISTS = 3
GROUP = 16
QUADRANT = 32
HALF = S // 2
PIECE = S // 4
RUN = 4
DMA_ALIGN = 256


def tile_picked_anc8_relu_p_kernel(tc, x_words, x_scales, w1, emb, w2, offs, up1, up2, up3, out):
    nc = tc.nc
    with ExitStack() as ctx:
        keep = ctx.enter_context(tc.tile_pool(name="keep", bufs=1))
        reused = ctx.enter_context(tc.tile_pool(name="reused", bufs=1))
        psum = ctx.enter_context(tc.psum_pool(name="psum", bufs=1))

        x_scale_table = keep.tile([P, T], U8, name="x_scale_table", align_bytes=DMA_ALIGN)
        emb_planes = emb.rearrange("(p t) u -> p t u", t=PACK)
        ups = [keep.tile([P, S // GROUP], U16, name="up_list%d" % l) for l in range(LISTS)]
        picks = keep.tile([P, S // GROUP], U16, name="picks")
        emb_wide = [keep.tile([P, 2 * U], F32, name="emb_wide%d" % t, align_bytes=DMA_ALIGN) for t in range(PACK)]
        w1_first = keep.tile([P, PACK, H], F32, name="w1_raw0", tag="w1_raw0", align_bytes=DMA_ALIGN)
        w1_second = reused.tile([P, PACK, H], F32, name="w1_raw1", align_bytes=DMA_ALIGN, offset=0)
        w1_raw = [w1_first[:], w1_second[:]]
        stage = keep.tile([P, PACK * H + HALF], F32, name="stage", align_bytes=DMA_ALIGN)
        w2_flat = [keep.tile([P, PACK * N // 2], F32, name="w2_raw%d" % h, align_bytes=DMA_ALIGN) for h in range(2)]
        w2_raw = [flat[:].rearrange("p (j c) -> p j c", j=PACK) for flat in w2_flat]
        x_word_table = [keep.tile([P, T], I32, name="x_word_table%d" % g, align_bytes=DMA_ALIGN) for g in range(PASSES)]

        nc.vector.memset(x_scale_table[:].bitcast(I32), 0)
        for t in range(PACK - 1):
            nc.vector.memset(emb_wide[t][:, U : 2 * U], 0.0)
        nc.scalar.activation(out=emb_wide[PACK - 1][:, U : 2 * U], in_=emb_wide[0][:, U : 2 * U], func=COPY)

        def load_emb(t):
            nc.sync.dma_start(out=emb_wide[t][:, 0:U], in_=emb_planes[:, t, :])

        def load_w1(g):
            rows = w1[g * P * PACK : (g + 1) * P * PACK, :]
            nc.sync.dma_start(out=w1_raw[g], in_=rows.rearrange("(p j) c -> p j c", j=PACK))

        def load_x(g):
            nc.sync.dma_start(out=x_word_table[g][:], in_=x_words[g].rearrange("p n t -> p (n t)").bitcast(I32))

        def load_scales(number):
            g, r = number % PASSES, number // PASSES
            nc.sync.dma_start(
                out=x_scale_table[4 * g + r : P : QUADRANT, :].bitcast(I32),
                in_=x_scales[g, r : 16 : 4, :].bitcast(I32),
            )

        load_emb(0)
        nc.sync.dma_start(ups[0][:], up1)
        load_emb(1)
        nc.sync.dma_start(ups[1][:], up2)
        load_emb(2)
        load_emb(3)
        for number in range(3):
            load_scales(number)
        load_w1(0)
        nc.sync.dma_start(ups[2][:], up3)
        load_w1(1)
        nc.sync.dma_start(picks[:], offs)
        for number in range(3, 8):
            load_scales(number)
        load_x(0)
        load_x(1)
        w2_rows = w2.rearrange("(p j) c -> p j c", j=PACK)
        for h in range(2):
            nc.sync.dma_start(out=w2_raw[h], in_=w2_rows[:, :, h * N // 2 : (h + 1) * N // 2])

        def looked_up(t, l, first, count):
            return emb_wide[t][:].indirect(ups[l][:, first // GROUP : (first + count) // GROUP])

        def quantised(name, grouped, count, tag=None):
            codes = keep.tile([P, count], U32, name=name + "_codes", tag=tag or name, align_bytes=DMA_ALIGN)
            scales = keep.tile([P, count], U8, name=name + "_scales", align_bytes=64)
            nc.vector.quantize_mx(out=codes[:].bitcast(FP8X4), scales=scales[:], in_=grouped)
            return codes, scales

        def fetch(values, t, l, first, count):
            nc.scalar.activation(out=values[:, first : first + count], in_=looked_up(t, l, first, count), func=COPY)

        firsts = [keep.tile([P, S], F32, name="first%d" % t)[:] for t in range(PACK)]
        pairs = keep.tile([P, PACK, S], F32, name="pairs")
        nc.vector.tensor_copy(out=firsts[0][:, 0:HALF], in_=looked_up(0, 0, 0, HALF))
        fetch(firsts[0], 0, 0, HALF, HALF)
        for t in range(1, PACK):
            fetch(firsts[t], t, 0, 0, S)
        w1_mx = {}

        def w1_views(g, t0):
            first = (g * PACK + (t0 if g == 0 else 2 - t0)) * H // 2
            grouped = stage[:, first : first + H].bitcast(BF16)
            dealt = grouped.rearrange("p (t m j) -> p m j t", t=2, j=PACK)
            return grouped, dealt, w1_raw[g].rearrange("p j (m t) -> p m j t", t=PACK)[:, :, :, t0 : t0 + 2]

        def quantise_w1(g, t0, tag=None):
            codes, scales = quantised("w1_%d_%d" % (g, t0), w1_views(g, t0)[0], 2 * P, tag)
            for t in range(2):
                w1_mx[g, t0 + t] = (codes[:, t * P : (t + 1) * P], scales[:, t * P : (t + 1) * P])

        nc.scalar.activation(out=w1_views(0, 0)[1], in_=w1_views(0, 0)[2], func=COPY)
        early_thirds = keep.tile([P, 2, HALF], F32, name="early_thirds")
        thirds = {(0, 0): early_thirds[:]}

        def fetch_thirds(h, t0):
            for t in range(2):
                nc.scalar.activation(out=thirds[h, t0][:, t, :], in_=looked_up(t0 + t, 2, h * HALF, HALF), func=COPY)

        fetch_thirds(0, 0)
        for t in range(PACK):
            nc.vector.tensor_tensor(out=pairs[:, t, :], in0=looked_up(t, 1, 0, S), in1=firsts[t], op=ADD)
        nc.vector.tensor_copy(out=w1_views(0, 2)[1], in_=w1_views(0, 2)[2])
        quantise_w1(0, 0)
        quantise_w1(0, 2, "w1_raw0")
        nc.scalar.activation(out=w1_views(1, 0)[1], in_=w1_views(1, 0)[2], func=COPY)
        nc.vector.tensor_copy(out=w1_views(1, 2)[1], in_=w1_views(1, 2)[2])
        for t0 in (2, 0):
            quantise_w1(1, t0)
        late_thirds = reused.tile([P, 3, 2, HALF], F32, name="late_thirds", align_bytes=DMA_ALIGN, offset=0)
        for place, (h, t0) in enumerate(((0, 2), (1, 0), (1, 2))):
            thirds[h, t0] = late_thirds[:, place]
            fetch_thirds(h, t0)
        x_scale = reused.tile([P, S], U8, name="x_scale", align_bytes=DMA_ALIGN, offset=3 * S * 4)
        nc.vector.tensor_copy(out=x_scale[:], in_=x_scale_table[:].indirect(picks[:]))
        early = stage[:, PACK * H - 3 * HALF : PACK * H + HALF]
        sums = [early.rearrange("p (t s) -> p t s", t=PACK), keep.tile([P, PACK, HALF], F32, name="late_sums")[:]]
        for h, t0 in ((0, 0), (0, 2), (1, 0), (1, 2)):
            planes, nodes = slice(t0, t0 + 2), slice(h * HALF, (h + 1) * HALF)
            nc.gpsimd.tensor_tensor(out=sums[h][:, planes, :], in0=thirds[h, t0], in1=pairs[:, planes, nodes], op=ADD)

        x_codes = [keep.tile([P, S], U32, name="x_codes%d" % g, align_bytes=64) for g in range(PASSES)]
        for g in range(PASSES):
            for first, count in ((0, PIECE), (PIECE, PIECE), (HALF, HALF)):
                entries = picks[:, first // GROUP : (first + count) // GROUP]
                nc.vector.tensor_copy(out=x_codes[g][:, first : first + count], in_=x_word_table[g][:].bitcast(U32).indirect(entries))

        def first_layer(bank, q, g, opens=0):
            cols = slice(q * PIECE, (q + 1) * PIECE)
            for t in range(PACK):
                nc.tensor.matmul_mx(
                    out=bank[:, t, :],
                    lhsT=w1_mx[g, t][0].bitcast(FP8X4),
                    lhsT_scale=w1_mx[g, t][1],
                    rhs=x_codes[g][:, cols].bitcast(FP8X4),
                    rhs_scale=x_scale[4 * g : P, cols],
                    start=(g == opens and t == 0),
                    stop=(g != opens and t == PACK - 1),
                )

        y_banks = [psum.tile([P, PACK, PIECE], F32, name="y_bank%d" % q, tag="bank%d" % q) for q in range(PACK - 1)]
        for g in range(PASSES):
            for q in range(2):
                first_layer(y_banks[q], q, g)
        for g in (1, 0):
            first_layer(y_banks[2], 2, g, 1)

        w2_grouped = [keep.tile([P, PACK * N // 2], BF16, name="w2_grouped%d" % h, align_bytes=64) for h in range(2)]
        for h in range(2):
            nc.scalar.activation(
                out=w2_grouped[h][:].rearrange("p (c i j) -> p c j i", i=RUN, j=PACK),
                in_=w2_raw[h].rearrange("p j (c i) -> p c j i", i=RUN),
                func=COPY,
            )

        out_tiles = out.rearrange("(t p) s -> p t s", p=P)

        def interleaved(grouped):
            return grouped.rearrange("p (c i t) -> p c t i", i=RUN, t=PACK)

        def by_runs(planes):
            return planes.rearrange("p t (c i) -> p c t i", i=RUN)

        z_codes = [keep.tile([P, HALF], U32, name="z_codes%d" % h, align_bytes=64) for h in range(2)]
        z_scales = [keep.tile([P, HALF], U8, name="z_scales%d" % h, align_bytes=64) for h in range(2)]

        def quantise_z(q):
            nodes = slice(q % 2 * PIECE, (q % 2 + 1) * PIECE)
            nc.vector.quantize_mx(out=z_codes[q // 2][:, nodes].bitcast(FP8X4), scales=z_scales[q // 2][:, nodes], in_=z[q])

        def leave(q, t0, tiles, bank, copy, result, pieces=1, stored=True):
            cols = slice(q * PIECE, (q + pieces) * PIECE)
            acc = psum.tile([P, tiles, pieces * PIECE], F32, name="acc%d_%d" % (q, t0), tag="bank%d" % bank)
            for t in range(t0, t0 + tiles):
                codes, scales = w2_mx[t // 2]
                m = slice(t % 2 * P, (t % 2 + 1) * P)
                nc.tensor.matmul_mx(
                    out=acc[:, t - t0, :],
                    lhsT=codes[:, m].bitcast(FP8X4),
                    lhsT_scale=scales[:, m],
                    rhs=z_codes[q // 2][:, q % 2 * PIECE : (q % 2 + pieces) * PIECE].bitcast(FP8X4),
                    rhs_scale=z_scales[q // 2][:, q % 2 * PIECE : (q % 2 + pieces) * PIECE],
                    start=True,
                    stop=True,
                )
            rows = result.rearrange("p (t s) -> p t s", t=tiles)
            copy(out=rows, in_=acc[:])
            if stored:
                nc.sync.dma_start(out=out_tiles[:, t0 : t0 + tiles, cols], in_=rows)

        width = PACK * PIECE

        def finish(q, pre, z):
            added = sums[q // 2][:, :, q % 2 * PIECE : (q % 2 + 1) * PIECE]
            if q != 2:
                nc.vector.tensor_tensor(out=interleaved(pre), in0=by_runs(y_banks[q][:]), in1=by_runs(added), op=ADD)
                nc.vector.tensor_scalar_max(z, pre, 0.0)
            else:
                planes = pre.rearrange("p (t s) -> p t s", t=PACK)
                nc.vector.tensor_tensor(out=planes, in0=y_banks[q][:], in1=added, op=ADD)
                nc.scalar.activation(out=interleaved(z), in_=by_runs(planes), func=RELU)

        def result(name, tiles):
            return keep.tile([P, tiles * PIECE], F32, name=name, align_bytes=DMA_ALIGN)[:]

        words = width // 2
        pre = [keep.tile([P, width], BF16, name="pre%d" % q, align_bytes=64)[:] for q in range(2)]
        z = [w2_flat[0][:, 0:words].bitcast(BF16), pre[0]] + [keep.tile([P, width], BF16, name="z%d" % q, align_bytes=64)[:] for q in (2, 3)]
        finish(0, pre[0], z[0])
        w2_mx = [quantised("w2_%d" % h, w2_grouped[h][:], N // 2) for h in range(2)]
        quantise_z(0)
        y_banks.append(psum.tile([P, PACK, PIECE], F32, name="y_bank3", tag="bank0"))
        for g in range(PASSES):
            first_layer(y_banks[3], 3, g)
        finish(1, pre[1], z[1])
        leave(0, 0, 2, 4, nc.scalar.copy, w2_flat[1][:, words:width])
        finish(2, w2_grouped[0][:].bitcast(F32), z[2])
        quantise_z(1)
        leave(1, 0, 2, 2, nc.scalar.copy, result("result1_0", 2))
        leave(0, 2, 2, 5, nc.scalar.copy, result("result01_2", PACK), 2)
        finish(3, w2_flat[1][:, 0:words].bitcast(BF16), z[3])
        quantise_z(2)
        leave(2, 0, 2, 6, nc.scalar.copy, result("result2_0", 2))
        quantise_z(3)
        leave(2, 2, 2, 3, nc.vector.tensor_copy, w2_flat[1][:, 0:words])
        for t0, banks in ((0, (7, 1)), (2, (4, 0))):
            last = result("result3_%d" % t0, 2)
            leave(3, t0, 1, banks[0], nc.scalar.copy, last[:, 0:PIECE], stored=False)
            leave(3, t0 + 1, 1, banks[1], nc.vector.tensor_copy, last[:, PIECE:], stored=False)
            nc.sync.dma_start(out=out_tiles[:, t0 : t0 + 2, 3 * PIECE :], in_=last.rearrange("p (t s) -> p t s", t=2))
